import numpy as np, ml_dtypes
CORES = [113,118,241,246]
N = 4
BF = ml_dtypes.bfloat16
M, P, W, ST, SH, VM = 4096, 512, 160, 4, 1, 2048
NB, VB = 4075, 2046
AIM = np.array([255] * 14 + [16, 1])
def spot(u):
    return ((u * 241) >> 6) & (P - 1)
def lanes(u):
    b = u % 255
    return np.array([min(15, max(0, u // 255 - 15 * i)) for i in range(14)] + [b // 16, b % 16])
def aim(rng, c):
    u = np.arange(53000); return lanes(int(rng.choice(u[spot(u) == c])))
def below(rng, n):
    return (rng.random((N, 8, 16, n.shape[3]), dtype=np.float32) * n.astype(np.float32)).astype(np.int32)
def names(rng, pool, share, n):
    z = (N, 8, 16, n); p = np.take_along_axis(np.broadcast_to(pool, (N,) + pool.shape), rng.integers(0, pool.shape[2], z), 3)
    return np.where(rng.random(z) < share, p, rng.integers(0, M, z))
def parts(rng):
    g = below(rng, rng.integers(5, 17, (N, 8, 1, M))); e = below(rng, rng.integers(4, 17, (N, 8, 1, M)))
    pool = rng.integers(0, M, (8, 16, 6)); asl = rng.random((N, 8, 16, W)) < 0.5
    nm = np.where(asl, names(rng, pool, 0.8, W), names(rng, pool, 0.0, W))
    k = np.where(rng.random((N, 8, 16, P)) < 0.7, names(rng, pool, 0.7, P), M)
    return {"g": g, "e": e, "y": below(rng, rng.integers(8, 17, (N, 8, 1, P))), "k": k, "x": rng.integers(0, 16, (N, 8, 16, W)), "nm": nm, "asl": asl,
            "d": rng.integers(4, 15, (N, 8, 16, ST)), "h": rng.integers(0, 256, (N, 8, 16, 1)), "th": rng.integers(50, 101, (N, 8, 1, 1))}
def pack(s):
    def fl(a, n): return np.ascontiguousarray(a.reshape(N, 128, n)).astype(np.float32).astype(BF)
    def wh(a, n): return np.ascontiguousarray(a.reshape(N, 128, n)).astype(np.int32)
    return {"fx": fl(s["g"] + 16 * s["e"], M), "y0": fl(s["y"], P), "k0": wh(s["k"], P), "x0": fl(s["x"], W), "t0": wh(s["nm"] + M * s["asl"].astype(np.int64), W),
            "dw": wh(s["d"], ST), "hw": wh(s["h"], 1), "th": wh(np.repeat(s["th"], 16, axis=2), 1)}
def setup_inputs(rng):
    return pack(parts(rng))
def setup_inputs_spread(rng):
    s = parts(rng)
    s["g"] = below(rng, np.exp2(4 * rng.random((N, 8, 1, M))).astype(np.int64) + 1); s["e"] = below(rng, np.exp2(4 * rng.random((N, 8, 1, M))).astype(np.int64) + 1)
    s["g"] = np.minimum(s["g"], 15); s["e"] = np.minimum(s["e"], 15)
    s["x"] = np.minimum(below(rng, np.exp2(1 + 3 * rng.random((N, 8, 1, W))).astype(np.int64) + 1), 15)
    s["y"] = np.minimum(below(rng, np.exp2(1 + 3 * rng.random((N, 8, 1, P))).astype(np.int64) + 1), 15)
    s["asl"] = rng.random((N, 8, 16, W)) < rng.random((N, 8, 1, W))
    uneven = np.minimum(np.exp2(np.log2(M) * rng.random((N, 8, 16, W))).astype(np.int64) - 1, M - 1)
    s["nm"] = np.where(rng.random((N, 8, 1, W)) < 0.5, uneven, s["nm"])
    s["k"] = np.where(rng.random((N, 8, 16, P)) < rng.random((N, 8, 1, P)), s["k"], M)
    s["h"] = np.minimum(np.exp2(8 * rng.random((N, 8, 16, 1))).astype(np.int64), 255)
    s["d"] = rng.integers(1, 17, (N, 8, 16, ST)); s["th"] = rng.integers(0, 241, (N, 8, 1, 1))
    return pack(s)
def setup_inputs_ends(rng):
    s = parts(rng); z = (N, 8, 16, W)
    f = np.where(rng.random((N, 8, 1, M)) < 0.8, 255 * rng.integers(0, 2, (N, 8, 16, M)), s["g"] + 16 * s["e"])
    f[..., 0] = 0; f[..., 1] = 48; f[..., NB] = 0; f[..., M - 1] = 255
    s["g"] = f & 15; s["e"] = f >> 4
    th = np.where((np.arange(N)[:, None] + np.arange(8)[None, :]) % 2 == 0, 240, 0).reshape(N, 8, 1, 1)
    th[::2, 6] = 239; th[1::2, 6] = 1; s["th"] = th
    r = rng.random((N, 8, 1, P)); s["y"] = np.where(r < 0.3, 15, np.where(r < 0.6, 0, 15 * rng.integers(0, 2, (N, 8, 16, P))))
    s["y"][..., spot(61200)] = np.where(th[..., 0] >= 239, 0, 15)
    for q in range(1, N, 2):
        b = (q >> 1) & 1; s["y"][q, 6, 15, spot(61200)] = 14 - b; s["y"][q, 6, :, 0] = 0; s["y"][q, 6, 15, 0] = 2 - b
    r = rng.random((N, 8, 16, P)); s["k"] = np.where(r < 0.4, 0, np.where(r < 0.8, M, np.where(r < 0.9, M - 1, s["k"])))
    kind = rng.choice(4, (N, 8, 1, W), p=[0.3, 0.2, 0.3, 0.2]); kind[..., W - 4:] = np.array([3, 2, 1, 0])
    x = np.where(kind == 0, 15, np.where(kind == 1, 0, np.where(kind == 2, 15 * rng.integers(0, 2, z), 7)))
    both = (2 * M - 1) * rng.integers(0, 2, z); r = rng.random(z)
    t = np.where((kind == 0) | (r < 0.75), both, np.where(r < 0.85, M - 1, np.where(r < 0.95, M, s["nm"] + M * s["asl"])))
    t = np.where(kind == 3, np.where((np.arange(16) % 2 == 0)[None, None, :, None], 1, 2 * M - 1), t)
    h = 255 * rng.integers(0, 2, (N, 8, 16, 1)); h[:, 0] = 255; h[:, 6] = 255; h[:, 7] = 255; h[:, 3] = 0; h[:, 5, :, 0] = AIM
    for q in range(N):
        for w in (1, W - 6, W - 5):
            x[q, 5, :, w] = aim(rng, P - 1); t[q, 5, :, w] = both[q, 5, :, w]
        for w in (2, W - 8):
            x[q, 5, :, w] = lanes(int(rng.choice(np.arange(VB, 53000, VM)))); t[q, 5, :, w] = NB
    s["x"] = x; s["nm"] = t & (M - 1); s["asl"] = t >= M; s["h"] = h
    s["d"] = np.where(rng.random((N, 8, 16, ST)) < 0.5, 16, 1)
    return pack(s)
def setup_inputs_corners(rng):
    s = parts(rng); z = (N, 8, 16, W); row = np.arange(16)[None, None, :, None]
    o = np.argsort(rng.random((N, 8, 16, 64)), axis=2); s["g"][..., :64] = np.where(o < 8 + np.arange(64) % 4, 0, 15)
    s["g"][..., M - 1] = 0; s["e"][..., M - 1] = 0; s["g"][..., M - 2] = 15
    kind = rng.integers(0, 8, (N, 8, 1, W)); kind[:, 5, :, :8] = 1; kind[:, 5, :, W - 8:] = 1
    x = np.where(kind == 7, s["x"], rng.integers(1, 14, z)); one = rng.integers(0, 16, (N, 8, 1, W)); end = 15 * rng.integers(0, 2, (N, 8, 1, W))
    low = rng.integers(0, 64, z); nm = s["nm"]
    asl = np.where(kind == 0, True, np.where(kind <= 4, False, np.where(kind == 5, row != end, s["asl"])))
    nm = np.where(kind == 1, M - 1, np.where(kind == 2, M - 2, np.where(kind == 3, np.where(row == one, M - 1, M - 2), nm)))
    nm = np.where((kind == 4) | ((kind == 5) & (row == end)), low, np.where(kind == 6, (M - 1) * rng.integers(0, 2, z), nm))
    s["h"][:, 5, :, 0] = AIM; s["h"][:, 2] = 255; s["h"][:, 6, 15] = 0
    s["d"] = rng.choice(np.array([1, 2, 8, 15, 16]), (N, 8, 16, ST))
    s["th"] = rng.choice(np.array([0, 1, 60, 240]), (N, 8, 1, 1)); s["th"][:, 0] = 1; s["th"][:, 4] = 0; s["th"][:, 7] = 240
    r = rng.random((N, 8, 1, P)); s["k"] = np.where(r < 0.25, M, np.where((r < 0.5) & (s["k"] == M), (M - 1) * rng.integers(0, 2, (N, 8, 16, P)), s["k"]))
    for q in range(N):
        for w in list(range(8)) + list(range(W - 8, W)):
            x[q, 5, :, w] = aim(rng, (0, P - 1)[(w + q) & 1])
        for g in range(8):
            w = np.flatnonzero(kind[q, g, 0] == 0)
            if len(w) == 0: continue
            xs = np.array(x[q, g][:, w]); c = spot(np.add.reduce(s["h"][q, g] * xs, axis=0))
            xs[15] = xs[15] + rng.integers(0, 3, len(w)); s["y"][q, g][:, c] = xs
            m = rng.random((16, len(w))); own = nm[q, g][:, w]
            s["k"][q, g][:, c] = np.where(m < 0.6, own, np.where(m < 0.8, M, (own + 1) & (M - 1)))
    s["x"] = x; s["nm"] = nm; s["asl"] = asl
    return pack(s)
def setup_inputs_crowd(rng):
    s = parts(rng); row = np.arange(16)[None, None, :, None]; w = np.arange(W)[None, None, None, :]
    s["e"][:, :3] = 0; s["g"][:, 0] = 0; a = rng.integers(0, 16, (8, 16, 1)); a[:, 0] = 2; s["x"][:, :3] = a[None, :3]
    for q in range(N): s["x"][q, 1, :, (0, W - 1)[q & 1]] = 15 - a[1, :, 0]
    b = rng.integers(0, 3, (N, 1, W)); s["x"][:, 2] = np.where(b == 0, a[None, 2], np.where(b == 1, 15 - a[None, 2], (a[None, 2] + 5) & 15))
    s["h"][:, 3] = 0
    one = rng.integers(0, 16, (N, 1, 1, W)); s["asl"][:, :1] = np.where(w % 4 == 0, False, np.where(w % 4 == 1, row == one, s["asl"][:, :1]))
    two = rng.integers(0, M, (8, 16, 2)); t = names(rng, two, 1.0, W); k = names(rng, two, 1.0, P)
    s["nm"][:, :4] = np.where(s["asl"], t, s["nm"])[:, :4]; s["k"][:, :4] = np.where(s["k"] < M, k, M)[:, :4]
    s["th"][:, 0] = 0; s["th"][:, 1] = 240 * rng.integers(0, 2, (N, 1, 1))
    s["e"][:, 4] = 0; s["h"][:, 4, :, 0] = AIM
    s["asl"][:, 5] = True; s["x"][:, 5] = rng.integers(1, 15, (N, 16, W)); s["g"][:, 5, :, 0] = 0; s["e"][:, 5, :, 0] = 15; s["d"][:, 5, :, 0] = 1
    for q in range(N):
        o = rng.permutation(53000); i = np.unique(spot(o), return_index=True)[1]
        i = rng.permutation(np.concatenate([i[:1], i[-1:], rng.permutation(i[1:-1])[:W - 2]]))
        s["x"][q, 4] = np.stack([lanes(int(j)) for j in o[i]], axis=1); s["th"][q, 4] = 16 * (q & 1)
        m = (2, 4, 8, W)[q & 3]; at = np.arange(m - 1, W, m); ro = rng.integers(0, 15, len(at))
        s["asl"][q, 5, ro, at] = False; s["nm"][q, 5, ro, at] = 0
    s["asl"][:, 6] = False; s["g"][:, 6] = 15; s["g"][:, 6, :, 0] = 0; s["e"][:, 6, :, 0] = np.minimum(s["e"][:, 6, :, 0], 14); s["x"][:, 6] = np.minimum(s["x"][:, 6], 14)
    s["nm"][:, 6] = np.where(row[0] == one[:, 0], 0, np.maximum(s["nm"][:, 6], 1))
    return pack(s)
def check_inputs(d):
    bad = []
    for k, lo, hi in (("fx", 0, 255), ("y0", 0, 15), ("k0", 0, M), ("x0", 0, 15), ("t0", 0, 2 * M - 1), ("dw", 1, 16), ("hw", 0, 255), ("th", 0, 240)):
        a = np.asarray(d[k]).astype(np.float64)
        if not (np.min(a) >= lo and np.max(a) <= hi): bad.append("range of " + k)
        elif not np.all(a == np.floor(a)): bad.append("whole numbers in " + k)
    a = np.asarray(d["th"]).reshape(-1, 16)
    if not np.all(a == a[:, :1]): bad.append("th alike in a group")
    return bad
def reference(fx, y0, k0, x0, t0, dw, hw, th):
    F = fx.astype(np.float32).astype(np.int32).reshape(N, 8, 16, M); Y = y0.astype(np.float32).astype(np.int32).reshape(N, 8, 16, P); K = np.array(k0, np.int32).reshape(N, 8, 16, P)
    X = x0.astype(np.float32).astype(np.int32).reshape(N, 8, 16, W); t1 = np.array(t0, np.int32).reshape(N, 8, 16, W)
    T = t1 & (M - 1); S = t1 >= M; A = np.zeros((N, 8, W), np.int32)
    dd = dw.reshape(N, 8, 16, ST); hh = hw.astype(np.int32).reshape(N, 8, 16, 1); top = th.reshape(N, 8, 16)[:, :, :1]
    row = np.arange(16, dtype=np.int32)[None, :, None]; turn = (np.arange(W) & 3)[None, :]
    for t in range(ST):
        if t > 0: X = np.roll(X, SH, axis=0); T = np.roll(T, SH, axis=0); S = np.roll(S, SH, axis=0); A = np.roll(A, SH, axis=0)
        for q in range(N):
            x = X[q]; nm = T[q]; asl = S[q]
            f = np.take_along_axis(F[q], nm.reshape(8, 1, 16 * W), 2).reshape(8, 16, 16, W)
            gu = f & 15; ef = f >> 4; xx = x[:, :, None, :]
            en = np.add.reduce((xx >= gu).astype(np.int32), axis=1) >= 9 + A[q][:, None, :]
            cand = en & ~asl; ci = cand.astype(np.int32); before = np.add.accumulate(ci, axis=1) - ci
            pos = np.minimum(turn, np.add.reduce(ci, axis=1) - 1)[:, None, :]
            go = cand & (before == pos)
            e = np.add.reduce(ef * go[:, None, :, :].astype(np.int32), axis=2, dtype=np.int32); ee = e[:, :, None, :]
            asl = asl | (cand & (before < pos))
            differ = np.abs(np.abs(xx - ef) - ee) != np.abs(np.abs(xx - ee) - ef)
            asl = asl & (np.add.reduce(differ.astype(np.int32), axis=1) < dd[q][:, :, t:t + 1])
            x = np.abs(x - e)
            u = np.add.reduce(hh[q] * x, axis=1); v = (u & (VM - 1))[:, None, :]
            nm = np.where(asl, nm, (((nm * (2 * v + 1)) >> 5) + nm + 37 * row) & (M - 1))
            c = ((u * 241) >> 6) & (P - 1)
            yc = np.take_along_axis(Y[q], c[:, None, :], 2); kc = np.take_along_axis(K[q], c[:, None, :], 2)
            hit = np.add.reduce(np.abs(yc - x), axis=1) <= top[q]; hb = hit[:, None, :]
            same = asl & (kc == nm)
            y1 = np.where(hb, yc, x); k1 = np.where(hb, np.where(same, kc, M), np.where(asl, nm, M))
            get = hb & (kc < M) & ~same
            nm = np.where(get, kc, nm); asl = asl & ~get
            for g in range(8):
                win = np.full(P, -1); np.maximum.at(win, c[g], np.arange(W)); at = np.flatnonzero(win >= 0)
                Y[q, g][:, at] = y1[g][:, win[at]]; K[q, g][:, at] = k1[g][:, win[at]]
            X[q] = x; T[q] = nm; S[q] = asl; A[q] = hit
    return {"yx": X.reshape(N, 128, W).astype(np.float32).astype(BF), "yt": (T + M * S.astype(np.int32)).reshape(N, 128, W).astype(np.float32),
            "yy": Y.reshape(N, 128, P).astype(np.float32).astype(BF), "yk": K.reshape(N, 128, P).astype(np.float32)}

@@ -1,0 +1,617 @@
+from concourse.mybir import AluOpType as OP, ActivationFunctionType as AF
+
+M, P, W, ST = 4096, 512, 160, 4
+CH = [80, 80]
+A_ENG = ["act", "act", "act"]
+G_ENG = ["act", "dve", "act"]
+E_ENG = ["dve", "dve", "dve"]
+B_ENG = "dve"
+GO_ENG = "act"
+LAG = 4000.0
+ROUNDS = 100
+SEED = 1
+JIT = 150.0
+BIG = 16384.0
+STEP = 131072.0
+NC = len(CH)
+C0 = [sum(CH[:i]) for i in range(NC)]
+NM = max(CH)
+NS = NM // 16
+MATS = ["I", "nI", "I16", "nI16", "I2", "I17", "Is", "IB", "I16B", "I32B", "nI32B", "nI128", "nI2k", "nIm",
+        "OH", "OB", "O2k", "KW", "H4", "H2n", "TRI", "TRS", "TRU", "TRV"]
+NB16 = ["sa0", "xz", "cand", "fst", "go", "mx", "b", "bz", "dy", "ady", "mM", "he", "hd", "c3", "x0s"]
+NF32 = ["n", "sv1", "sv2", "sv3", "kc", "kp", "newM", "tA", "t1", "zc", "t0f", "tM", "nk"]
+NI32 = ["w1", "v2", "prod", "sh", "sm2", "new", "c1", "c2", "t0s"]
+TILES = ["kq", "turn", "kr", "w16", "d0", "dt0", "dt1", "dt2", "dt3", "tht", "mk", "rr", "da", "db", "dc", "cm8"]
+
+SCRATCH = {
+    "ft": ("sbuf", [128, 2 * M], "bfloat16"),
+    "ys": ("sbuf", [128, P + NM], "bfloat16"), "ks": ("sbuf", [128, P + NM], "float32"), "k0s": ("sbuf", [128, P], "int32"),
+    "mats": ("sbuf", [128, 128 * len(MATS)], "bfloat16"), "i32s": ("sbuf", [128, 128], "float32"),
+    "selh": ("sbuf", [128, 144], "bfloat16"), "jrow": ("sbuf", [128, 144], "bfloat16"), "grow": ("sbuf", [128, 128], "bfloat16"),
+    "jd": ("sbuf", [128, 128], "bfloat16"),
+    "rm": ("sbuf", [128, 16 * NM], "bfloat16"), "ones": ("sbuf", [128, 16 * NM], "bfloat16"), "zr": ("sbuf", [128, NS * NM], "bfloat16"),
+    "tiles": ("sbuf", [128, NM * len(TILES)], "bfloat16"), "dl": ("sbuf", [128, NM], "float32"),
+    "cols": ("sbuf", [128, 32], "float32"), "icol": ("sbuf", [128, 8], "int32"),
+    "dws": ("sbuf", [128, 4], "int32"), "hws": ("sbuf", [128, 4], "int32"), "ths": ("sbuf", [128, 4], "int32"),
+    "off": ("sbuf", [128, W], "uint16"), "so": ("sbuf", [128, 32 * NC], "uint16"),
+    "t12": ("sbuf", [128, 2 * W], "bfloat16"),
+}
+for _n in NB16:
+    SCRATCH[_n] = ("sbuf", [128, W], "bfloat16")
+for _n in NF32:
+    SCRATCH[_n] = ("sbuf", [128, W], "float32")
+for _n in NI32:
+    SCRATCH[_n] = ("sbuf", [128, W], "int32")
+for _c in range(NC):
+    SCRATCH["fw%d" % _c] = ("sbuf", [128, 16 * CH[_c]], "bfloat16")
+    SCRATCH["e16_%d" % _c] = ("sbuf", [128, 16 * CH[_c] + 16], "bfloat16")
+    SCRATCH["wa%d" % _c] = ("sbuf", [128, 16 * CH[_c]], "bfloat16")
+    SCRATCH["wq%d" % _c] = ("sbuf", [128, 16 * CH[_c]], "bfloat16")
+    SCRATCH["xt%d" % _c] = ("sbuf", [128, 128], "bfloat16")
+    SCRATCH["ct%d" % _c] = ("sbuf", [128, 128], "bfloat16")
+    SCRATCH["cd%d" % _c] = ("sbuf", [128, 8], "bfloat16")
+    SCRATCH["eq%d" % _c] = ("sbuf", [128, 8 * NS * (NS + 1)], "bfloat16")
+for _s in range(ST):
+    SCRATCH["ox%d" % _s] = ("sbuf", [128, 3 * W], "bfloat16")
+    SCRATCH["ot%d" % _s] = ("sbuf", [128, W], "float32")
+    if _s:
+        SCRATCH["lx%d" % _s] = ("sbuf", [128, 3 * W], "bfloat16")
+        SCRATCH["lt%d" % _s] = ("sbuf", [128, W], "float32")
+for _b in range(8):
+    SCRATCH["pb%d" % _b] = ("psum", [128, 512], "float32")
+
+LOADS = ["fa", "fb", "t0", "x0", "y0", "k0", "dw", "hw", "th"]
+SEMAPHORES = ["pe", "dve", "act", "pool", "sent"] + ["l" + s for s in LOADS] + ["oyy", "oyk"]
+for _c in range(NC):
+    SEMAPHORES += ["oyx%d" % _c, "oyt%d" % _c]
+    for _s in range(1, ST):
+        SEMAPHORES += ["ax%d_%d" % (_s, _c), "at%d_%d" % (_s, _c)]
+
+CYC = 1.0
+PCYC = 0.5
+FIXV, FIXA, GATH, SCAT, TT2 = 55.0, 65.0, 1.55, 3.8, 2.0
+LAT_X, LAT_S, LAT_NET = 120.0, 80.0, 3000.0
+
+
+def V(name, c0=0, c1=None, step=1, p0=0, p1=128):
+    if c1 is None:
+        c1 = SCRATCH[name][1][1]
+    return (name, p0, p1, c0, c1, step)
+
+
+def IND(win, off):
+    return ("#", win, off)
+
+
+def width(v):
+    if v[0] == "#":
+        return 16 * width(v[2])
+    return len(range(v[3], v[4], v[5]))
+
+
+def two_bytes(v):
+    return SCRATCH[v[1][0] if v[0] == "#" else v[0]][2] in ("bfloat16", "uint16")
+
+
+def in_psum(v):
+    return v[0] != "#" and SCRATCH[v[0]][0] == "psum"
+
+
+def ap(T, v):
+    if not isinstance(v, tuple):
+        return v
+    if v[0] == "#":
+        return ap(T, v[1]).indirect(ap(T, v[2]))
+    if v[5] == 1:
+        return T[v[0]][v[1]:v[2], v[3]:v[4]]
+    return T[v[0]][v[1]:v[2], v[3]:v[4]:v[5]]
+
+
+def plan():
+    ops = []
+    wr, rd, bank = {}, {}, {}
+    cur = [0.0]
+
+    def add(eng, cost, fn, reads, writes, lat=0.0, sem=None):
+        i = len(ops)
+        deps = {}
+
+        def dep(j, sync):
+            deps[j] = deps.get(j, False) or sync or ops[j]["sem"] is not None or ops[j]["eng"] != eng
+
+        rs, ws = [], []
+        for v in reads:
+            if isinstance(v, tuple):
+                rs += [v[1], v[2]] if v[0] == "#" else [v]
+        for v in writes:
+            if v[0] == "#":
+                ws.append(v[1])
+                rs.append(v[2])
+            else:
+                ws.append(v)
+        for v in rs + ws:
+            if in_psum(v):
+                for j in bank.setdefault(v[0], {}).values():
+                    dep(j, False)
+        for v in rs:
+            for (j, a, b) in wr.get(v[0], []):
+                if a < v[4] and v[3] < b:
+                    dep(j, True)
+        for v in ws:
+            if not in_psum(v):
+                for (j, a, b) in wr.get(v[0], []) + rd.get(v[0], []):
+                    if a < v[4] and v[3] < b:
+                        dep(j, True)
+        for v in rs + ws:
+            if in_psum(v):
+                bank[v[0]][eng] = i
+        for v in ws:
+            full = v[1] == 0 and v[2] == 128 and v[5] == 1
+            wr[v[0]] = [e for e in wr.get(v[0], []) if not (full and v[3] <= e[1] and e[2] <= v[4])] + [(i, v[3], v[4])]
+            if full:
+                rd[v[0]] = [e for e in rd.get(v[0], []) if not (v[3] <= e[1] and e[2] <= v[4])]
+        for v in rs:
+            if not in_psum(v):
+                rd.setdefault(v[0], []).append((i, v[3], v[4]))
+        deps.pop(i, None)
+        ops.append({"eng": eng, "cost": cost, "fn": fn, "deps": deps, "lat": lat, "sem": sem, "lag": cur[0],
+                    "tag": (ws[0][0] if ws else "out")})
+        return i
+
+    def ecost(eng, out, ins, per):
+        if out[0] == "#":
+            per = SCAT
+        elif ins[0][0] == "#":
+            per = max(per, GATH)
+        return (FIXV if eng == "dve" else FIXA) + max(16, width(out) * per) * CYC
+
+    def ts(out, in0, s1, op0, s2=None, op1=None):
+        per = 0.5 if two_bytes(out) and two_bytes(in0) else 1.0
+        if op1 is None:
+            fn = lambda g, T, x: g.vector.tensor_scalar(ap(T, out), ap(T, in0), ap(T, s1), None, op0)
+        else:
+            fn = lambda g, T, x: g.vector.tensor_scalar(ap(T, out), ap(T, in0), ap(T, s1), ap(T, s2), op0, op1)
+        add("dve", ecost("dve", out, [in0], per), fn, [in0, s1, s2], [out])
+
+    def tt(out, in0, in1, op):
+        per = 1.0 if in_psum(in0) or in_psum(in1) else TT2
+        add("dve", ecost("dve", out, [in0], per), lambda g, T, x: g.vector.tensor_tensor(ap(T, out), ap(T, in0), ap(T, in1), op), [in0, in1], [out])
+
+    def cp(out, in0):
+        per = 0.5 if two_bytes(out) and two_bytes(in0) else 1.0
+        add("dve", ecost("dve", out, [in0], per), lambda g, T, x: g.vector.tensor_copy(ap(T, out), ap(T, in0)), [in0], [out])
+
+    def ms(out, val):
+        add("dve", ecost("dve", out, [out], 0.5 if two_bytes(out) else 1.0), lambda g, T, x: g.vector.memset(ap(T, out), val), [], [out])
+
+    def scan(out, d0, d1, op0=OP.add):
+        add("dve", ecost("dve", out, [d1], 1.0),
+            lambda g, T, x: g.vector.tensor_tensor_scan(ap(T, out), ap(T, d0), ap(T, d1), 0.0, op0, OP.min), [d0, d1], [out])
+
+    def act(out, in0, func, bias=0.0, scale=1.0):
+        if func == AF.Copy:
+            fn = lambda g, T, x: g.scalar.activation(ap(T, out), ap(T, in0), func)
+        else:
+            fn = lambda g, T, x: g.scalar.activation(ap(T, out), ap(T, in0), func, bias=ap(T, bias), scale=ap(T, scale))
+        add("act", ecost("act", out, [in0], 1.0), fn, [in0, bias, scale], [out])
+
+    def mm(out, lhs, rhs, start, stop):
+        c = max(64, width(rhs)) * PCYC * (1 if two_bytes(rhs) else 4)
+        add("pe", c, lambda g, T, x: g.tensor.matmul(ap(T, out), ap(T, lhs), ap(T, rhs), start, stop), [lhs, rhs], [out], lat=60.0)
+
+    def group(out, terms):
+        for i, (lhs, rhs) in enumerate(terms):
+            mm(out, lhs, rhs, i == 0, i == len(terms) - 1)
+
+    def iota(out, pattern, base, ch):
+        if SCRATCH[out[0]][2] == "int32":
+            fn = lambda g, T, x: g.iota(ap(T, out), pattern, base, ch)
+        else:
+            fn = lambda g, T, x: g.iota(ap(T, out), pattern, base, ch, allow_small_or_imprecise_dtypes=True)
+        add("pool", 130 + 2 * width(out) * CYC, fn, [], [out])
+
+    def sel(out, in0, pattern, cmp, fill, base, ch):
+        add("pool", 170 + 2 * width(out) * CYC, lambda g, T, x: g.affine_select(ap(T, out), ap(T, in0), pattern, cmp, fill, base, ch), [in0], [out])
+
+    def load(q, out, src, sem, lat):
+        add(q, 60.0, lambda g, T, x: (g.sync if q == "sp" else g.scalar).dma_start(ap(T, out), T[src][:]), [], [out], lat=lat, sem=sem)
+
+    def store(q, dst, c0, c1, src, sem):
+        add(q, 60.0, lambda g, T, x: (g.sync if q == "sp" else g.scalar).dma_start(T[dst][:, c0:c1], ap(T, src)), [src], [], lat=2000.0, sem=sem)
+
+    def send(src, dst, sem):
+        i = add("pool", 600.0, lambda g, T, x: g.remote_dma(ap(T, dst), ap(T, src), T.sem[sem], T.sem.sent, x["pid"], x["rid"], x["mask"]), [src], [])
+        ops[i]["send"] = True
+        j = add("net", 0.0, None, [], [dst], lat=LAT_NET, sem=sem)
+        ops[j]["deps"][i] = False
+
+    def mat(n):
+        return V("mats", 128 * MATS.index(n), 128 * MATS.index(n) + 128)
+
+    def tile(n, w=NM):
+        return V("tiles", NM * TILES.index(n), NM * TILES.index(n) + w)
+
+    def col(i):
+        return V("cols", i, i + 1)
+
+    cur[0] = -1e6
+    load("sp", V("ft", 0, M), "fx", "lfa", 6000.0)
+    load("act", V("t0s"), "t0", "lt0", 2000.0)
+    load("act", V("x0s"), "x0", "lx0", 2000.0)
+    cur[0] = 0.0
+    load("act", V("hws", 0, 1), "hw", "lhw", 2500.0)
+    load("act", V("dws"), "dw", "ldw", 2500.0)
+    load("act", V("ths", 0, 1), "th", "lth", 2500.0)
+    load("sp", V("k0s"), "k0", "lk0", 3000.0)
+    ops[-1]["deps"][0] = True
+    load("sp", V("ys", 0, P), "y0", "ly0", 3500.0)
+    ops[-1]["deps"][len(ops) - 2] = False
+    load("sp", V("ft", M, 2 * M), "fx", "lfb", 8000.0)
+    ops[-1]["deps"][len(ops) - 2] = False
+
+    KC, G16, SC, SC256, K37, G15, KQ, HF, H4C, H2C, THC, TA_, TB_, KR, DF = 0, 1, 2, 3, 4, 5, 6, 7, 8, 9, 10, 11, 12, 13, 16
+    iota(V("jd"), [[1, 128]], 0, -1)
+    iota(V("icol", 0, 1), [[0, 1]], 0, 1)
+    iota(V("grow"), [[16, 8], [0, 16]], 0, 0)
+    iota(V("jrow"), [[1, 144]], 0, 0)
+    ms(V("ones"), 1.0)
+    sel(V("rm"), V("ones"), [[1, NM], [0, 16]], OP.is_equal, 0.0, 0, -1)
+    ts(mat("I"), V("jd"), 0.0, OP.is_equal)
+    for n, c in (("nI", -1.0), ("I16", 16.0), ("nI16", -16.0), ("I2", 2.0), ("I17", 17.0), ("Is", 1 / 16), ("IB", BIG), ("I16B", 16 * BIG),
+                 ("I32B", 32 * BIG), ("nI32B", -32 * BIG), ("nI128", -32 * BIG / M), ("nI2k", -2048.0), ("nIm", -2.0 / M)):
+        ts(mat(n), V("jd"), 0.0, OP.is_equal, c, OP.mult)
+    ts(V("i32s"), V("jd"), 0.0, OP.is_equal)
+    ts(V("icol", 1, 2), V("icol", 0, 1), 15, OP.bitwise_and)
+    ts(V("icol", 2, 3), V("icol", 0, 1), 112, OP.bitwise_and)
+    cp(V("cols", KC, G16 + 1), V("icol", 1, 3))
+    ts(col(SC), col(KC), -STEP, OP.mult, 15 * STEP, OP.add)
+    ts(col(SC256), col(KC), -STEP, OP.mult, 15 * STEP + 256, OP.add)
+    ts(col(K37), col(KC), 37.0, OP.mult)
+    ts(col(G15), col(G16), 15.0, OP.add)
+    ts(col(KQ), col(KC), -0.5, OP.mult, -32.0, OP.add)
+    ts(col(KR), col(KC), 0.5, OP.mult, -7.0, OP.add)
+    ts(V("selh"), V("jrow"), col(G15), OP.is_equal, BIG / 2, OP.mult)
+    ts(col(H4C), V("hws", 0, 1), 4.0, OP.mult)
+    ts(col(H2C), V("hws", 0, 1), -2.0, OP.mult)
+    for n, c in (("OH", -0.5), ("OB", BIG), ("O2k", -2048.0), ("KW", col(KC)), ("H4", col(H4C)), ("H2n", col(H2C))):
+        ts(mat(n), V("grow"), col(G16), OP.is_equal, c, OP.mult)
+    sel(mat("TRS"), mat("OH"), [[1, 128]], OP.is_gt, 0.0, 0, -1)
+    sel(mat("TRI"), mat("TRS"), [[1, 128]], OP.not_equal, 32.0, 0, -1)
+    sel(mat("TRV"), mat("OH"), [[-1, 128]], OP.is_gt, 0.0, 0, 1)
+    sel(mat("TRU"), mat("TRV"), [[1, 128]], OP.not_equal, 0.5, 0, -1)
+    iota(tile("turn"), [[0, NM // 4], [1, 4]], 0, 0)
+    iota(tile("w16"), [[16, NM]], 2048, 0)
+    iota(tile("rr"), [[0, NS], [1, 16]], 0, 0)
+    ts(tile("kq"), tile("turn"), col(KQ), OP.add)
+    ts(tile("mk"), tile("rr"), col(KC), OP.not_equal)
+    ts(tile("da"), tile("rr"), col(KC), OP.is_equal, 64 * STEP, OP.mult)
+    ts(tile("db"), tile("rr"), col(KC), OP.is_gt, -STEP, OP.mult)
+    tt(tile("d0"), tile("da"), tile("db"), OP.add)
+    ts(V("cols", DF, DF + 4), V("dws"), -8.5, OP.add)
+    for s in range(ST):
+        ts(tile("dt%d" % s), V("ones", 0, NM), col(DF + s), OP.mult)
+    ts(col(HF), V("ths", 0, 1), -1.0, OP.mult)
+    ts(col(TA_), col(KC), 0.0, OP.is_equal, col(HF), OP.mult)
+    ts(col(TB_), col(KC), 1.0, OP.is_equal, -0.5, OP.mult)
+    tt(col(THC), col(TA_), col(TB_), OP.add)
+    ts(tile("tht"), V("ones", 0, NM), col(THC), OP.mult)
+    dve_a = "dve" in A_ENG
+    if dve_a:
+        for i, e in enumerate(A_ENG):
+            if 32 * i < NM:
+                ms(V("tiles", tile("cm8")[3] + 32 * i, tile("cm8")[3] + min(NM, 32 * i + 32)), -8.0 if e == "dve" else 0.0)
+    iota(V("dl"), [[1, NM]], 256, 0)
+    ts(tile("dc"), tile("mk"), -4096.0, OP.mult)
+    tt(V("dl"), V("dl"), tile("dc"), OP.add)
+    sel(V("zr", p0=0, p1=32), V("ones", 0, NS * NM, p0=0, p1=32), [[1, NS], [0, NM]], OP.is_equal, 0.0, 0, -1)
+    sel(V("zr", p0=32, p1=64), V("ones", 0, NS * NM, p0=32, p1=64), [[-16, NS], [1, NM]], OP.is_ge, 0.0, 0, -1)
+    ms(V("ys", P, P + NM), 0.0)
+    ms(V("ks", P, P + NM), 0.0)
+    cp(V("ks", 0, P), V("k0s"))
+    for c in range(NC):
+        ms(V("ct%d" % c, p0=0, p1=32), 0.0)
+        for h in range(0, 128, NM):
+            e = min(128, h + NM)
+            ts(V("ct%d" % c, h, e, p0=32, p1=64), V("tiles", tile("rr")[3], tile("rr")[3] + e - h, p0=32, p1=64),
+               V("cols", KC, KC + 1, p0=32, p1=64), OP.is_equal, 1024.0, OP.mult)
+        ms(V("e16_%d" % c, 16 * CH[c], 16 * CH[c] + 16), 2064.0)
+
+    nbk = 8 // NC
+
+    def walk(s, c):
+        n, c0 = CH[c], C0[c]
+        ns = n // 16
+        cur[0] = LAG * c
+        al, be = "pb%d" % (c * nbk), "pb%d" % (c * nbk + 1)
+        wide = ["pb%d" % (c * nbk + 2 + i) for i in range(nbk - 2)]
+
+        def N(name):
+            return V(name, c0, c0 + n)
+
+        def S(name):
+            return V(name, c0 + 15, c0 + n, 16)
+
+        def t(name):
+            return tile(name, n)
+
+        fw, e16, wa, wq = "fw%d" % c, "e16_%d" % c, "wa%d" % c, "wq%d" % c
+        xo, ho, sw = [V("ox%d" % s, 3 * c0 + i * n, 3 * c0 + (i + 1) * n) for i in range(3)]
+        to = V("ot%d" % s, c0, c0 + n)
+        pn, pk = V(be, 512 - n, 512), (V(be, 512 - 2 * n, 512 - n) if 8 * ns * (ns + 1) + 2 * n <= 512 else N("nk"))
+        if s == 0:
+            x, hit0, sa, tin = N("x0s"), None, N("sa0"), N("t0f")
+            ts(N("w1"), N("t0s"), M - 1, OP.bitwise_and)
+            cp(N("off"), N("w1"))
+            cp(tin, N("t0s"))
+            act(sa, tin, AF.Sign, -4095.5)
+            win = V("ft", 0, M)
+        else:
+            x, hit0, sa = [V("lx%d" % s, 3 * c0 + i * n, 3 * c0 + (i + 1) * n) for i in range(3)]
+            tin = V("lt%d" % s, c0, c0 + n)
+            cp(N("off"), tin)
+            win = V("ft")
+        group(V(be, 0, 128, p1=n), [(x, mat("I"))])
+        act(V("xt%d" % c, p1=n), V(be, 0, 128, p1=n), AF.Copy)
+        act(N("xz"), x, AF.Relu, 256.0, -256.0)
+        group(pn, [(V("i32s"), tin), (mat("nI2k"), sa), (mat("nI2k"), V("ones", 0, n))])
+        act(N("n"), pn, AF.Copy)
+        act(pk, pn, AF.Identity, col(K37))
+        act(N("tM"), pn, AF.Identity, float(M))
+        for i, a in enumerate(range(0, n, 32)):
+            b = min(n, a + 32)
+            src = IND(win, V("off", c0 + a, c0 + b))
+            if G_ENG[i] == "act":
+                act(V(fw, 16 * a, 16 * b), src, AF.Copy)
+            else:
+                cp(V(fw, 16 * a, 16 * b), src)
+            if E_ENG[i] == "act":
+                act(V(e16, 16 * a, 16 * b), V(fw, 16 * a, 16 * b), AF.Identity, 2056.5)
+            else:
+                ts(V(e16, 16 * a, 16 * b), V(fw, 16 * a, 16 * b), 2056.5, OP.add)
+            z = V(wide[i % len(wide)], 0, 16 * (b - a))
+            group(z, [(V("xt%d" % c, p1=n), V("rm", 16 * a, 16 * b, p1=n)), (mat("nI"), V(fw, 16 * a, 16 * b)), (mat("I"), V(e16, 16 * a, 16 * b))])
+            if A_ENG[i] == "act":
+                act(V(wa, 16 * a, 16 * b), z, AF.Sign, 2063.5, -1.0)
+            else:
+                ts(V(wa, 16 * a, 16 * b), z, 2064.0, OP.is_lt, 2.0, OP.mult)
+        terms = [(mat("I16B"), sa)]
+        if hit0:
+            terms.append((mat("IB"), hit0))
+        if dve_a:
+            terms.append((mat("IB"), t("cm8")))
+        group(V(al, 0, n), terms + [(V("selh", 15 - k, 143 - k), V(wa, k, 16 * n, 16)) for k in range(16)])
+        act(N("cand"), V(al, 0, n), AF.Sign, -16.5 * BIG, -1.0)
+        group(V(al, 0, n), [(mat("I"), t("kq")), (mat("TRI"), N("cand"))])
+        act(N("fst"), V(al, 0, n), AF.Sign, 0.5)
+        group(V(al, 0, n), [(mat("TRU"), N("fst"))])
+        if GO_ENG == "act":
+            act(N("go"), V(al, 0, n), AF.Relu, col(KR))
+        else:
+            ts(N("go"), V(al, 0, n), col(KR), OP.add, 0.0, OP.max)
+        group(V(be, 0, n), [(mat("I"), t("w16")), (mat("KW"), N("go")), (mat("O2k"), N("go"))])
+        scan(N("sv1"), t("d0"), V(be, 0, n))
+        ko, co, lo = V("so", 32 * c, 32 * c + ns), V("so", 32 * c + 8, 32 * c + 8 + ns), V("so", 32 * c + 16, 32 * c + 16 + ns)
+        ts(ko, S("sv1"), col(SC), OP.add, float(16 * n), OP.min)
+        if B_ENG == "act":
+            act(N("b"), IND(V(e16), ko), AF.Identity, -129.0, 1 / 16)
+        else:
+            ts(N("b"), IND(V(e16), ko), 1 / 16, OP.mult, -129.0, OP.add)
+        act(N("bz"), IND(V(e16), ko), AF.Relu, 33280.0, -16.0)
+        tt(N("mx"), N("b"), x, OP.max)
+        group(V(be, 0, n), [(mat("H2n"), x), (mat("H2n"), N("b")), (mat("H4"), N("mx"))])
+        group(V(al, 0, n), [(mat("I17"), x), (mat("I"), N("xz")), (mat("I"), N("bz")), (mat("nI16"), N("mx"))])
+        group(V(al, n, 2 * n), [(mat("Is"), N("xz")), (mat("Is"), N("bz")), (mat("I"), N("mx"))])
+        group(V(al, 2 * n, 3 * n), [(mat("nI"), x), (mat("nI"), N("b")), (mat("I2"), N("mx"))])
+        t1_, t2_ = V("t12", 2 * c0, 2 * c0 + n), V("t12", 2 * c0 + n, 2 * c0 + 2 * n)
+        act(V("t12", 2 * c0, 2 * c0 + 2 * n), V(al, 0, 2 * n), AF.Relu, -1.0)
+        act(xo, V(al, 2 * n, 3 * n), AF.Copy)
+        ts(N("c1"), V(be, 0, n), 120.5, OP.mult)
+        ts(N("w1"), V(be, 0, n), 1.0, OP.add)
+        ts(N("c2"), N("c1"), 6, OP.logical_shift_right, P - 1, OP.bitwise_and)
+        ts(N("c3"), N("c2"), -256.0, OP.add)
+        scan(N("sv2"), t("d0"), N("c3"))
+        ts(co, S("sv2"), col(SC256), OP.add)
+        tt(N("dy"), IND(V("ys", 0, P), co), xo, OP.subtract)
+        act(N("kc"), IND(V("ks", 0, P), co), AF.Copy)
+        act(N("ady"), N("dy"), AF.Abs)
+        ts(N("v2"), N("w1"), M - 1, OP.bitwise_and)
+        tt(N("prod"), pn, N("v2"), OP.mult)
+        ts(N("sh"), N("prod"), 5, OP.logical_shift_right)
+        tt(N("sm2"), pk, N("sh"), OP.add)
+        ts(N("new"), N("sm2"), M - 1, OP.bitwise_and)
+        group(V(be, 0, n), [(mat("OB"), t("tht")), (mat("OB"), N("ady"))])
+        tt(N("kp"), V(be, 0, n), N("kc"), OP.max)
+        ts(ho, V(be, 0, n), 0.0, OP.is_lt)
+        if s == ST - 1:
+            store("act", "yx", c0, c0 + n, xo, "oyx%d" % c)
+        ts(N("mM"), N("kp"), float(M), OP.is_lt, float(M), OP.mult)
+        tt(N("he"), pn, N("kp"), OP.is_equal)
+        cd, ct, eq = V("cd%d" % c, 0, ns), "ct%d" % c, "eq%d" % c
+        act(cd, S("sv2"), AF.Identity, col(SC))
+        group(V(be, 0, 128, p1=ns), [(cd, mat("I"))])
+        act(V(ct, p1=ns), V(be, 0, 128, p1=ns), AF.Identity, 0.0, -1.0)
+        o = 0
+        for j in range(ns):
+            wd = 16 * (j + 1)
+            group(V(be, o, o + wd), [(V(ct, p1=48), V("zr", j * NM, j * NM + wd, p1=48)), (mat("I"), V("c3", c0, c0 + wd))])
+            o += wd
+        ts(V(eq, 0, o), V(be, 0, o), 0.0, OP.is_equal, 1 / 16, OP.mult)
+        mm(V(be, 0, n), mat("I"), N("c3"), True, False)
+        mm(V(be, 0, n), mat("IB"), t("mk"), False, False)
+        o = 0
+        for j in range(ns):
+            wd = 16 * (j + 1)
+            mm(V(be, 0, wd), mat("OB"), V(eq, o, o + wd), False, j == ns - 1)
+            o += wd
+        scan(N("sv3"), V("dl", 0, n), V(be, 0, n), OP.max)
+        ts(lo, S("sv3"), 256.0, OP.add)
+        tt(N("newM"), N("new"), N("mM"), OP.add)
+        tt(N("tA"), N("kp"), N("newM"), OP.min)
+        npc = -(-16 // (512 // n))
+        cuts = [-(-16 * i // npc) for i in range(npc + 1)]
+        pacc = V(al, 0, n)
+        for j, (lhs, rhs) in enumerate([(mat("IB"), t("dt%d" % s)), (mat("I16B"), sa), (mat("I16B"), N("fst")), (mat("nI32B"), N("go"))]):
+            mm(pacc, lhs, rhs, j == 0, False)
+        for i in range(npc):
+            ka, kb = cuts[i], cuts[i + 1]
+            zb, zc = wide[0], wide[1]
+            for k in range(ka, kb):
+                group(V(zb, (k - ka) * n, (k - ka + 1) * n), [(mat("nI"), V(e16, k, 16 * n, 16)), (mat("I16"), t1_)])
+            act(V(wa, ka * n, kb * n), V(zb, 0, (kb - ka) * n), AF.Sign, 2072.0)
+            for k in range(ka, kb):
+                group(V(zc, (k - ka) * n, (k - ka + 1) * n), [(mat("nI"), V(e16, k, 16 * n, 16)), (mat("I16"), t2_)])
+            ts(V(wq, ka * n, kb * n), V(zc, 0, (kb - ka) * n), -2080.0, OP.is_equal, 2.0, OP.mult)
+        for i in range(npc):
+            for src in (wa, wq):
+                for k in range(cuts[i], cuts[i + 1]):
+                    mm(pacc, V("selh", 15 - k, 143 - k), V(src, k * n, (k + 1) * n), False, False)
+        mm(pacc, mat("nI128"), N("mM"), False, False)
+        mm(pacc, mat("I32B"), N("he"), False, True)
+        tt(N("t1"), pacc, N("tA"), OP.max)
+        tt(to, N("tM"), N("t1"), OP.min)
+        if s < ST - 1:
+            send(to, V("lt%d" % (s + 1), c0, c0 + n), "at%d_%d" % (s + 1, c))
+        else:
+            store("sp", "yt", c0, c0 + n, to, "oyt%d" % c)
+        act(sw, to, AF.Sign, -4095.5)
+        if s < ST - 1:
+            send(V("ox%d" % s, 3 * c0, 3 * c0 + 3 * n), V("lx%d" % (s + 1), 3 * c0, 3 * c0 + 3 * n), "ax%d_%d" % (s + 1, c))
+        tt(N("hd"), N("dy"), ho, OP.mult)
+        group(V(be, 0, n), [(mat("I2"), ho), (mat("nIm"), N("mM")), (mat("nI"), sw)])
+        ts(N("zc"), V(be, 0, n), 0.0, OP.is_gt, float(M), OP.mult)
+        return xo, lo
+
+    for s in range(ST):
+        left = [walk(s, c) for c in range(NC)]
+        for c in range(NC):
+            xo, lo = left[c]
+            a, b = C0[c], C0[c] + CH[c]
+            cur[0] = LAG * c
+            tt(IND(V("ys"), lo), xo, V("hd", a, b), OP.add)
+            tt(IND(V("ks"), lo), V("n", a, b), V("zc", a, b), OP.max)
+    store("act", "yy", 0, P, V("ys", 0, P), "oyy")
+    store("sp", "yk", 0, P, V("ks", 0, P), "oyk")
+    return ops
+
+
+def schedule(ops):
+    n = len(ops)
+    pred = [[] for _ in range(n)]
+    succ = [[] for _ in range(n)]
+    for i, o in enumerate(ops):
+        for j, sync in o["deps"].items():
+            gp = (ops[j]["lat"] + (LAT_S if ops[j]["eng"] == o["eng"] else LAT_X)) if sync else 0.0
+            pred[i].append((j, gp))
+            succ[j].append((i, gp))
+    cost = [max(o["cost"], 1.0) for o in ops]
+
+    def place(seq, before, head):
+        busy, end = {}, [0.0] * n
+        for i in seq:
+            st = max([head[i]] + [end[j] + gp for j, gp in before[i]])
+            lst = busy.setdefault(ops[i]["eng"], [])
+            lo, hi = 0, len(lst)
+            while lo < hi:
+                mid = (lo + hi) // 2
+                if lst[mid][1] <= st:
+                    lo = mid + 1
+                else:
+                    hi = mid
+            while lo < len(lst) and lst[lo][0] < st + cost[i]:
+                st = max(st, lst[lo][1])
+                lo += 1
+            lst.insert(lo, (st, st + cost[i]))
+            end[i] = st + cost[i]
+        return end
+
+    z = [SEED]
+
+    def rnd():
+        z[0] = (z[0] * 1103515245 + 12345) % 2147483648
+        return z[0] / 2147483648
+
+    def by_key(key):
+        for i in range(n - 1, -1, -1):
+            for k, gp in succ[i]:
+                key[i] = max(key[i], key[k] + 1e-3)
+        return sorted(range(n), key=lambda i: (-key[i], i))
+
+    pri = [0.0] * n
+    for i in range(n - 1, -1, -1):
+        pri[i] = cost[i] + max([ops[i]["lat"]] + [gp + pri[k] for k, gp in succ[i]])
+    seq = by_key([pri[i] - ops[i]["lag"] for i in range(n)])
+    zero, tail = [0.0] * n, [o["lat"] for o in ops]
+    best = None
+    for r in range(ROUNDS):
+        for p in range(2):
+            end = place(seq, pred, zero)
+            span = max(end[i] + tail[i] for i in range(n))
+            if best is None or span <= best[0]:
+                best = (span, end)
+            back = place(sorted(range(n), key=lambda i: (-end[i], -i)), succ, tail)
+            seq = sorted(range(n), key=lambda i: (-back[i], i))
+        seq = by_key([cost[i] - best[1][i] + JIT * rnd() for i in range(n)])
+    span, end = best
+    order = {}
+    for i in sorted(range(n), key=lambda i: (end[i] - cost[i], i)):
+        ops[i]["at"] = end[i] - cost[i]
+        order.setdefault(ops[i]["eng"], []).append(i)
+    return order, span
+
+
+CACHE = {}
+
+
+def rank_program(g, core, T, topo):
+    rank = T.rank_of(core)
+    if rank is None:
+        return
+    if not CACHE:
+        CACHE["ops"] = plan()
+        CACHE["order"] = schedule(CACHE["ops"])[0]
+    ops, order = CACHE["ops"], CACHE["order"]
+    nr = len(T.cores)
+    nxt, prv = T.cores[(rank + 1) % nr], T.cores[(rank - 1) % nr]
+    rid, pid = topo.addr(nxt, core)
+    ctx = {"rid": rid, "pid": pid, "mask": topo.mask(core, nxt)}
+    n_out, n_in = len(topo.engines(core, nxt)), len(topo.engines(prv, core))
+    place = {i: k for lst in order.values() for k, i in enumerate(lst)}
+    waits, needed = {}, set()
+    for e, lst in order.items():
+        seen = {}
+        for i in lst:
+            want = {}
+            if e == "pool" and place[i] and not ops[i].get("send") and not ops[lst[place[i] - 1]].get("send"):
+                want[e] = lst[place[i] - 1]
+            for j, sync in ops[i]["deps"].items():
+                key = ops[j]["sem"] or ops[j]["eng"]
+                if sync and place[j] > seen.get(key, -1) and (key not in want or place[j] > place[want[key]]):
+                    want[key] = j
+            for key, j in want.items():
+                seen[key] = place[j]
+                needed.add(j)
+            waits[i] = list(want.values())
+    mark, total = {}, {}
+    for e, lst in order.items():
+        for i in lst:
+            if ops[i]["sem"]:
+                mark[i] = (ops[i]["sem"], n_in if e == "net" else 16)
+                total[ops[i]["sem"]] = mark[i][1]
+            elif i in needed:
+                total[e] = total.get(e, 0) + 1
+                mark[i] = (e, total[e])
+    queues = {"pe": g.tensor, "dve": g.vector, "act": g.scalar, "pool": g, "sp": g.sync}
+    sends = 0
+    for e, q in queues.items():
+        for i in order.get(e, []):
+            for j in waits[i]:
+                q.wait_ge(T.sem[mark[j][0]], mark[j][1])
+            ins = ops[i]["fn"](g, T, ctx)
+            if ops[i].get("send"):
+                sends += 1
+            elif i in mark:
+                ins.then_inc(T.sem[mark[i][0]], 16 if ops[i]["sem"] else 1)
+    for sem, cnt in total.items():
+        g.wait_ge(T.sem[sem], cnt)
+    g.wait_ge(T.sem.sent, sends * n_out)

@@ -2,40 +2,46 @@ from concourse.mybir import AluOpType as OP, ActivationFunctionType as AF
 
 M, P, W, ST = 4096, 512, 160, 4
 CH = [80, 80]
-A_ENG = ["act", "act", "act"]
-G_ENG = ["act", "dve", "act"]
-E_ENG = ["dve", "dve", "dve"]
-B_ENG = "dve"
-GO_ENG = "act"
+A_ENG = ["dve", "dve", "dve"]
+G_ENG = ["act", "act", "act"]
+NLOAD, NFIX = 4, 8
 LAG = 4000.0
-ROUNDS = 100
+ROUNDS = 60
 SEED = 1
 JIT = 150.0
 BIG = 16384.0
 STEP = 131072.0
+XO = 2320.0
+LOW = 240.0
+FOLD = 0.192 / 16
+MAGIC = 1.5 * 2 ** 17
+VB = 786432.0
 NC = len(CH)
 C0 = [sum(CH[:i]) for i in range(NC)]
 NM = max(CH)
 NS = NM // 16
-MATS = ["I", "nI", "I16", "nI16", "I2", "I17", "Is", "IB", "I16B", "I32B", "nI32B", "nI128", "nI2k", "nIm",
-        "OH", "OB", "O2k", "KW", "H4", "H2n", "TRI", "TRS", "TRU", "TRV"]
-NB16 = ["sa0", "xz", "cand", "fst", "go", "mx", "b", "bz", "dy", "ady", "mM", "he", "hd", "c3", "x0s"]
-NF32 = ["n", "sv1", "sv2", "sv3", "kc", "kp", "newM", "tA", "t1", "zc", "t0f", "tM", "nk"]
-NI32 = ["w1", "v2", "prod", "sh", "sm2", "new", "c1", "c2", "t0s"]
-TILES = ["kq", "turn", "kr", "w16", "d0", "dt0", "dt1", "dt2", "dt3", "tht", "mk", "rr", "da", "db", "dc", "cm8"]
+DIAG = {"I": 1.0, "nI": -1.0, "I2": 2.0, "I17": 17.0, "nI16": -16.0, "IB": BIG, "I16B": 16 * BIG, "nI16B": -16 * BIG, "I32B": 32 * BIG,
+        "Im": -32 * BIG / M, "nI2k": -2048.0, "I240": LOW, "Iv": VB, "nIm": -2.0 / M}
+MATS = list(DIAG) + ["OH", "On2", "OB", "nOB", "O2B", "O1k", "nO1k", "KW", "nKW", "Hp", "Hn", "H2", "TRI", "TRS", "TRL", "TRV"]
+NB16 = ["sa", "cand", "mx", "e", "bz", "tq", "xp", "r", "my", "yg", "mM", "he", "hd", "c3", "x0s", "sw"]
+NF32 = ["n", "sv1", "sv2", "sv3", "kc", "kp", "prod", "newM", "tA", "t1", "zc", "t0f", "tout"]
+NI32 = ["w1", "sm", "new", "t0s"]
+TILES = ["turn", "w16", "d0", "dt0", "dt1", "dt2", "dt3", "tht", "mk", "rr", "da", "db", "dc", "cm8"]
 
 SCRATCH = {
-    "ft": ("sbuf", [128, 2 * M], "bfloat16"),
+    "fr": ("sbuf", [128, M], "bfloat16"), "fq": ("sbuf", [128, M], "bfloat16"), "ft": ("sbuf", [128, 2 * M], "bfloat16"),
     "ys": ("sbuf", [128, P + NM], "bfloat16"), "ks": ("sbuf", [128, P + NM], "float32"), "k0s": ("sbuf", [128, P], "int32"),
     "mats": ("sbuf", [128, 128 * len(MATS)], "bfloat16"), "i32s": ("sbuf", [128, 128], "float32"),
-    "selh": ("sbuf", [128, 144], "bfloat16"), "jrow": ("sbuf", [128, 144], "bfloat16"), "grow": ("sbuf", [128, 128], "bfloat16"),
-    "jd": ("sbuf", [128, 128], "bfloat16"),
-    "rm": ("sbuf", [128, 16 * NM], "bfloat16"), "ones": ("sbuf", [128, 16 * NM], "bfloat16"), "zr": ("sbuf", [128, NS * NM], "bfloat16"),
+    "selh": ("sbuf", [128, 144], "bfloat16"), "selq": ("sbuf", [128, 144], "bfloat16"),
+    "jrow": ("sbuf", [128, 144], "bfloat16"), "grow": ("sbuf", [128, 128], "bfloat16"),
+    "jd": ("sbuf", [128, 128], "bfloat16"), "cio": ("sbuf", [128, P], "bfloat16"),
+    "rm": ("sbuf", [128, 16 * NM], "bfloat16"), "rm0": ("sbuf", [128, 16 * NM], "bfloat16"),
+    "ones": ("sbuf", [128, 16 * NM], "bfloat16"), "zr": ("sbuf", [128, NS * NM], "bfloat16"),
     "tiles": ("sbuf", [128, NM * len(TILES)], "bfloat16"), "dl": ("sbuf", [128, NM], "float32"),
-    "cols": ("sbuf", [128, 32], "float32"), "icol": ("sbuf", [128, 8], "int32"),
+    "cols": ("sbuf", [128, 32], "float32"), "icol": ("sbuf", [128, 8], "int32"), "hb": ("sbuf", [128, 8], "bfloat16"),
     "dws": ("sbuf", [128, 4], "int32"), "hws": ("sbuf", [128, 4], "int32"), "ths": ("sbuf", [128, 4], "int32"),
-    "off": ("sbuf", [128, W], "uint16"), "so": ("sbuf", [128, 32 * NC], "uint16"),
-    "t12": ("sbuf", [128, 2 * W], "bfloat16"),
+    "off": ("sbuf", [128, W], "uint16"), "so": ("sbuf", [128, 32 * NC], "uint16"), "ci": ("sbuf", [128, 16 * NC], "int32"),
+    "f3": ("sbuf", [128, 3 * W], "bfloat16"), "kq": ("sbuf", [128, 3 * W], "bfloat16"),
 }
 for _n in NB16:
     SCRATCH[_n] = ("sbuf", [128, W], "bfloat16")
@@ -55,23 +61,21 @@ for _c in range(NC):
 for _s in range(ST):
     SCRATCH["ox%d" % _s] = ("sbuf", [128, 3 * W], "bfloat16")
     SCRATCH["ot%d" % _s] = ("sbuf", [128, W], "float32")
+    SCRATCH["lx%d" % _s] = ("sbuf", [128, 3 * W], "bfloat16")
     if _s:
-        SCRATCH["lx%d" % _s] = ("sbuf", [128, 3 * W], "bfloat16")
         SCRATCH["lt%d" % _s] = ("sbuf", [128, W], "float32")
 for _b in range(8):
     SCRATCH["pb%d" % _b] = ("psum", [128, 512], "float32")
 
-LOADS = ["fa", "fb", "t0", "x0", "y0", "k0", "dw", "hw", "th"]
+LOADS = ["f%d" % _i for _i in range(NLOAD)] + ["fb", "t0", "x0", "y0", "k0", "dw", "hw", "th"]
 SEMAPHORES = ["pe", "dve", "act", "pool", "sent"] + ["l" + s for s in LOADS] + ["oyy", "oyk"]
 for _c in range(NC):
     SEMAPHORES += ["oyx%d" % _c, "oyt%d" % _c]
     for _s in range(1, ST):
         SEMAPHORES += ["ax%d_%d" % (_s, _c), "at%d_%d" % (_s, _c)]
 
-CYC = 1.0
-PCYC = 0.5
-FIXV, FIXA, GATH, SCAT, TT2 = 55.0, 65.0, 1.55, 3.8, 2.0
-LAT_X, LAT_S, LAT_NET = 120.0, 80.0, 3000.0
+PAR = {"CYC": 0.83, "PCYC": 0.45, "FIXV": 60.0, "FIXA": 75.0, "FIXP": 5.0, "GATH": 1.56, "SCAT": 3.8,
+       "LAT_X": 180.0, "LAT_S": 120.0, "LAT_B": 180.0, "LAT_NET": 3000.0, "SEND": 500.0}
 
 
 def V(name, c0=0, c1=None, step=1, p0=0, p1=128):
@@ -110,10 +114,11 @@ def ap(T, v):
 
 def plan():
     ops = []
-    wr, rd, bank = {}, {}, {}
+    wr, rd, pe_in, shut = {}, {}, {}, {}
     cur = [0.0]
+    CYC, PCYC = PAR["CYC"], PAR["PCYC"]
 
-    def add(eng, cost, fn, reads, writes, lat=0.0, sem=None):
+    def add(eng, cost, fns, reads, writes, lat=0.0, sem=None):
         i = len(ops)
         deps = {}
 
@@ -130,41 +135,32 @@ def plan():
                 rs.append(v[2])
             else:
                 ws.append(v)
-        for v in rs + ws:
-            if in_psum(v):
-                for j in bank.setdefault(v[0], {}).values():
-                    dep(j, False)
         for v in rs:
             for (j, a, b) in wr.get(v[0], []):
                 if a < v[4] and v[3] < b:
                     dep(j, True)
         for v in ws:
-            if not in_psum(v):
-                for (j, a, b) in wr.get(v[0], []) + rd.get(v[0], []):
-                    if a < v[4] and v[3] < b:
-                        dep(j, True)
-        for v in rs + ws:
-            if in_psum(v):
-                bank[v[0]][eng] = i
+            for (j, a, b) in wr.get(v[0], []) + rd.get(v[0], []):
+                if a < v[4] and v[3] < b:
+                    dep(j, not in_psum(v))
         for v in ws:
             full = v[1] == 0 and v[2] == 128 and v[5] == 1
             wr[v[0]] = [e for e in wr.get(v[0], []) if not (full and v[3] <= e[1] and e[2] <= v[4])] + [(i, v[3], v[4])]
             if full:
                 rd[v[0]] = [e for e in rd.get(v[0], []) if not (v[3] <= e[1] and e[2] <= v[4])]
         for v in rs:
-            if not in_psum(v):
-                rd.setdefault(v[0], []).append((i, v[3], v[4]))
+            rd.setdefault(v[0], []).append((i, v[3], v[4]))
         deps.pop(i, None)
-        ops.append({"eng": eng, "cost": cost, "fn": fn, "deps": deps, "lat": lat, "sem": sem, "lag": cur[0],
-                    "tag": (ws[0][0] if ws else "out")})
+        ops.append({"eng": eng, "cost": cost, "fns": fns, "deps": deps, "lat": lat, "sem": sem, "lag": cur[0],
+                    "banks": sorted(set(v[0] for v in rs + ws if in_psum(v))), "tag": (ws[0][0] + str(ws[0][3]) if ws else "out")})
         return i
 
     def ecost(eng, out, ins, per):
         if out[0] == "#":
-            per = SCAT
+            per = PAR["SCAT"]
         elif ins[0][0] == "#":
-            per = max(per, GATH)
-        return (FIXV if eng == "dve" else FIXA) + max(16, width(out) * per) * CYC
+            per = max(per, PAR["GATH"])
+        return PAR["FIXV" if eng == "dve" else "FIXA"] + max(16, width(out) * per) * CYC
 
     def ts(out, in0, s1, op0, s2=None, op1=None):
         per = 0.5 if two_bytes(out) and two_bytes(in0) else 1.0
@@ -172,58 +168,77 @@ def plan():
             fn = lambda g, T, x: g.vector.tensor_scalar(ap(T, out), ap(T, in0), ap(T, s1), None, op0)
         else:
             fn = lambda g, T, x: g.vector.tensor_scalar(ap(T, out), ap(T, in0), ap(T, s1), ap(T, s2), op0, op1)
-        add("dve", ecost("dve", out, [in0], per), fn, [in0, s1, s2], [out])
+        add("dve", ecost("dve", out, [in0], per), [fn], [in0, s1, s2], [out])
 
     def tt(out, in0, in1, op):
-        per = 1.0 if in_psum(in0) or in_psum(in1) else TT2
-        add("dve", ecost("dve", out, [in0], per), lambda g, T, x: g.vector.tensor_tensor(ap(T, out), ap(T, in0), ap(T, in1), op), [in0, in1], [out])
+        per = 1.0 if in_psum(in0) or in_psum(in1) else 2.0
+        add("dve", ecost("dve", out, [in0], per), [lambda g, T, x: g.vector.tensor_tensor(ap(T, out), ap(T, in0), ap(T, in1), op)], [in0, in1], [out])
 
     def cp(out, in0):
         per = 0.5 if two_bytes(out) and two_bytes(in0) else 1.0
-        add("dve", ecost("dve", out, [in0], per), lambda g, T, x: g.vector.tensor_copy(ap(T, out), ap(T, in0)), [in0], [out])
+        add("dve", ecost("dve", out, [in0], per), [lambda g, T, x: g.vector.tensor_copy(ap(T, out), ap(T, in0))], [in0], [out])
 
     def ms(out, val):
-        add("dve", ecost("dve", out, [out], 0.5 if two_bytes(out) else 1.0), lambda g, T, x: g.vector.memset(ap(T, out), val), [], [out])
+        add("dve", ecost("dve", out, [out], 0.5 if two_bytes(out) else 1.0), [lambda g, T, x: g.vector.memset(ap(T, out), val)], [], [out])
 
     def scan(out, d0, d1, op0=OP.add):
         add("dve", ecost("dve", out, [d1], 1.0),
-            lambda g, T, x: g.vector.tensor_tensor_scan(ap(T, out), ap(T, d0), ap(T, d1), 0.0, op0, OP.min), [d0, d1], [out])
+            [lambda g, T, x: g.vector.tensor_tensor_scan(ap(T, out), ap(T, d0), ap(T, d1), 0.0, op0, OP.min)], [d0, d1], [out])
 
     def act(out, in0, func, bias=0.0, scale=1.0):
         if func == AF.Copy:
             fn = lambda g, T, x: g.scalar.activation(ap(T, out), ap(T, in0), func)
         else:
             fn = lambda g, T, x: g.scalar.activation(ap(T, out), ap(T, in0), func, bias=ap(T, bias), scale=ap(T, scale))
-        add("act", ecost("act", out, [in0], 1.0), fn, [in0, bias, scale], [out])
+        return add("act", ecost("act", out, [in0], 1.0), [fn], [in0, bias, scale], [out])
 
-    def mm(out, lhs, rhs, start, stop):
-        c = max(64, width(rhs)) * PCYC * (1 if two_bytes(rhs) else 4)
-        add("pe", c, lambda g, T, x: g.tensor.matmul(ap(T, out), ap(T, lhs), ap(T, rhs), start, stop), [lhs, rhs], [out], lat=60.0)
+    def mms(items, opens=False, closes=False):
+        fns, c = [], 0.0
+        for (out, lhs, rhs, a, b) in items:
+            c += PAR["FIXP"] + max(min(64, width(lhs)), width(rhs)) * PCYC * (1 if two_bytes(rhs) else 4)
+            fns.append(lambda g, T, x, out=out, lhs=lhs, rhs=rhs, a=a, b=b: g.tensor.matmul(ap(T, out), ap(T, lhs), ap(T, rhs), a, b))
+        i = add("pe", c, fns, [v for it in items for v in it[1:3]], [it[0] for it in items], lat=60.0)
+        bk = items[0][0][0]
+        if opens:
+            for j in pe_in.get(bk, []):
+                ops[i]["deps"].setdefault(j, False)
+        if bk in shut:
+            ops[i]["deps"].setdefault(shut[bk], False)
+        if closes:
+            shut[bk] = i
+            pe_in[bk] = []
+        pe_in.setdefault(bk, []).append(i)
+        return i
 
-    def group(out, terms):
-        for i, (lhs, rhs) in enumerate(terms):
-            mm(out, lhs, rhs, i == 0, i == len(terms) - 1)
+    def terms(out, ts_):
+        return [(out, lhs, rhs, i == 0, i == len(ts_) - 1) for i, (lhs, rhs) in enumerate(ts_)]
+
+    def group(out, ts_):
+        mms(terms(out, ts_))
 
     def iota(out, pattern, base, ch):
         if SCRATCH[out[0]][2] == "int32":
             fn = lambda g, T, x: g.iota(ap(T, out), pattern, base, ch)
         else:
             fn = lambda g, T, x: g.iota(ap(T, out), pattern, base, ch, allow_small_or_imprecise_dtypes=True)
-        add("pool", 130 + 2 * width(out) * CYC, fn, [], [out])
+        add("pool", 130 + 2 * width(out) * CYC, [fn], [], [out])
 
     def sel(out, in0, pattern, cmp, fill, base, ch):
-        add("pool", 170 + 2 * width(out) * CYC, lambda g, T, x: g.affine_select(ap(T, out), ap(T, in0), pattern, cmp, fill, base, ch), [in0], [out])
+        add("pool", 170 + 2 * width(out) * CYC, [lambda g, T, x: g.affine_select(ap(T, out), ap(T, in0), pattern, cmp, fill, base, ch)], [in0], [out])
 
-    def load(q, out, src, sem, lat):
-        add(q, 60.0, lambda g, T, x: (g.sync if q == "sp" else g.scalar).dma_start(ap(T, out), T[src][:]), [], [out], lat=lat, sem=sem)
+    def queue(g, q):
+        return g.sync if q == "sp" else g.scalar
+
+    def load(q, out, src, sem, lat, c0=None, c1=None):
+        return add(q, 60.0, [lambda g, T, x: queue(g, q).dma_start(ap(T, out), T[src][:] if c0 is None else T[src][:, c0:c1])], [], [out], lat=lat, sem=sem)
 
     def store(q, dst, c0, c1, src, sem):
-        add(q, 60.0, lambda g, T, x: (g.sync if q == "sp" else g.scalar).dma_start(T[dst][:, c0:c1], ap(T, src)), [src], [], lat=2000.0, sem=sem)
+        add(q, 60.0, [lambda g, T, x: queue(g, q).dma_start(T[dst][:, c0:c1], ap(T, src))], [src], [], lat=2000.0, sem=sem)
 
     def send(src, dst, sem):
-        i = add("pool", 600.0, lambda g, T, x: g.remote_dma(ap(T, dst), ap(T, src), T.sem[sem], T.sem.sent, x["pid"], x["rid"], x["mask"]), [src], [])
+        i = add("pool", PAR["SEND"], [lambda g, T, x: g.remote_dma(ap(T, dst), ap(T, src), T.sem[sem], T.sem.sent, x["pid"], x["rid"], x["mask"])], [src], [])
         ops[i]["send"] = True
-        j = add("net", 0.0, None, [], [dst], lat=LAT_NET, sem=sem)
+        j = add("net", 0.0, [], [], [dst], lat=PAR["LAT_NET"], sem=sem)
         ops[j]["deps"][i] = False
 
     def mat(n):
@@ -236,59 +251,74 @@ def plan():
         return V("cols", i, i + 1)
 
     cur[0] = -1e6
-    load("sp", V("ft", 0, M), "fx", "lfa", 6000.0)
-    load("act", V("t0s"), "t0", "lt0", 2000.0)
-    load("act", V("x0s"), "x0", "lx0", 2000.0)
+    for i in range(NLOAD):
+        a, b = M * i // NLOAD, M * (i + 1) // NLOAD
+        j = load("sp", V("fr", a, b), "fx", "lf%d" % i, 2500.0 + 3500.0 * (i + 1) / NLOAD, a, b)
+        if i:
+            ops[j]["deps"][j - 1] = None
+    last = len(ops) - 1
+    load("act", V("t0s"), "t0", "lt0", 2500.0)
+    load("act", V("x0s"), "x0", "lx0", 2500.0)
     cur[0] = 0.0
     load("act", V("hws", 0, 1), "hw", "lhw", 2500.0)
     load("act", V("dws"), "dw", "ldw", 2500.0)
     load("act", V("ths", 0, 1), "th", "lth", 2500.0)
-    load("sp", V("k0s"), "k0", "lk0", 3000.0)
-    ops[-1]["deps"][0] = True
-    load("sp", V("ys", 0, P), "y0", "ly0", 3500.0)
-    ops[-1]["deps"][len(ops) - 2] = False
-    load("sp", V("ft", M, 2 * M), "fx", "lfb", 8000.0)
-    ops[-1]["deps"][len(ops) - 2] = False
+    j = load("sp", V("k0s"), "k0", "lk0", 3000.0)
+    ops[j]["deps"][last] = True
+    j = load("sp", V("ys", 0, P), "y0", "ly0", 3500.0)
+    ops[j]["deps"][j - 1] = None
 
-    KC, G16, SC, SC256, K37, G15, KQ, HF, H4C, H2C, THC, TA_, TB_, KR, DF = 0, 1, 2, 3, 4, 5, 6, 7, 8, 9, 10, 11, 12, 13, 16
+    KC, G16, SC, SCK, CU, RB, PK, G15, KQ, HF, H1, H2C, H3, THC, TA_, TB_, KH, NKH, KL, DF = list(range(19)) + [20]
     iota(V("jd"), [[1, 128]], 0, -1)
     iota(V("icol", 0, 1), [[0, 1]], 0, 1)
     iota(V("grow"), [[16, 8], [0, 16]], 0, 0)
     iota(V("jrow"), [[1, 144]], 0, 0)
     ms(V("ones"), 1.0)
-    sel(V("rm"), V("ones"), [[1, NM], [0, 16]], OP.is_equal, 0.0, 0, -1)
-    ts(mat("I"), V("jd"), 0.0, OP.is_equal)
-    for n, c in (("nI", -1.0), ("I16", 16.0), ("nI16", -16.0), ("I2", 2.0), ("I17", 17.0), ("Is", 1 / 16), ("IB", BIG), ("I16B", 16 * BIG),
-                 ("I32B", 32 * BIG), ("nI32B", -32 * BIG), ("nI128", -32 * BIG / M), ("nI2k", -2048.0), ("nIm", -2.0 / M)):
+    sel(V("rm0"), V("ones"), [[1, NM], [0, 16]], OP.is_equal, 0.0, 0, -1)
+    sel(V("rm", p0=64, p1=128), V("rm0", p0=64, p1=128), [[0, 16 * NM]], OP.not_equal, 1.0, 64 - NM, 1)
+    cp(V("rm", p0=0, p1=64), V("rm0", p0=0, p1=64))
+    for n, c in DIAG.items():
         ts(mat(n), V("jd"), 0.0, OP.is_equal, c, OP.mult)
     ts(V("i32s"), V("jd"), 0.0, OP.is_equal)
     ts(V("icol", 1, 2), V("icol", 0, 1), 15, OP.bitwise_and)
     ts(V("icol", 2, 3), V("icol", 0, 1), 112, OP.bitwise_and)
     cp(V("cols", KC, G16 + 1), V("icol", 1, 3))
     ts(col(SC), col(KC), -STEP, OP.mult, 15 * STEP, OP.add)
-    ts(col(SC256), col(KC), -STEP, OP.mult, 15 * STEP + 256, OP.add)
-    ts(col(K37), col(KC), 37.0, OP.mult)
+    ts(col(SCK), col(KC), -STEP, OP.mult, 15 * STEP + 60 + 2048 - 16384, OP.add)
+    ts(col(PK), col(KC), 37.0 * 32, OP.mult, 33.0 * M - 2.0 ** 23, OP.add)
     ts(col(G15), col(G16), 15.0, OP.add)
-    ts(col(KQ), col(KC), -0.5, OP.mult, -32.0, OP.add)
-    ts(col(KR), col(KC), 0.5, OP.mult, -7.0, OP.add)
-    ts(V("selh"), V("jrow"), col(G15), OP.is_equal, BIG / 2, OP.mult)
-    ts(col(H4C), V("hws", 0, 1), 4.0, OP.mult)
-    ts(col(H2C), V("hws", 0, 1), -2.0, OP.mult)
-    for n, c in (("OH", -0.5), ("OB", BIG), ("O2k", -2048.0), ("KW", col(KC)), ("H4", col(H4C)), ("H2n", col(H2C))):
+    ts(col(KQ), col(KC), -0.5, OP.mult, -3.5, OP.add)
+    ts(col(KL), col(KC), 1.5, OP.mult, -34.5, OP.add)
+    ts(col(KH), col(KC), 0.5, OP.mult)
+    ts(col(NKH), col(KC), -0.5, OP.mult)
+    ts(V("selh"), V("jrow"), col(G15), OP.is_equal, -BIG, OP.mult)
+    act_a = "act" in A_ENG
+    if act_a:
+        ts(V("selq"), V("jrow"), col(G15), OP.is_equal, -BIG / 2, OP.mult)
+    ts(col(H1), V("hws", 0, 1), 0.25, OP.mult)
+    ts(col(H2C), V("hws", 0, 1), -0.125, OP.mult)
+    ts(col(H3), V("hws", 0, 1), 2.0, OP.mult)
+    for n, c in (("OH", -0.5), ("On2", -2.0), ("OB", BIG), ("nOB", -BIG), ("O2B", 2 * BIG), ("O1k", 1024.0), ("nO1k", -1024.0),
+                 ("KW", col(KH)), ("nKW", col(NKH)), ("Hp", col(H1)), ("Hn", col(H2C)), ("H2", col(H3))):
         ts(mat(n), V("grow"), col(G16), OP.is_equal, c, OP.mult)
     sel(mat("TRS"), mat("OH"), [[1, 128]], OP.is_gt, 0.0, 0, -1)
-    sel(mat("TRI"), mat("TRS"), [[1, 128]], OP.not_equal, 32.0, 0, -1)
-    sel(mat("TRV"), mat("OH"), [[-1, 128]], OP.is_gt, 0.0, 0, 1)
-    sel(mat("TRU"), mat("TRV"), [[1, 128]], OP.not_equal, 0.5, 0, -1)
+    sel(mat("TRI"), mat("TRS"), [[1, 128]], OP.not_equal, 4.0, 0, -1)
+    sel(mat("TRV"), mat("On2"), [[-1, 128]], OP.is_gt, 0.0, 0, 1)
+    tt(mat("TRL"), mat("TRI"), mat("TRV"), OP.add)
     iota(tile("turn"), [[0, NM // 4], [1, 4]], 0, 0)
-    iota(tile("w16"), [[16, NM]], 2048, 0)
+    iota(tile("w16"), [[16, NM]], 0, 0)
     iota(tile("rr"), [[0, NS], [1, 16]], 0, 0)
-    ts(tile("kq"), tile("turn"), col(KQ), OP.add)
+    iota(V("cio"), [[1, P]], -256, 0)
+    for c in range(NC):
+        n, o = CH[c], 3 * C0[c]
+        ts(V("kq", o, o + n), tile("turn", n), col(KQ), OP.add)
+        ts(V("kq", o + n, o + 2 * n), tile("turn", n), col(KQ), OP.add, -1.0, OP.add)
+        ts(V("kq", o + 2 * n, o + 3 * n), tile("turn", n), col(KL), OP.add)
     ts(tile("mk"), tile("rr"), col(KC), OP.not_equal)
     ts(tile("da"), tile("rr"), col(KC), OP.is_equal, 64 * STEP, OP.mult)
     ts(tile("db"), tile("rr"), col(KC), OP.is_gt, -STEP, OP.mult)
     tt(tile("d0"), tile("da"), tile("db"), OP.add)
-    ts(V("cols", DF, DF + 4), V("dws"), -8.5, OP.add)
+    ts(V("cols", DF, DF + 4), V("dws"), -48.5, OP.add)
     for s in range(ST):
         ts(tile("dt%d" % s), V("ones", 0, NM), col(DF + s), OP.mult)
     ts(col(HF), V("ths", 0, 1), -1.0, OP.mult)
@@ -296,11 +326,14 @@ def plan():
     ts(col(TB_), col(KC), 1.0, OP.is_equal, -0.5, OP.mult)
     tt(col(THC), col(TA_), col(TB_), OP.add)
     ts(tile("tht"), V("ones", 0, NM), col(THC), OP.mult)
-    dve_a = "dve" in A_ENG
-    if dve_a:
+    ms(V("hb"), XO)
+    group(V("pb1", 0, 2), [(mat("Hn"), V("hb", 0, 2))])
+    ts(col(CU), V("pb1", 0, 1), col(SC), OP.add)
+    ts(col(RB), V("pb1", 0, 1), VB - 2047.0, OP.add)
+    if act_a:
         for i, e in enumerate(A_ENG):
             if 32 * i < NM:
-                ms(V("tiles", tile("cm8")[3] + 32 * i, tile("cm8")[3] + min(NM, 32 * i + 32)), -8.0 if e == "dve" else 0.0)
+                ms(V("tiles", tile("cm8")[3] + 32 * i, tile("cm8")[3] + min(NM, 32 * i + 32)), -8.0 if e == "act" else 0.0)
     iota(V("dl"), [[1, NM]], 256, 0)
     ts(tile("dc"), tile("mk"), -4096.0, OP.mult)
     tt(V("dl"), V("dl"), tile("dc"), OP.add)
@@ -310,21 +343,31 @@ def plan():
     ms(V("ks", P, P + NM), 0.0)
     cp(V("ks", 0, P), V("k0s"))
     for c in range(NC):
+        ms(V("xt%d" % c), -XO)
         ms(V("ct%d" % c, p0=0, p1=32), 0.0)
         for h in range(0, 128, NM):
             e = min(128, h + NM)
             ts(V("ct%d" % c, h, e, p0=32, p1=64), V("tiles", tile("rr")[3], tile("rr")[3] + e - h, p0=32, p1=64),
                V("cols", KC, KC + 1, p0=32, p1=64), OP.is_equal, 1024.0, OP.mult)
-        ms(V("e16_%d" % c, 16 * CH[c], 16 * CH[c] + 16), 2064.0)
+        ms(V("e16_%d" % c, 16 * CH[c], 16 * CH[c] + 16), XO - LOW)
+    j = act(V("lx0", 0, CH[0]), V("x0s", 0, CH[0]), AF.Gelu, XO, 16.0)
+    ops[j]["cost"] += 1300.0
 
     nbk = 8 // NC
+    for i in range(NFIX):
+        a, b = M * i // NFIX, M * (i + 1) // NFIX
+        z = V("pb%d" % ((i % NC) * nbk + 2 + (i // NC) % 2), 0, b - a)
+        ts(V("fq", a, b), V("fr", a, b), 16.0, OP.is_lt, -LOW, OP.mult)
+        group(z, [(mat("I"), V("fr", a, b)), (mat("I"), V("fq", a, b))])
+        act(V("ft", a, b), z, AF.Copy)
+    add("sp", 60.0, [lambda g, T, x: g.sync.dma_start(T.ft[:, M:2 * M], T.ft[:, 0:M])], [V("ft", 0, M)], [V("ft", M, 2 * M)], lat=8000.0, sem="lfb")
 
     def walk(s, c):
         n, c0 = CH[c], C0[c]
         ns = n // 16
         cur[0] = LAG * c
-        al, be = "pb%d" % (c * nbk), "pb%d" % (c * nbk + 1)
-        wide = ["pb%d" % (c * nbk + 2 + i) for i in range(nbk - 2)]
+        al, be, w0, w1 = ["pb%d" % (c * nbk + i) for i in range(4)]
+        wide = [w0, w1]
 
         def N(name):
             return V(name, c0, c0 + n)
@@ -335,161 +378,179 @@ def plan():
         def t(name):
             return tile(name, n)
 
+        def R(bk, i, k=1):
+            return V(bk, i * n, (i + k) * n)
+
         fw, e16, wa, wq = "fw%d" % c, "e16_%d" % c, "wa%d" % c, "wq%d" % c
-        xo, ho, sw = [V("ox%d" % s, 3 * c0 + i * n, 3 * c0 + (i + 1) * n) for i in range(3)]
+        xo, zo, ho = [V("ox%d" % s, 3 * c0 + i * n, 3 * c0 + (i + 1) * n) for i in range(3)]
+        x, xz, hit0 = [V("lx%d" % s, 3 * c0 + i * n, 3 * c0 + (i + 1) * n) for i in range(3)]
         to = V("ot%d" % s, c0, c0 + n)
-        pn, pk = V(be, 512 - n, 512), (V(be, 512 - 2 * n, 512 - n) if 8 * ns * (ns + 1) + 2 * n <= 512 else N("nk"))
+        one = V("ones", 0, n)
+        sa, pn, pk = N("sa"), R(be, 0), R(be, 1)
         if s == 0:
-            x, hit0, sa, tin = N("x0s"), None, N("sa0"), N("t0f")
+            tin = N("t0f")
             ts(N("w1"), N("t0s"), M - 1, OP.bitwise_and)
             cp(N("off"), N("w1"))
-            cp(tin, N("t0s"))
-            act(sa, tin, AF.Sign, -4095.5)
+            ts(tin, N("t0s"), -float(M), OP.add)
+            if c:
+                act(x, N("x0s"), AF.Identity, XO, 16.0)
+            act(xz, N("x0s"), AF.Relu, 8192.0, -8192.0)
             win = V("ft", 0, M)
         else:
-            x, hit0, sa = [V("lx%d" % s, 3 * c0 + i * n, 3 * c0 + (i + 1) * n) for i in range(3)]
             tin = V("lt%d" % s, c0, c0 + n)
-            cp(N("off"), tin)
+            ts(N("off"), tin, float(M), OP.add)
             win = V("ft")
-        group(V(be, 0, 128, p1=n), [(x, mat("I"))])
-        act(V("xt%d" % c, p1=n), V(be, 0, 128, p1=n), AF.Copy)
-        act(N("xz"), x, AF.Relu, 256.0, -256.0)
-        group(pn, [(V("i32s"), tin), (mat("nI2k"), sa), (mat("nI2k"), V("ones", 0, n))])
-        act(N("n"), pn, AF.Copy)
-        act(pk, pn, AF.Identity, col(K37))
-        act(N("tM"), pn, AF.Identity, float(M))
+        act(sa, tin, AF.Sign, 0.5)
+        xq = V(be, 2 * n, 2 * n + 128, p1=n)
+        group(xq, [(x, mat("I"))])
+        act(V("xt%d" % c, p1=n), xq, AF.Identity, -XO / 16, 1 / 16)
+        group(pn, [(V("i32s"), tin), (mat("nI2k"), sa), (mat("nI2k"), one)])
+        act(N("n"), pn, AF.Identity, float(M))
+        act(pk, pn, AF.Identity, col(PK), 33.0)
+        sums = []
         for i, a in enumerate(range(0, n, 32)):
             b = min(n, a + 32)
             src = IND(win, V("off", c0 + a, c0 + b))
+            fp, ep, wp = V(fw, 16 * a, 16 * b), V(e16, 16 * a, 16 * b), V(wa, 16 * a, 16 * b)
             if G_ENG[i] == "act":
-                act(V(fw, 16 * a, 16 * b), src, AF.Copy)
+                act(fp, src, AF.Copy)
             else:
-                cp(V(fw, 16 * a, 16 * b), src)
-            if E_ENG[i] == "act":
-                act(V(e16, 16 * a, 16 * b), V(fw, 16 * a, 16 * b), AF.Identity, 2056.5)
-            else:
-                ts(V(e16, 16 * a, 16 * b), V(fw, 16 * a, 16 * b), 2056.5, OP.add)
-            z = V(wide[i % len(wide)], 0, 16 * (b - a))
-            group(z, [(V("xt%d" % c, p1=n), V("rm", 16 * a, 16 * b, p1=n)), (mat("nI"), V(fw, 16 * a, 16 * b)), (mat("I"), V(e16, 16 * a, 16 * b))])
+                cp(fp, src)
+            ts(ep, fp, XO - 7.5, OP.add)
+            z = V(wide[i % 2], 0, 16 * (b - a))
+            tm = [(V("xt%d" % c, p1=NM + 1), V("rm", 16 * a, 16 * b, p1=NM + 1)), (mat("I"), ep)]
             if A_ENG[i] == "act":
-                act(V(wa, 16 * a, 16 * b), z, AF.Sign, 2063.5, -1.0)
+                group(z, tm + [(mat("nI"), fp)])
+                act(wp, z, AF.Sign, 0.5)
             else:
-                ts(V(wa, 16 * a, 16 * b), z, 2064.0, OP.is_lt, 2.0, OP.mult)
-        terms = [(mat("I16B"), sa)]
-        if hit0:
-            terms.append((mat("IB"), hit0))
-        if dve_a:
-            terms.append((mat("IB"), t("cm8")))
-        group(V(al, 0, n), terms + [(V("selh", 15 - k, 143 - k), V(wa, k, 16 * n, 16)) for k in range(16)])
-        act(N("cand"), V(al, 0, n), AF.Sign, -16.5 * BIG, -1.0)
-        group(V(al, 0, n), [(mat("I"), t("kq")), (mat("TRI"), N("cand"))])
-        act(N("fst"), V(al, 0, n), AF.Sign, 0.5)
-        group(V(al, 0, n), [(mat("TRU"), N("fst"))])
-        if GO_ENG == "act":
-            act(N("go"), V(al, 0, n), AF.Relu, col(KR))
-        else:
-            ts(N("go"), V(al, 0, n), col(KR), OP.add, 0.0, OP.max)
-        group(V(be, 0, n), [(mat("I"), t("w16")), (mat("KW"), N("go")), (mat("O2k"), N("go"))])
-        scan(N("sv1"), t("d0"), V(be, 0, n))
+                group(z, tm)
+                tt(wp, z, fp, OP.is_ge)
+        tm = [(mat("I16B"), sa)]
+        if s:
+            tm.append((mat("IB"), hit0))
+        if act_a:
+            tm.append((mat("IB"), t("cm8")))
+        it = [(R(al, 0), l_, r_, i == 0, False) for i, (l_, r_) in enumerate(tm)]
+        runs = []
+        for i, a in enumerate(range(0, n, 32)):
+            if runs and runs[-1][2] == A_ENG[i]:
+                runs[-1][1] = min(n, a + 32)
+            else:
+                runs.append([a, min(n, a + 32), A_ENG[i]])
+        for a, b, e in runs:
+            it += [(V(al, a, b), V("selq" if e == "act" else "selh", 15 - k, 143 - k), V(wa, 16 * a + k, 16 * b, 16), False, False) for k in range(16)]
+        it[-1] = it[-1][:4] + (True,)
+        mms(it)
+        act(N("cand"), R(al, 0), AF.Sign, -24.5 * BIG, -1.0)
+        f3 = [V("f3", 3 * c0 + i * n, 3 * c0 + (i + 1) * n) for i in range(3)]
+        mms([(R(al, 1, 3), mat("I"), V("kq", 3 * c0, 3 * c0 + 3 * n), True, False), (R(al, 1), mat("TRI"), N("cand"), False, False),
+             (R(al, 2), mat("TRI"), N("cand"), False, False), (R(al, 3), mat("TRL"), N("cand"), False, True)])
+        act(V("f3", 3 * c0, 3 * c0 + 3 * n), R(al, 1, 3), AF.Sign)
+        group(R(al, 0), [(mat("I"), t("w16")), (mat("KW"), f3[0]), (mat("nO1k"), f3[0]), (mat("nKW"), f3[1]), (mat("O1k"), f3[1]),
+                         (mat("KW"), f3[2]), (mat("nO1k"), f3[2])])
+        scan(N("sv1"), t("d0"), R(al, 0))
         ko, co, lo = V("so", 32 * c, 32 * c + ns), V("so", 32 * c + 8, 32 * c + 8 + ns), V("so", 32 * c + 16, 32 * c + 16 + ns)
-        ts(ko, S("sv1"), col(SC), OP.add, float(16 * n), OP.min)
-        if B_ENG == "act":
-            act(N("b"), IND(V(e16), ko), AF.Identity, -129.0, 1 / 16)
+        ts(ko, S("sv1"), col(SCK), OP.add, float(16 * n), OP.min)
+        tt(N("mx"), IND(V(e16), ko), x, OP.max)
+        act(N("e"), IND(V(e16), ko), AF.Relu, -XO)
+        act(N("bz"), IND(V(e16), ko), AF.Relu, 32 * (XO + 16), -32.0)
+        pu, pp, px = R(al, 2), R(al, 1), R(w1, 0)
+        group(pu, [(mat("Hn"), x), (mat("Hp"), N("mx")), (mat("Hn"), N("e"))])
+        group(pp, [(mat("I240"), one), (mat("I17"), x), (mat("I"), xz), (mat("nI16"), N("mx")), (mat("I"), N("bz"))])
+        group(px, [(mat("nI"), x), (mat("I2"), N("mx")), (mat("nI"), N("e"))])
+        tt(N("tq"), pp, N("mx"), OP.max)
+        act(N("xp"), px, AF.Identity, -XO / 16, 1 / 16)
+        if s < ST - 1:
+            act(xo, px, AF.Copy)
+            act(zo, px, AF.Relu, 8192.0 + 512 * XO, -512.0)
         else:
-            ts(N("b"), IND(V(e16), ko), 1 / 16, OP.mult, -129.0, OP.add)
-        act(N("bz"), IND(V(e16), ko), AF.Relu, 33280.0, -16.0)
-        tt(N("mx"), N("b"), x, OP.max)
-        group(V(be, 0, n), [(mat("H2n"), x), (mat("H2n"), N("b")), (mat("H4"), N("mx"))])
-        group(V(al, 0, n), [(mat("I17"), x), (mat("I"), N("xz")), (mat("I"), N("bz")), (mat("nI16"), N("mx"))])
-        group(V(al, n, 2 * n), [(mat("Is"), N("xz")), (mat("Is"), N("bz")), (mat("I"), N("mx"))])
-        group(V(al, 2 * n, 3 * n), [(mat("nI"), x), (mat("nI"), N("b")), (mat("I2"), N("mx"))])
-        t1_, t2_ = V("t12", 2 * c0, 2 * c0 + n), V("t12", 2 * c0 + n, 2 * c0 + 2 * n)
-        act(V("t12", 2 * c0, 2 * c0 + 2 * n), V(al, 0, 2 * n), AF.Relu, -1.0)
-        act(xo, V(al, 2 * n, 3 * n), AF.Copy)
-        ts(N("c1"), V(be, 0, n), 120.5, OP.mult)
-        ts(N("w1"), V(be, 0, n), 1.0, OP.add)
-        ts(N("c2"), N("c1"), 6, OP.logical_shift_right, P - 1, OP.bitwise_and)
-        ts(N("c3"), N("c2"), -256.0, OP.add)
-        scan(N("sv2"), t("d0"), N("c3"))
-        ts(co, S("sv2"), col(SC256), OP.add)
-        tt(N("dy"), IND(V("ys", 0, P), co), xo, OP.subtract)
-        act(N("kc"), IND(V("ks", 0, P), co), AF.Copy)
-        act(N("ady"), N("dy"), AF.Abs)
-        ts(N("v2"), N("w1"), M - 1, OP.bitwise_and)
-        tt(N("prod"), pn, N("v2"), OP.mult)
-        ts(N("sh"), N("prod"), 5, OP.logical_shift_right)
-        tt(N("sm2"), pk, N("sh"), OP.add)
-        ts(N("new"), N("sm2"), M - 1, OP.bitwise_and)
-        group(V(be, 0, n), [(mat("OB"), t("tht")), (mat("OB"), N("ady"))])
-        tt(N("kp"), V(be, 0, n), N("kc"), OP.max)
-        ts(ho, V(be, 0, n), 0.0, OP.is_lt)
-        if s == ST - 1:
-            store("act", "yx", c0, c0 + n, xo, "oyx%d" % c)
-        ts(N("mM"), N("kp"), float(M), OP.is_lt, float(M), OP.mult)
+            store("act", "yx", c0, c0 + n, N("xp"), "oyx%d" % c)
+        scan(N("sv2"), t("d0"), pu)
+        c1, c2 = V("ci", 16 * c, 16 * c + ns), V("ci", 16 * c + 8, 16 * c + 8 + ns)
+        ts(c1, S("sv2"), col(CU), OP.add, 120.5, OP.mult)
+        ts(c2, c1, 6, OP.logical_shift_right, P - 1, OP.bitwise_and)
+        cp(co, c2)
+        tt(N("my"), IND(V("ys", 0, P), co), N("xp"), OP.max)
+        act(N("yg"), IND(V("ys", 0, P), co), AF.Copy)
+        act(N("kc"), IND(V("ks", 0, P), co), AF.Identity, -float(M))
+        act(N("c3"), IND(V("cio"), co), AF.Copy)
+        act(N("r"), pu, AF.Identity, col(RB))
+        pv, ph, pd, pz = R(be, 2), R(be, 3), R(be, 4), R(be, 5)
+        group(pv, [(mat("Iv"), one), (mat("nI"), N("r")), (mat("H2"), N("xp"))])
+        tt(N("prod"), pv, N("n"), OP.mult)
+        tt(N("sm"), pk, N("prod"), OP.add)
+        ts(N("new"), N("sm"), 5, OP.logical_shift_right, M - 1, OP.bitwise_and)
+        group(ph, [(mat("OB"), t("tht")), (mat("nOB"), N("xp")), (mat("nOB"), N("yg")), (mat("O2B"), N("my"))])
+        group(pd, [(mat("nI"), N("xp")), (mat("I"), N("yg"))])
+        tt(N("kp"), ph, N("kc"), OP.max)
+        ts(ho, ph, 0.0, OP.is_lt)
+        if s < ST - 1:
+            send(V("ox%d" % s, 3 * c0, 3 * c0 + 3 * n), V("lx%d" % (s + 1), 3 * c0, 3 * c0 + 3 * n), "ax%d_%d" % (s + 1, c))
+        ts(N("mM"), N("kp"), 0.0, OP.is_ge, -float(M), OP.mult)
         tt(N("he"), pn, N("kp"), OP.is_equal)
-        cd, ct, eq = V("cd%d" % c, 0, ns), "ct%d" % c, "eq%d" % c
-        act(cd, S("sv2"), AF.Identity, col(SC))
-        group(V(be, 0, 128, p1=ns), [(cd, mat("I"))])
-        act(V(ct, p1=ns), V(be, 0, 128, p1=ns), AF.Identity, 0.0, -1.0)
-        o = 0
-        for j in range(ns):
-            wd = 16 * (j + 1)
-            group(V(be, o, o + wd), [(V(ct, p1=48), V("zr", j * NM, j * NM + wd, p1=48)), (mat("I"), V("c3", c0, c0 + wd))])
-            o += wd
-        ts(V(eq, 0, o), V(be, 0, o), 0.0, OP.is_equal, 1 / 16, OP.mult)
-        mm(V(be, 0, n), mat("I"), N("c3"), True, False)
-        mm(V(be, 0, n), mat("IB"), t("mk"), False, False)
-        o = 0
-        for j in range(ns):
-            wd = 16 * (j + 1)
-            mm(V(be, 0, wd), mat("OB"), V(eq, o, o + wd), False, j == ns - 1)
-            o += wd
-        scan(N("sv3"), V("dl", 0, n), V(be, 0, n), OP.max)
-        ts(lo, S("sv3"), 256.0, OP.add)
         tt(N("newM"), N("new"), N("mM"), OP.add)
         tt(N("tA"), N("kp"), N("newM"), OP.min)
         npc = -(-16 // (512 // n))
         cuts = [-(-16 * i // npc) for i in range(npc + 1)]
-        pacc = V(al, 0, n)
-        for j, (lhs, rhs) in enumerate([(mat("IB"), t("dt%d" % s)), (mat("I16B"), sa), (mat("I16B"), N("fst")), (mat("nI32B"), N("go"))]):
-            mm(pacc, lhs, rhs, j == 0, False)
+        pacc = R(al, 5)
         for i in range(npc):
             ka, kb = cuts[i], cuts[i + 1]
-            zb, zc = wide[0], wide[1]
+            zb = wide[i % 2]
+            it = []
             for k in range(ka, kb):
-                group(V(zb, (k - ka) * n, (k - ka + 1) * n), [(mat("nI"), V(e16, k, 16 * n, 16)), (mat("I16"), t1_)])
-            act(V(wa, ka * n, kb * n), V(zb, 0, (kb - ka) * n), AF.Sign, 2072.0)
-            for k in range(ka, kb):
-                group(V(zc, (k - ka) * n, (k - ka + 1) * n), [(mat("nI"), V(e16, k, 16 * n, 16)), (mat("I16"), t2_)])
-            ts(V(wq, ka * n, kb * n), V(zc, 0, (kb - ka) * n), -2080.0, OP.is_equal, 2.0, OP.mult)
+                it += terms(V(zb, (k - ka) * n, (k - ka + 1) * n), [(mat("I"), V(e16, k, 16 * n, 16)), (mat("nI"), N("tq"))])
+            mms(it)
+            act(V(wa, ka * n, kb * n), V(zb, 0, (kb - ka) * n), AF.Gelu, 0.0, FOLD)
+            ts(V(wq, ka * n, kb * n), V(wa, ka * n, kb * n), MAGIC, OP.add, MAGIC, OP.not_equal)
         for i in range(npc):
-            for src in (wa, wq):
-                for k in range(cuts[i], cuts[i + 1]):
-                    mm(pacc, V("selh", 15 - k, 143 - k), V(src, k * n, (k + 1) * n), False, False)
-        mm(pacc, mat("nI128"), N("mM"), False, False)
-        mm(pacc, mat("I32B"), N("he"), False, True)
+            it = []
+            if i == 0:
+                it = [(pacc, l_, r_, j == 0, False) for j, (l_, r_) in
+                      enumerate([(mat("IB"), t("dt%d" % s)), (mat("I16B"), sa), (mat("I16B"), f3[1]), (mat("nI16B"), f3[2])])]
+            it += [(pacc, V("selh", 15 - k, 143 - k), V(wq, k * n, (k + 1) * n), False, False) for k in range(cuts[i], cuts[i + 1])]
+            mms(it, opens=(i == 0))
+        mms([(pacc, mat("Im"), N("mM"), False, False), (pacc, mat("I32B"), N("he"), False, True)], closes=True)
         tt(N("t1"), pacc, N("tA"), OP.max)
-        tt(to, N("tM"), N("t1"), OP.min)
+        tt(to, N("n"), N("t1"), OP.min)
         if s < ST - 1:
             send(to, V("lt%d" % (s + 1), c0, c0 + n), "at%d_%d" % (s + 1, c))
         else:
-            store("sp", "yt", c0, c0 + n, to, "oyt%d" % c)
-        act(sw, to, AF.Sign, -4095.5)
-        if s < ST - 1:
-            send(V("ox%d" % s, 3 * c0, 3 * c0 + 3 * n), V("lx%d" % (s + 1), 3 * c0, 3 * c0 + 3 * n), "ax%d_%d" % (s + 1, c))
-        tt(N("hd"), N("dy"), ho, OP.mult)
-        group(V(be, 0, n), [(mat("I2"), ho), (mat("nIm"), N("mM")), (mat("nI"), sw)])
-        ts(N("zc"), V(be, 0, n), 0.0, OP.is_gt, float(M), OP.mult)
-        return xo, lo
+            act(N("tout"), to, AF.Identity, float(M))
+            store("sp", "yt", c0, c0 + n, N("tout"), "oyt%d" % c)
+        act(N("sw"), to, AF.Sign, 0.5)
+        tt(N("hd"), pd, ho, OP.mult)
+        group(pz, [(mat("I2"), ho), (mat("nIm"), N("mM")), (mat("nI"), N("sw"))])
+        ts(N("zc"), pz, 2.0, OP.is_gt, float(M), OP.mult)
+        cd, ct, eq = V("cd%d" % c, 0, ns), "ct%d" % c, "eq%d" % c
+        ts(cd, c2, -256.0, OP.add)
+        pt = V(w1, 0, 128, p1=ns)
+        group(pt, [(cd, mat("I"))])
+        act(V(ct, p1=ns), pt, AF.Identity, 0.0, -1.0)
+        o, it = 0, []
+        for j in range(ns):
+            wd = 16 * (j + 1)
+            it += terms(V(w1, 128 + o, 128 + o + wd), [(V(ct, p1=48), V("zr", j * NM, j * NM + wd, p1=48)), (mat("I"), V("c3", c0, c0 + wd))])
+            o += wd
+        mms(it)
+        ts(V(eq, 0, o), V(w1, 128, 128 + o), 0.0, OP.is_equal, 1 / 16, OP.mult)
+        it = [(V(w1, 0, n), mat("I"), N("c3"), True, False), (V(w1, 0, n), mat("IB"), t("mk"), False, False)]
+        o = 0
+        for j in range(ns):
+            wd = 16 * (j + 1)
+            it.append((V(w1, 0, wd), mat("OB"), V(eq, o, o + wd), False, j == ns - 1))
+            o += wd
+        mms(it)
+        scan(N("sv3"), V("dl", 0, n), V(w1, 0, n), OP.max)
+        ts(lo, S("sv3"), 256.0, OP.add)
+        return lo
 
     for s in range(ST):
         left = [walk(s, c) for c in range(NC)]
         for c in range(NC):
-            xo, lo = left[c]
             a, b = C0[c], C0[c] + CH[c]
             cur[0] = LAG * c
-            tt(IND(V("ys"), lo), xo, V("hd", a, b), OP.add)
-            tt(IND(V("ks"), lo), V("n", a, b), V("zc", a, b), OP.max)
+            tt(IND(V("ys"), left[c]), V("xp", a, b), V("hd", a, b), OP.add)
+            tt(IND(V("ks"), left[c]), V("n", a, b), V("zc", a, b), OP.max)
     store("act", "yy", 0, P, V("ys", 0, P), "oyy")
     store("sp", "yk", 0, P, V("ks", 0, P), "oyk")
     return ops
@@ -501,28 +562,49 @@ def schedule(ops):
     succ = [[] for _ in range(n)]
     for i, o in enumerate(ops):
         for j, sync in o["deps"].items():
-            gp = (ops[j]["lat"] + (LAT_S if ops[j]["eng"] == o["eng"] else LAT_X)) if sync else 0.0
+            gp = (ops[j]["lat"] + PAR["LAT_S" if ops[j]["eng"] == o["eng"] else "LAT_X"]) if sync else 0.0
             pred[i].append((j, gp))
             succ[j].append((i, gp))
     cost = [max(o["cost"], 1.0) for o in ops]
+    lb = PAR["LAT_B"]
+
+    def first(lst, t):
+        lo, hi = 0, len(lst)
+        while lo < hi:
+            mid = (lo + hi) // 2
+            if lst[mid][1] <= t:
+                lo = mid + 1
+            else:
+                hi = mid
+        return lo
 
     def place(seq, before, head):
         busy, end = {}, [0.0] * n
         for i in seq:
             st = max([head[i]] + [end[j] + gp for j, gp in before[i]])
-            lst = busy.setdefault(ops[i]["eng"], [])
-            lo, hi = 0, len(lst)
-            while lo < hi:
-                mid = (lo + hi) // 2
-                if lst[mid][1] <= st:
-                    lo = mid + 1
-                else:
-                    hi = mid
-            while lo < len(lst) and lst[lo][0] < st + cost[i]:
-                st = max(st, lst[lo][1])
-                lo += 1
-            lst.insert(lo, (st, st + cost[i]))
-            end[i] = st + cost[i]
+            e, c = ops[i]["eng"], cost[i]
+            lst = busy.setdefault(e, [])
+            while True:
+                s0 = st
+                lo = first(lst, st)
+                while lo < len(lst) and lst[lo][0] < st + c:
+                    st = max(st, lst[lo][1])
+                    lo += 1
+                for bk in ops[i]["banks"]:
+                    for e2 in ("pe", "dve", "act"):
+                        if e2 != e:
+                            bl = busy.get((bk, e2), [])
+                            k = first(bl, st - lb)
+                            while k < len(bl) and bl[k][0] < st + c + lb:
+                                st = max(st, bl[k][1] + lb)
+                                k += 1
+                if st == s0:
+                    break
+            lst.insert(lo, (st, st + c))
+            for bk in ops[i]["banks"]:
+                bl = busy.setdefault((bk, e), [])
+                bl.insert(first(bl, st), (st, st + c))
+            end[i] = st + c
         return end
 
     z = [SEED]
@@ -553,11 +635,38 @@ def schedule(ops):
             seq = sorted(range(n), key=lambda i: (-back[i], i))
         seq = by_key([cost[i] - best[1][i] + JIT * rnd() for i in range(n)])
     span, end = best
-    order = {}
-    for i in sorted(range(n), key=lambda i: (end[i] - cost[i], i)):
+    for i in range(n):
         ops[i]["at"] = end[i] - cost[i]
-        order.setdefault(ops[i]["eng"], []).append(i)
-    return order, span
+    return sorted(range(n), key=lambda i: (ops[i]["at"], i)), span
+
+
+def link(ops, seq):
+    order, place, known, waits, needed = {}, {}, {}, {}, set()
+    after, bank = {}, {}
+    for i in seq:
+        o = ops[i]
+        e = o["eng"]
+        lst = order.setdefault(e, [])
+        place[i] = len(lst)
+        want = [j for j, sync in o["deps"].items() if sync]
+        if e == "pool" and lst and not o.get("send") and not ops[lst[-1]].get("send"):
+            want.append(lst[-1])
+        for bk in o["banks"]:
+            want += [j for e2, j in bank.setdefault(bk, {}).items() if e2 != e]
+            bank[bk][e] = i
+        lst.append(i)
+        kn = known.setdefault(e, {})
+        waits[i] = []
+        for j in sorted(set(want), key=lambda j: -(ops[j]["at"] + ops[j]["cost"] + ops[j]["lat"])):
+            key = ops[j]["sem"] or ops[j]["eng"]
+            if kn.get(key, -1) < place[j]:
+                waits[i].append(j)
+                needed.add(j)
+                for k, v in after[j].items():
+                    kn[k] = max(kn.get(k, -1), v)
+        after[i] = dict(kn) if e != "net" else {}
+        after[i][o["sem"] or e] = place[i]
+    return order, waits, needed
 
 
 CACHE = {}
@@ -569,29 +678,14 @@ def rank_program(g, core, T, topo):
         return
     if not CACHE:
         CACHE["ops"] = plan()
-        CACHE["order"] = schedule(CACHE["ops"])[0]
-    ops, order = CACHE["ops"], CACHE["order"]
+        CACHE["link"] = link(CACHE["ops"], schedule(CACHE["ops"])[0])
+    ops = CACHE["ops"]
+    order, waits, needed = CACHE["link"]
     nr = len(T.cores)
     nxt, prv = T.cores[(rank + 1) % nr], T.cores[(rank - 1) % nr]
     rid, pid = topo.addr(nxt, core)
     ctx = {"rid": rid, "pid": pid, "mask": topo.mask(core, nxt)}
     n_out, n_in = len(topo.engines(core, nxt)), len(topo.engines(prv, core))
-    place = {i: k for lst in order.values() for k, i in enumerate(lst)}
-    waits, needed = {}, set()
-    for e, lst in order.items():
-        seen = {}
-        for i in lst:
-            want = {}
-            if e == "pool" and place[i] and not ops[i].get("send") and not ops[lst[place[i] - 1]].get("send"):
-                want[e] = lst[place[i] - 1]
-            for j, sync in ops[i]["deps"].items():
-                key = ops[j]["sem"] or ops[j]["eng"]
-                if sync and place[j] > seen.get(key, -1) and (key not in want or place[j] > place[want[key]]):
-                    want[key] = j
-            for key, j in want.items():
-                seen[key] = place[j]
-                needed.add(j)
-            waits[i] = list(want.values())
     mark, total = {}, {}
     for e, lst in order.items():
         for i in lst:
@@ -607,7 +701,8 @@ def rank_program(g, core, T, topo):
         for i in order.get(e, []):
             for j in waits[i]:
                 q.wait_ge(T.sem[mark[j][0]], mark[j][1])
-            ins = ops[i]["fn"](g, T, ctx)
+            for fn in ops[i]["fns"]:
+                ins = fn(g, T, ctx)
             if ops[i].get("send"):
                 sends += 1
             elif i in mark:

@@ -3,11 +3,11 @@ from concourse.mybir import AluOpType as OP, ActivationFunctionType as AF
 M, P, W, ST = 4096, 512, 160, 4
 CH = [80, 80]
 A_ENG = ["dve", "dve", "dve"]
-G_ENG = ["act", "act", "act"]
+G_ENG = ["dve", "act", "act"]
 NLOAD, NFIX = 4, 8
-LAG = 4000.0
+LAG = 2500.0
 ROUNDS = 60
-SEED = 1
+SEED = 2
 JIT = 150.0
 BIG = 16384.0
 STEP = 131072.0
@@ -20,22 +20,24 @@ NC = len(CH)
 C0 = [sum(CH[:i]) for i in range(NC)]
 NM = max(CH)
 NS = NM // 16
+KX = 97
 DIAG = {"I": 1.0, "nI": -1.0, "I2": 2.0, "I17": 17.0, "nI16": -16.0, "IB": BIG, "I16B": 16 * BIG, "nI16B": -16 * BIG, "I32B": 32 * BIG,
-        "Im": -32 * BIG / M, "nI2k": -2048.0, "I240": LOW, "Iv": VB, "nIm": -2.0 / M}
+        "nI2k": -2048.0, "I240": LOW, "Iv": VB}
 MATS = list(DIAG) + ["OH", "On2", "OB", "nOB", "O2B", "O1k", "nO1k", "KW", "nKW", "Hp", "Hn", "H2", "TRI", "TRS", "TRL", "TRV"]
-NB16 = ["sa", "cand", "mx", "e", "bz", "tq", "xp", "r", "my", "yg", "mM", "he", "hd", "c3", "x0s", "sw"]
-NF32 = ["n", "sv1", "sv2", "sv3", "kc", "kp", "prod", "newM", "tA", "t1", "zc", "t0f", "tout"]
+NB16 = ["sa", "cand", "mx", "e", "bz", "tq", "xp", "r", "my", "yg", "gs", "he", "hd", "c3", "x0s", "sw", "rb", "s2"]
+NF32 = ["n", "sv1", "sv2", "sv3", "kc", "kp", "prod", "nM", "tA", "t1", "zc", "t0f", "tout"]
 NI32 = ["w1", "sm", "new", "t0s"]
 TILES = ["turn", "w16", "d0", "dt0", "dt1", "dt2", "dt3", "tht", "mk", "rr", "da", "db", "dc", "cm8"]
 
 SCRATCH = {
-    "fr": ("sbuf", [128, M], "bfloat16"), "fq": ("sbuf", [128, M], "bfloat16"), "ft": ("sbuf", [128, 2 * M], "bfloat16"),
+    "fr": ("sbuf", [128, M], "bfloat16"), "fq": ("sbuf", [128, M], "bfloat16"), "ft": ("sbuf", [128, 3 * M], "bfloat16"),
+    "kf": ("sbuf", [128, P + NM], "float32"),
     "ys": ("sbuf", [128, P + NM], "bfloat16"), "ks": ("sbuf", [128, P + NM], "float32"), "k0s": ("sbuf", [128, P], "int32"),
     "mats": ("sbuf", [128, 128 * len(MATS)], "bfloat16"), "i32s": ("sbuf", [128, 128], "float32"),
     "selh": ("sbuf", [128, 144], "bfloat16"), "selq": ("sbuf", [128, 144], "bfloat16"),
     "jrow": ("sbuf", [128, 144], "bfloat16"), "grow": ("sbuf", [128, 128], "bfloat16"),
     "jd": ("sbuf", [128, 128], "bfloat16"), "cio": ("sbuf", [128, P], "bfloat16"),
-    "rm": ("sbuf", [128, 16 * NM], "bfloat16"), "rm0": ("sbuf", [128, 16 * NM], "bfloat16"),
+    "rm": ("sbuf", [128, 16 * NM], "bfloat16"),
     "ones": ("sbuf", [128, 16 * NM], "bfloat16"), "zr": ("sbuf", [128, NS * NM], "bfloat16"),
     "tiles": ("sbuf", [128, NM * len(TILES)], "bfloat16"), "dl": ("sbuf", [128, NM], "float32"),
     "cols": ("sbuf", [128, 32], "float32"), "icol": ("sbuf", [128, 8], "int32"), "hb": ("sbuf", [128, 8], "bfloat16"),
@@ -67,15 +69,15 @@ for _s in range(ST):
 for _b in range(8):
     SCRATCH["pb%d" % _b] = ("psum", [128, 512], "float32")
 
-LOADS = ["f%d" % _i for _i in range(NLOAD)] + ["fb", "t0", "x0", "y0", "k0", "dw", "hw", "th"]
+LOADS = ["f%d" % _i for _i in range(NLOAD)] + ["fb", "fc", "t0", "x0", "y0", "k0", "dw", "hw", "th"]
 SEMAPHORES = ["pe", "dve", "act", "pool", "sent"] + ["l" + s for s in LOADS] + ["oyy", "oyk"]
 for _c in range(NC):
     SEMAPHORES += ["oyx%d" % _c, "oyt%d" % _c]
     for _s in range(1, ST):
         SEMAPHORES += ["ax%d_%d" % (_s, _c), "at%d_%d" % (_s, _c)]
 
-PAR = {"CYC": 0.83, "PCYC": 0.45, "FIXV": 60.0, "FIXA": 75.0, "FIXP": 5.0, "GATH": 1.56, "SCAT": 3.8,
-       "LAT_X": 180.0, "LAT_S": 120.0, "LAT_B": 180.0, "LAT_NET": 3000.0, "SEND": 500.0}
+PAR = {"CYC": 0.83, "PCYC": 0.42, "FIXV": 35.0, "FIXA": 45.0, "FIXP": 0.0, "GATH": 1.56, "SCAT": 3.8,
+       "LAT_X": 200.0, "LAT_S": 200.0, "LAT_B": 230.0, "LAT_NET": 3000.0, "SEND": 500.0}
 
 
 def V(name, c0=0, c1=None, step=1, p0=0, p1=128):
@@ -263,9 +265,9 @@ def plan():
     load("act", V("hws", 0, 1), "hw", "lhw", 2500.0)
     load("act", V("dws"), "dw", "ldw", 2500.0)
     load("act", V("ths", 0, 1), "th", "lth", 2500.0)
-    j = load("sp", V("k0s"), "k0", "lk0", 3000.0)
-    ops[j]["deps"][last] = True
-    j = load("sp", V("ys", 0, P), "y0", "ly0", 3500.0)
+    j = load("sp", V("k0s"), "k0", "lk0", 6800.0)
+    ops[j]["deps"][last] = None
+    j = load("sp", V("ys", 0, P), "y0", "ly0", 7200.0)
     ops[j]["deps"][j - 1] = None
 
     KC, G16, SC, SCK, CU, RB, PK, G15, KQ, HF, H1, H2C, H3, THC, TA_, TB_, KH, NKH, KL, DF = list(range(19)) + [20]
@@ -274,9 +276,8 @@ def plan():
     iota(V("grow"), [[16, 8], [0, 16]], 0, 0)
     iota(V("jrow"), [[1, 144]], 0, 0)
     ms(V("ones"), 1.0)
-    sel(V("rm0"), V("ones"), [[1, NM], [0, 16]], OP.is_equal, 0.0, 0, -1)
-    sel(V("rm", p0=64, p1=128), V("rm0", p0=64, p1=128), [[0, 16 * NM]], OP.not_equal, 1.0, 64 - NM, 1)
-    cp(V("rm", p0=0, p1=64), V("rm0", p0=0, p1=64))
+    sel(V("rm", p1=KX - 1), V("ones", p1=KX - 1), [[1, NM], [0, 16]], OP.is_equal, 0.0, 0, -1)
+    ms(V("rm", p0=KX - 1), 1.0)
     for n, c in DIAG.items():
         ts(mat(n), V("jd"), 0.0, OP.is_equal, c, OP.mult)
     ts(V("i32s"), V("jd"), 0.0, OP.is_equal)
@@ -318,7 +319,7 @@ def plan():
     ts(tile("da"), tile("rr"), col(KC), OP.is_equal, 64 * STEP, OP.mult)
     ts(tile("db"), tile("rr"), col(KC), OP.is_gt, -STEP, OP.mult)
     tt(tile("d0"), tile("da"), tile("db"), OP.add)
-    ts(V("cols", DF, DF + 4), V("dws"), -48.5, OP.add)
+    ts(V("cols", DF, DF + 4), V("dws"), -32.5, OP.add)
     for s in range(ST):
         ts(tile("dt%d" % s), V("ones", 0, NM), col(DF + s), OP.mult)
     ts(col(HF), V("ths", 0, 1), -1.0, OP.mult)
@@ -341,7 +342,9 @@ def plan():
     sel(V("zr", p0=32, p1=64), V("ones", 0, NS * NM, p0=32, p1=64), [[-16, NS], [1, NM]], OP.is_ge, 0.0, 0, -1)
     ms(V("ys", P, P + NM), 0.0)
     ms(V("ks", P, P + NM), 0.0)
-    cp(V("ks", 0, P), V("k0s"))
+    ms(V("kf", P, P + NM), 0.0)
+    ts(V("pb5"), V("k0s"), float(M), OP.is_ge, 2.0 * M, OP.mult)
+    tt(V("ks", 0, P), V("pb5"), V("k0s"), OP.add)
     for c in range(NC):
         ms(V("xt%d" % c), -XO)
         ms(V("ct%d" % c, p0=0, p1=32), 0.0)
@@ -361,6 +364,7 @@ def plan():
         group(z, [(mat("I"), V("fr", a, b)), (mat("I"), V("fq", a, b))])
         act(V("ft", a, b), z, AF.Copy)
     add("sp", 60.0, [lambda g, T, x: g.sync.dma_start(T.ft[:, M:2 * M], T.ft[:, 0:M])], [V("ft", 0, M)], [V("ft", M, 2 * M)], lat=8000.0, sem="lfb")
+    add("sp", 60.0, [lambda g, T, x: g.sync.dma_start(T.ft[:, 2 * M:3 * M], T.ft[:, 0:M])], [V("ft", 0, M)], [V("ft", 2 * M, 3 * M)], lat=12000.0, sem="lfc")
 
     def walk(s, c):
         n, c0 = CH[c], C0[c]
@@ -391,7 +395,7 @@ def plan():
             tin = N("t0f")
             ts(N("w1"), N("t0s"), M - 1, OP.bitwise_and)
             cp(N("off"), N("w1"))
-            ts(tin, N("t0s"), -float(M), OP.add)
+            cp(tin, N("t0s"))
             if c:
                 act(x, N("x0s"), AF.Identity, XO, 16.0)
             act(xz, N("x0s"), AF.Relu, 8192.0, -8192.0)
@@ -400,12 +404,14 @@ def plan():
             tin = V("lt%d" % s, c0, c0 + n)
             ts(N("off"), tin, float(M), OP.add)
             win = V("ft")
-        act(sa, tin, AF.Sign, 0.5)
+        act(sa, tin, AF.Sign, 0.5 - M)
+        act(N("rb"), tin, AF.Identity, VB + M - 2047.5)
         xq = V(be, 2 * n, 2 * n + 128, p1=n)
         group(xq, [(x, mat("I"))])
         act(V("xt%d" % c, p1=n), xq, AF.Identity, -XO / 16, 1 / 16)
-        group(pn, [(V("i32s"), tin), (mat("nI2k"), sa), (mat("nI2k"), one)])
+        group(pn, [(V("i32s"), tin), (mat("nI"), N("rb")), (mat("Iv"), one)])
         act(N("n"), pn, AF.Identity, float(M))
+        act(N("nM"), pn, AF.Identity, 2.0 * M)
         act(pk, pn, AF.Identity, col(PK), 33.0)
         sums = []
         for i, a in enumerate(range(0, n, 32)):
@@ -417,8 +423,8 @@ def plan():
             else:
                 cp(fp, src)
             ts(ep, fp, XO - 7.5, OP.add)
-            z = V(wide[i % 2], 0, 16 * (b - a))
-            tm = [(V("xt%d" % c, p1=NM + 1), V("rm", 16 * a, 16 * b, p1=NM + 1)), (mat("I"), ep)]
+            z = V(wide[i], 0, 16 * (b - a)) if i < 2 else V(al, 256, 256 + 16 * (b - a))
+            tm = [(V("xt%d" % c, p1=KX), V("rm", 16 * a, 16 * b, p1=KX)), (mat("I"), ep)]
             if A_ENG[i] == "act":
                 group(z, tm + [(mat("nI"), fp)])
                 act(wp, z, AF.Sign, 0.5)
@@ -454,15 +460,15 @@ def plan():
         tt(N("mx"), IND(V(e16), ko), x, OP.max)
         act(N("e"), IND(V(e16), ko), AF.Relu, -XO)
         act(N("bz"), IND(V(e16), ko), AF.Relu, 32 * (XO + 16), -32.0)
-        pu, pp, px = R(al, 2), R(al, 1), R(w1, 0)
+        pu, pp, px = R(be, 4), R(al, 1), R(w1, 0)
         group(pu, [(mat("Hn"), x), (mat("Hp"), N("mx")), (mat("Hn"), N("e"))])
         group(pp, [(mat("I240"), one), (mat("I17"), x), (mat("I"), xz), (mat("nI16"), N("mx")), (mat("I"), N("bz"))])
         group(px, [(mat("nI"), x), (mat("I2"), N("mx")), (mat("nI"), N("e"))])
         tt(N("tq"), pp, N("mx"), OP.max)
         act(N("xp"), px, AF.Identity, -XO / 16, 1 / 16)
         if s < ST - 1:
-            act(xo, px, AF.Copy)
-            act(zo, px, AF.Relu, 8192.0 + 512 * XO, -512.0)
+            act(xo, N("xp"), AF.Identity, XO, 16.0)
+            act(zo, N("xp"), AF.Relu, 8192.0, -8192.0)
         else:
             store("act", "yx", c0, c0 + n, N("xp"), "oyx%d" % c)
         scan(N("sv2"), t("d0"), pu)
@@ -486,16 +492,15 @@ def plan():
         ts(ho, ph, 0.0, OP.is_lt)
         if s < ST - 1:
             send(V("ox%d" % s, 3 * c0, 3 * c0 + 3 * n), V("lx%d" % (s + 1), 3 * c0, 3 * c0 + 3 * n), "ax%d_%d" % (s + 1, c))
-        ts(N("mM"), N("kp"), 0.0, OP.is_ge, -float(M), OP.mult)
+        act(N("gs"), N("kp"), AF.Sign, 0.5)
         tt(N("he"), pn, N("kp"), OP.is_equal)
-        tt(N("newM"), N("new"), N("mM"), OP.add)
-        tt(N("tA"), N("kp"), N("newM"), OP.min)
+        tt(N("tA"), N("kp"), N("new"), OP.min)
         npc = -(-16 // (512 // n))
         cuts = [-(-16 * i // npc) for i in range(npc + 1)]
         pacc = R(al, 5)
         for i in range(npc):
             ka, kb = cuts[i], cuts[i + 1]
-            zb = wide[i % 2]
+            zb = (wide + [al])[i]
             it = []
             for k in range(ka, kb):
                 it += terms(V(zb, (k - ka) * n, (k - ka + 1) * n), [(mat("I"), V(e16, k, 16 * n, 16)), (mat("nI"), N("tq"))])
@@ -509,18 +514,20 @@ def plan():
                       enumerate([(mat("IB"), t("dt%d" % s)), (mat("I16B"), sa), (mat("I16B"), f3[1]), (mat("nI16B"), f3[2])])]
             it += [(pacc, V("selh", 15 - k, 143 - k), V(wq, k * n, (k + 1) * n), False, False) for k in range(cuts[i], cuts[i + 1])]
             mms(it, opens=(i == 0))
-        mms([(pacc, mat("Im"), N("mM"), False, False), (pacc, mat("I32B"), N("he"), False, True)], closes=True)
+        mms([(pacc, mat("I16B"), N("gs"), False, False), (pacc, mat("I32B"), N("he"), False, True)], closes=True)
         tt(N("t1"), pacc, N("tA"), OP.max)
-        tt(to, N("n"), N("t1"), OP.min)
+        tt(to, N("nM"), N("t1"), OP.min)
         if s < ST - 1:
             send(to, V("lt%d" % (s + 1), c0, c0 + n), "at%d_%d" % (s + 1, c))
-        else:
-            act(N("tout"), to, AF.Identity, float(M))
+        act(N("sw"), to, AF.Sign, 0.5 - M)
+        if s == ST - 1:
+            act(N("s2"), to, AF.Sign, 0.5)
+            group(pv, [(V("i32s"), to), (mat("nI2k"), N("s2"))])
+            act(N("tout"), pv, AF.Identity, 2048.0)
             store("sp", "yt", c0, c0 + n, N("tout"), "oyt%d" % c)
-        act(N("sw"), to, AF.Sign, 0.5)
         tt(N("hd"), pd, ho, OP.mult)
-        group(pz, [(mat("I2"), ho), (mat("nIm"), N("mM")), (mat("nI"), N("sw"))])
-        ts(N("zc"), pz, 2.0, OP.is_gt, float(M), OP.mult)
+        group(pz, [(mat("I2"), ho), (mat("I"), N("gs")), (mat("nI"), N("sw"))])
+        ts(N("zc"), pz, 1.0, OP.is_gt, float(M if s == ST - 1 else 3 * M), OP.mult)
         cd, ct, eq = V("cd%d" % c, 0, ns), "ct%d" % c, "eq%d" % c
         ts(cd, c2, -256.0, OP.add)
         pt = V(w1, 0, 128, p1=ns)
@@ -550,9 +557,11 @@ def plan():
             a, b = C0[c], C0[c] + CH[c]
             cur[0] = LAG * c
             tt(IND(V("ys"), left[c]), V("xp", a, b), V("hd", a, b), OP.add)
-            tt(IND(V("ks"), left[c]), V("n", a, b), V("zc", a, b), OP.max)
+            tt(IND(V("kf" if s == ST - 1 else "ks"), left[c]), V("n", a, b), V("zc", a, b), OP.max)
+        if s == ST - 2:
+            ts(V("kf", 0, P), V("ks", 0, P), float(M), OP.min)
     store("act", "yy", 0, P, V("ys", 0, P), "oyy")
-    store("sp", "yk", 0, P, V("ks", 0, P), "oyk")
+    store("sp", "yk", 0, P, V("kf", 0, P), "oyk")
     return ops
 
 
@@ -565,7 +574,7 @@ def schedule(ops):
             gp = (ops[j]["lat"] + PAR["LAT_S" if ops[j]["eng"] == o["eng"] else "LAT_X"]) if sync else 0.0
             pred[i].append((j, gp))
             succ[j].append((i, gp))
-    cost = [max(o["cost"], 1.0) for o in ops]
+    cost = [max(o["cost"], 1.0) + (PAR["LAT_S"] if o["eng"] == "pool" and not o.get("send") else 0.0) for o in ops]
     lb = PAR["LAT_B"]
 
     def first(lst, t):

@@ -3,10 +3,17 @@ from concourse.mybir import AluOpType as OP, ActivationFunctionType as AF
 M, P, W, ST = 4096, 512, 160, 4
 CH = [80, 80]
 A_ENG = ["dve", "dve", "dve"]
-G_ENG = ["dve", "act", "act"]
+G_ENG = ["act", "act", "dve"]
 NLOAD, NFIX = 4, 8
-LAG = 2500.0
-ROUNDS = 60
+Q_ENG = ["act", "act"]
+G0_ENG = ["act", "act", "act"]
+FORCE = False
+NPOOL = 11
+LATE = ["mats3840", "mats4096", "dl0", "kf0", "ks0"]
+LAGS = [2000.0, 2500.0, 3000.0, 3500.0]
+ROUNDS = 10
+MOVES, TEMP = 15000, 60.0
+CASES = [(1.0, 190.0), (1.35, 190.0)]
 SEED = 2
 JIT = 150.0
 BIG = 16384.0
@@ -16,21 +23,26 @@ LOW = 240.0
 FOLD = 0.192 / 16
 MAGIC = 1.5 * 2 ** 17
 VB = 786432.0
+KS = 4.0 * M
 NC = len(CH)
 C0 = [sum(CH[:i]) for i in range(NC)]
 NM = max(CH)
 NS = NM // 16
 KX = 97
-DIAG = {"I": 1.0, "nI": -1.0, "I2": 2.0, "I17": 17.0, "nI16": -16.0, "IB": BIG, "I16B": 16 * BIG, "nI16B": -16 * BIG, "I32B": 32 * BIG,
-        "nI2k": -2048.0, "I240": LOW, "Iv": VB}
-MATS = list(DIAG) + ["OH", "On2", "OB", "nOB", "O2B", "O1k", "nO1k", "KW", "nKW", "Hp", "Hn", "H2", "TRI", "TRS", "TRL", "TRV"]
-NB16 = ["sa", "cand", "mx", "e", "bz", "tq", "xp", "r", "my", "yg", "gs", "he", "hd", "c3", "x0s", "sw", "rb", "s2"]
-NF32 = ["n", "sv1", "sv2", "sv3", "kc", "kp", "prod", "nM", "tA", "t1", "zc", "t0f", "tout"]
+DIAG = {"I": 1.0, "nI": -1.0, "I2": 2.0, "I17": 17.0, "nI16": -16.0, "IB": BIG, "I16B": 16 * BIG, "I32B": 32 * BIG,
+        "I8k": 2.0 * M, "I4k": 1.0 * M, "nI2k": -2048.0, "I240": LOW, "I120": LOW / 2, "Iv": VB * KS, "nIr": -KS, "Iw": VB - M}
+MATS = list(DIAG) + ["O1", "OH", "On2", "OB", "nOB", "O2B", "KW", "KW0", "KWL", "Hp", "Hn", "H2", "TRI", "TRS", "TRL", "TRV", "TR0", "D0", "D15", "nD15"]
+NB16 = ["sa", "cand", "mx", "e", "bz", "tq", "xp", "r", "my", "yg", "gs", "he", "hd", "c3", "x0s", "rb", "s2"]
+NF32 = ["n", "sv1", "sv2", "sv3", "kc", "kp", "prod", "zc", "tin", "tout"]
 NI32 = ["w1", "sm", "new", "t0s"]
-TILES = ["turn", "w16", "d0", "dt0", "dt1", "dt2", "dt3", "tht", "mk", "rr", "da", "db", "dc", "cm8"]
+TILES = ["turn", "w16", "d0", "tht", "mk", "rr", "da", "db", "dc", "cm8"]
+CUTS = [0, 6, 12, 16]
+FRESH = 1
+ON_DVE2 = 3
+ON_DVE = 3
 
 SCRATCH = {
-    "fr": ("sbuf", [128, M], "bfloat16"), "fq": ("sbuf", [128, M], "bfloat16"), "ft": ("sbuf", [128, 3 * M], "bfloat16"),
+    "fr": ("sbuf", [128, M], "bfloat16"), "qw": ("sbuf", [128, 16 * W], "bfloat16"), "ft": ("sbuf", [128, 3 * M], "bfloat16"),
     "kf": ("sbuf", [128, P + NM], "float32"),
     "ys": ("sbuf", [128, P + NM], "bfloat16"), "ks": ("sbuf", [128, P + NM], "float32"), "k0s": ("sbuf", [128, P], "int32"),
     "mats": ("sbuf", [128, 128 * len(MATS)], "bfloat16"), "i32s": ("sbuf", [128, 128], "float32"),
@@ -38,11 +50,12 @@ SCRATCH = {
     "jrow": ("sbuf", [128, 144], "bfloat16"), "grow": ("sbuf", [128, 128], "bfloat16"),
     "jd": ("sbuf", [128, 128], "bfloat16"), "cio": ("sbuf", [128, P], "bfloat16"),
     "rm": ("sbuf", [128, 16 * NM], "bfloat16"),
-    "ones": ("sbuf", [128, 16 * NM], "bfloat16"), "zr": ("sbuf", [128, NS * NM], "bfloat16"),
+    "ones": ("sbuf", [128, NM], "bfloat16"), "zr": ("sbuf", [128, NS * NM], "bfloat16"),
     "tiles": ("sbuf", [128, NM * len(TILES)], "bfloat16"), "dl": ("sbuf", [128, NM], "float32"),
     "cols": ("sbuf", [128, 32], "float32"), "icol": ("sbuf", [128, 8], "int32"), "hb": ("sbuf", [128, 8], "bfloat16"),
     "dws": ("sbuf", [128, 4], "int32"), "hws": ("sbuf", [128, 4], "int32"), "ths": ("sbuf", [128, 4], "int32"),
     "off": ("sbuf", [128, W], "uint16"), "so": ("sbuf", [128, 32 * NC], "uint16"), "ci": ("sbuf", [128, 16 * NC], "int32"),
+    "tn": ("sbuf", [128, 2 * W], "float32"), "t2": ("sbuf", [128, 2 * W], "float32"), "dt": ("sbuf", [128, 2 * NM * ST], "bfloat16"),
     "f3": ("sbuf", [128, 3 * W], "bfloat16"), "kq": ("sbuf", [128, 3 * W], "bfloat16"),
 }
 for _n in NB16:
@@ -62,14 +75,14 @@ for _c in range(NC):
     SCRATCH["eq%d" % _c] = ("sbuf", [128, 8 * NS * (NS + 1)], "bfloat16")
 for _s in range(ST):
     SCRATCH["ox%d" % _s] = ("sbuf", [128, 3 * W], "bfloat16")
-    SCRATCH["ot%d" % _s] = ("sbuf", [128, W], "float32")
+    SCRATCH["ot%d" % _s] = ("sbuf", [128, W], "uint16")
     SCRATCH["lx%d" % _s] = ("sbuf", [128, 3 * W], "bfloat16")
     if _s:
-        SCRATCH["lt%d" % _s] = ("sbuf", [128, W], "float32")
+        SCRATCH["lt%d" % _s] = ("sbuf", [128, W], "uint16")
 for _b in range(8):
     SCRATCH["pb%d" % _b] = ("psum", [128, 512], "float32")
 
-LOADS = ["f%d" % _i for _i in range(NLOAD)] + ["fb", "fc", "t0", "x0", "y0", "k0", "dw", "hw", "th"]
+LOADS = ["f%d" % _i for _i in range(NLOAD)] + ["fa", "fb", "fc", "t0", "x0", "y0", "k0", "dw", "hw", "th"]
 SEMAPHORES = ["pe", "dve", "act", "pool", "sent"] + ["l" + s for s in LOADS] + ["oyy", "oyk"]
 for _c in range(NC):
     SEMAPHORES += ["oyx%d" % _c, "oyt%d" % _c]
@@ -215,8 +228,11 @@ def plan():
     def terms(out, ts_):
         return [(out, lhs, rhs, i == 0, i == len(ts_) - 1) for i, (lhs, rhs) in enumerate(ts_)]
 
-    def group(out, ts_):
-        mms(terms(out, ts_))
+    def group(out, ts_, early=0):
+        it = terms(out, ts_)
+        if early:
+            mms(it[:early], opens=True)
+        mms(it[early:], closes=early > 0)
 
     def iota(out, pattern, base, ch):
         if SCRATCH[out[0]][2] == "int32":
@@ -252,7 +268,7 @@ def plan():
     def col(i):
         return V("cols", i, i + 1)
 
-    cur[0] = -1e6
+    cur[0] = -1e3
     for i in range(NLOAD):
         a, b = M * i // NLOAD, M * (i + 1) // NLOAD
         j = load("sp", V("fr", a, b), "fx", "lf%d" % i, 2500.0 + 3500.0 * (i + 1) / NLOAD, a, b)
@@ -270,58 +286,78 @@ def plan():
     j = load("sp", V("ys", 0, P), "y0", "ly0", 7200.0)
     ops[j]["deps"][j - 1] = None
 
-    KC, G16, SC, SCK, CU, RB, PK, G15, KQ, HF, H1, H2C, H3, THC, TA_, TB_, KH, NKH, KL, DF = list(range(19)) + [20]
-    iota(V("jd"), [[1, 128]], 0, -1)
+    KC, G16, SC, SCK, CU, RB, PK, G15, KQ, HF, H1, H2C, H3, THC, TA_, TB_, KH, NKH, KL, K15, DF, KA, KB, KD, KE, KF, KG, KI = list(range(21)) + list(range(24, 31))
     iota(V("icol", 0, 1), [[0, 1]], 0, 1)
+    iota(V("jd"), [[1, 128]], 0, -1)
     iota(V("grow"), [[16, 8], [0, 16]], 0, 0)
     iota(V("jrow"), [[1, 144]], 0, 0)
+    iota(tile("turn"), [[0, NM // 4], [1, 4]], 0, 0)
+    iota(tile("rr"), [[0, NS], [1, 16]], 0, 0)
+    ms(V("rm"), 1.0)
     ms(V("ones"), 1.0)
-    sel(V("rm", p1=KX - 1), V("ones", p1=KX - 1), [[1, NM], [0, 16]], OP.is_equal, 0.0, 0, -1)
-    ms(V("rm", p0=KX - 1), 1.0)
-    for n, c in DIAG.items():
-        ts(mat(n), V("jd"), 0.0, OP.is_equal, c, OP.mult)
-    ts(V("i32s"), V("jd"), 0.0, OP.is_equal)
+    ms(V("zr"), 1.0)
+    sel(V("rm", p1=KX - 1), V("rm", p1=KX - 1), [[1, NM], [0, 16]], OP.is_equal, 0.0, 0, -1)
+    for i, (n, c) in enumerate(DIAG.items()):
+        if i < ON_DVE:
+            ts(mat(n), V("jd"), 0.0, OP.is_equal, c, OP.mult)
+        else:
+            act(mat(n), mat("I"), AF.Identity, 0.0, c)
+    act(V("i32s"), mat("I"), AF.Copy)
     ts(V("icol", 1, 2), V("icol", 0, 1), 15, OP.bitwise_and)
     ts(V("icol", 2, 3), V("icol", 0, 1), 112, OP.bitwise_and)
     cp(V("cols", KC, G16 + 1), V("icol", 1, 3))
     ts(col(SC), col(KC), -STEP, OP.mult, 15 * STEP, OP.add)
-    ts(col(SCK), col(KC), -STEP, OP.mult, 15 * STEP + 60 + 2048 - 16384, OP.add)
+    ts(col(SCK), col(KC), -STEP, OP.mult, 15 * STEP + 60 + 1024, OP.add)
+    ts(col(K15), col(KC), 15.0, OP.is_equal)
+    ts(col(KD), col(K15), -16 * BIG, OP.mult, 16 * BIG, OP.add)
+    ts(col(KE), col(K15), 16 * BIG, OP.mult, -16 * BIG, OP.add)
+    ts(col(KF), col(K15), -4.5, OP.mult)
+    ts(col(KG), col(K15), -1.0, OP.mult, 1.0, OP.add)
     ts(col(PK), col(KC), 37.0 * 32, OP.mult, 33.0 * M - 2.0 ** 23, OP.add)
     ts(col(G15), col(G16), 15.0, OP.add)
     ts(col(KQ), col(KC), -0.5, OP.mult, -3.5, OP.add)
     ts(col(KL), col(KC), 1.5, OP.mult, -34.5, OP.add)
     ts(col(KH), col(KC), 0.5, OP.mult)
     ts(col(NKH), col(KC), -0.5, OP.mult)
+    ts(col(KA), col(K15), 1031.5, OP.mult, col(NKH), OP.add)
+    ts(col(KB), col(K15), -7.5, OP.mult, col(KH), OP.add)
+    ts(col(KI), col(K15), 3.5, OP.mult, col(KQ), OP.add)
     ts(V("selh"), V("jrow"), col(G15), OP.is_equal, -BIG, OP.mult)
     act_a = "act" in A_ENG
     if act_a:
         ts(V("selq"), V("jrow"), col(G15), OP.is_equal, -BIG / 2, OP.mult)
     ts(col(H1), V("hws", 0, 1), 0.25, OP.mult)
     ts(col(H2C), V("hws", 0, 1), -0.125, OP.mult)
-    ts(col(H3), V("hws", 0, 1), 2.0, OP.mult)
-    for n, c in (("OH", -0.5), ("On2", -2.0), ("OB", BIG), ("nOB", -BIG), ("O2B", 2 * BIG), ("O1k", 1024.0), ("nO1k", -1024.0),
-                 ("KW", col(KH)), ("nKW", col(NKH)), ("Hp", col(H1)), ("Hn", col(H2C)), ("H2", col(H3))):
-        ts(mat(n), V("grow"), col(G16), OP.is_equal, c, OP.mult)
+    ts(col(H3), V("hws", 0, 1), 2.0 * KS, OP.mult)
+    for i, (n, c) in enumerate((("O1", 1.0), ("OH", -0.5), ("On2", -2.0), ("OB", BIG), ("nOB", -BIG), ("O2B", 2 * BIG), ("KW", col(KH)),
+                                ("KW0", col(KA)), ("KWL", col(KB)), ("Hp", col(H1)), ("Hn", col(H2C)), ("H2", col(H3)))):
+        if i < ON_DVE2:
+            ts(mat(n), V("grow"), col(G16), OP.is_equal, c, OP.mult)
+        else:
+            act(mat(n), mat("O1"), AF.Identity, 0.0, c)
+    for n, c in (("D0", KF), ("D15", KD), ("nD15", KE)):
+        ts(mat(n), V("jd"), 0.0, OP.is_equal, col(c), OP.mult)
     sel(mat("TRS"), mat("OH"), [[1, 128]], OP.is_gt, 0.0, 0, -1)
     sel(mat("TRI"), mat("TRS"), [[1, 128]], OP.not_equal, 4.0, 0, -1)
     sel(mat("TRV"), mat("On2"), [[-1, 128]], OP.is_gt, 0.0, 0, 1)
     tt(mat("TRL"), mat("TRI"), mat("TRV"), OP.add)
-    iota(tile("turn"), [[0, NM // 4], [1, 4]], 0, 0)
+    tt(mat("TR0"), mat("TRI"), mat("D0"), OP.add)
     iota(tile("w16"), [[16, NM]], 0, 0)
-    iota(tile("rr"), [[0, NS], [1, 16]], 0, 0)
     iota(V("cio"), [[1, P]], -256, 0)
-    for c in range(NC):
+    for c in sorted(set(CH.index(n) for n in CH)):
         n, o = CH[c], 3 * C0[c]
         ts(V("kq", o, o + n), tile("turn", n), col(KQ), OP.add)
-        ts(V("kq", o + n, o + 2 * n), tile("turn", n), col(KQ), OP.add, -1.0, OP.add)
+        ts(V("kq", o + 2 * n, o + 3 * n), tile("turn", n), -1.0, OP.add, col(KG), OP.mult)
+        ts(V("kq", o + n, o + 2 * n), V("kq", o + 2 * n, o + 3 * n), col(KI), OP.add)
         ts(V("kq", o + 2 * n, o + 3 * n), tile("turn", n), col(KL), OP.add)
     ts(tile("mk"), tile("rr"), col(KC), OP.not_equal)
     ts(tile("da"), tile("rr"), col(KC), OP.is_equal, 64 * STEP, OP.mult)
     ts(tile("db"), tile("rr"), col(KC), OP.is_gt, -STEP, OP.mult)
     tt(tile("d0"), tile("da"), tile("db"), OP.add)
     ts(V("cols", DF, DF + 4), V("dws"), -32.5, OP.add)
+    ms(V("dt"), 1.0)
     for s in range(ST):
-        ts(tile("dt%d" % s), V("ones", 0, NM), col(DF + s), OP.mult)
+        ts(V("dt", 2 * NM * s + 1, 2 * NM * (s + 1), 2), V("ones", 0, NM), col(DF + s), OP.mult)
     ts(col(HF), V("ths", 0, 1), -1.0, OP.mult)
     ts(col(TA_), col(KC), 0.0, OP.is_equal, col(HF), OP.mult)
     ts(col(TB_), col(KC), 1.0, OP.is_equal, -0.5, OP.mult)
@@ -338,13 +374,14 @@ def plan():
     iota(V("dl"), [[1, NM]], 256, 0)
     ts(tile("dc"), tile("mk"), -4096.0, OP.mult)
     tt(V("dl"), V("dl"), tile("dc"), OP.add)
-    sel(V("zr", p0=0, p1=32), V("ones", 0, NS * NM, p0=0, p1=32), [[1, NS], [0, NM]], OP.is_equal, 0.0, 0, -1)
-    sel(V("zr", p0=32, p1=64), V("ones", 0, NS * NM, p0=32, p1=64), [[-16, NS], [1, NM]], OP.is_ge, 0.0, 0, -1)
+    sel(V("zr", p0=0, p1=32), V("zr", p0=0, p1=32), [[1, NS], [0, NM]], OP.is_equal, 0.0, 0, -1)
+    sel(V("zr", p0=32, p1=64), V("zr", p0=32, p1=64), [[-16, NS], [1, NM]], OP.is_ge, 0.0, 0, -1)
     ms(V("ys", P, P + NM), 0.0)
     ms(V("ks", P, P + NM), 0.0)
     ms(V("kf", P, P + NM), 0.0)
-    ts(V("pb5"), V("k0s"), float(M), OP.is_ge, 2.0 * M, OP.mult)
-    tt(V("ks", 0, P), V("pb5"), V("k0s"), OP.add)
+    ts(V("kf", 0, P), V("k0s"), 1 / KS, OP.mult)
+    act(V("pb5"), V("kf", 0, P), AF.Sign, (0.5 - M) / KS)
+    tt(V("ks", 0, P), V("pb5"), V("kf", 0, P), OP.max)
     for c in range(NC):
         ms(V("xt%d" % c), -XO)
         ms(V("ct%d" % c, p0=0, p1=32), 0.0)
@@ -353,23 +390,26 @@ def plan():
             ts(V("ct%d" % c, h, e, p0=32, p1=64), V("tiles", tile("rr")[3], tile("rr")[3] + e - h, p0=32, p1=64),
                V("cols", KC, KC + 1, p0=32, p1=64), OP.is_equal, 1024.0, OP.mult)
         ms(V("e16_%d" % c, 16 * CH[c], 16 * CH[c] + 16), XO - LOW)
+    consts = [i for i, o in enumerate(ops) if o["eng"] == "dve" and o["tag"] not in LATE]
+    pool = [i for i, o in enumerate(ops) if o["eng"] == "pool"][:NPOOL]
+    for a, b in zip(pool, pool[1:]):
+        ops[b]["deps"].setdefault(a, None)
     j = act(V("lx0", 0, CH[0]), V("x0s", 0, CH[0]), AF.Gelu, XO, 16.0)
     ops[j]["cost"] += 1300.0
 
     nbk = 8 // NC
     for i in range(NFIX):
         a, b = M * i // NFIX, M * (i + 1) // NFIX
-        z = V("pb%d" % ((i % NC) * nbk + 2 + (i // NC) % 2), 0, b - a)
-        ts(V("fq", a, b), V("fr", a, b), 16.0, OP.is_lt, -LOW, OP.mult)
-        group(z, [(mat("I"), V("fr", a, b)), (mat("I"), V("fq", a, b))])
-        act(V("ft", a, b), z, AF.Copy)
-    add("sp", 60.0, [lambda g, T, x: g.sync.dma_start(T.ft[:, M:2 * M], T.ft[:, 0:M])], [V("ft", 0, M)], [V("ft", M, 2 * M)], lat=8000.0, sem="lfb")
-    add("sp", 60.0, [lambda g, T, x: g.sync.dma_start(T.ft[:, 2 * M:3 * M], T.ft[:, 0:M])], [V("ft", 0, M)], [V("ft", 2 * M, 3 * M)], lat=12000.0, sem="lfc")
+        ts(V("ft", a, b), V("fr", a, b), 16.0, OP.is_lt, -LOW, OP.mult)
+    add("pool", 1000.0, [lambda g, T, x: g.dma_start(T.ft[:, 0:M], T.fr[:, 0:M], accum_op=OP.add, max_dma_last_dim=4096)],
+        [V("fr"), V("ft", 0, M)], [V("ft", 0, M)], lat=6000.0, sem="lfa")
+    add("sp", 60.0, [lambda g, T, x: g.sync.dma_start(T.ft[:, M:2 * M], T.ft[:, 0:M])], [V("ft", 0, M)], [V("ft", M, 2 * M)], lat=4000.0, sem="lfb")
+    add("sp", 60.0, [lambda g, T, x: g.sync.dma_start(T.ft[:, 2 * M:3 * M], T.ft[:, 0:M])], [V("ft", 0, M)], [V("ft", 2 * M, 3 * M)], lat=6000.0, sem="lfc")
 
     def walk(s, c):
         n, c0 = CH[c], C0[c]
         ns = n // 16
-        cur[0] = LAG * c
+        cur[0] = float(c)
         al, be, w0, w1 = ["pb%d" % (c * nbk + i) for i in range(4)]
         wide = [w0, w1]
 
@@ -391,38 +431,48 @@ def plan():
         to = V("ot%d" % s, c0, c0 + n)
         one = V("ones", 0, n)
         sa, pn, pk = N("sa"), R(be, 0), R(be, 1)
+        tin = N("tin")
+        tA, nM = V("tn", 2 * c0, 2 * c0 + 2 * n, 2), V("tn", 2 * c0 + 1, 2 * c0 + 2 * n, 2)
         if s == 0:
-            tin = N("t0f")
+            off = "off"
             ts(N("w1"), N("t0s"), M - 1, OP.bitwise_and)
             cp(N("off"), N("w1"))
-            cp(tin, N("t0s"))
+            ts(tin, N("t0s"), float(M), OP.add)
             if c:
                 act(x, N("x0s"), AF.Identity, XO, 16.0)
             act(xz, N("x0s"), AF.Relu, 8192.0, -8192.0)
-            win = V("ft", 0, M)
+            win = V("fr")
         else:
-            tin = V("lt%d" % s, c0, c0 + n)
-            ts(N("off"), tin, float(M), OP.add)
+            off = "lt%d" % s
+            cp(tin, N(off))
             win = V("ft")
-        act(sa, tin, AF.Sign, 0.5 - M)
-        act(N("rb"), tin, AF.Identity, VB + M - 2047.5)
+        act(sa, tin, AF.Sign, 0.5 - 2 * M)
+        act(N("rb"), tin, AF.Identity, VB - 2047.5)
         xq = V(be, 2 * n, 2 * n + 128, p1=n)
         group(xq, [(x, mat("I"))])
         act(V("xt%d" % c, p1=n), xq, AF.Identity, -XO / 16, 1 / 16)
-        group(pn, [(V("i32s"), tin), (mat("nI"), N("rb")), (mat("Iv"), one)])
-        act(N("n"), pn, AF.Identity, float(M))
-        act(N("nM"), pn, AF.Identity, 2.0 * M)
+        group(pn, [(V("i32s"), tin), (mat("nI"), N("rb")), (mat("Iw"), one)])
+        act(N("n"), pn, AF.Identity, M / KS, 1 / KS)
+        act(nM, pn, AF.Identity, 2.0 * M)
         act(pk, pn, AF.Identity, col(PK), 33.0)
         sums = []
         for i, a in enumerate(range(0, n, 32)):
             b = min(n, a + 32)
-            src = IND(win, V("off", c0 + a, c0 + b))
+            src = IND(win, V(off, c0 + a, c0 + b))
             fp, ep, wp = V(fw, 16 * a, 16 * b), V(e16, 16 * a, 16 * b), V(wa, 16 * a, 16 * b)
-            if G_ENG[i] == "act":
+            if (G_ENG if s else G0_ENG)[i] == "act":
                 act(fp, src, AF.Copy)
             else:
                 cp(fp, src)
             ts(ep, fp, XO - 7.5, OP.add)
+            if s == 0 and c == 0 and i == 0 and FORCE:
+                for j in consts:
+                    ops[-1]["deps"].setdefault(j, None)
+            if s == 0:
+                if Q_ENG[c] == "dve":
+                    ts(V("qw", 16 * (c0 + a), 16 * (c0 + b)), fp, 16.0, OP.is_lt, -2.0, OP.mult)
+                else:
+                    act(V("qw", 16 * (c0 + a), 16 * (c0 + b)), fp, AF.Sign, -15.5)
             z = V(wide[i], 0, 16 * (b - a)) if i < 2 else V(al, 256, 256 + 16 * (b - a))
             tm = [(V("xt%d" % c, p1=KX), V("rm", 16 * a, 16 * b, p1=KX)), (mat("I"), ep)]
             if A_ENG[i] == "act":
@@ -436,34 +486,34 @@ def plan():
             tm.append((mat("IB"), hit0))
         if act_a:
             tm.append((mat("IB"), t("cm8")))
-        it = [(R(al, 0), l_, r_, i == 0, False) for i, (l_, r_) in enumerate(tm)]
-        runs = []
+        mms([(R(be, 5), l_, r_, i == 0, False) for i, (l_, r_) in enumerate(tm)], opens=True)
+        it, runs = [], []
         for i, a in enumerate(range(0, n, 32)):
             if runs and runs[-1][2] == A_ENG[i]:
                 runs[-1][1] = min(n, a + 32)
             else:
                 runs.append([a, min(n, a + 32), A_ENG[i]])
         for a, b, e in runs:
-            it += [(V(al, a, b), V("selq" if e == "act" else "selh", 15 - k, 143 - k), V(wa, 16 * a + k, 16 * b, 16), False, False) for k in range(16)]
+            it += [(V(be, 5 * n + a, 5 * n + b), V("selq" if e == "act" else "selh", 15 - k, 143 - k), V(wa, 16 * a + k, 16 * b, 16), False, False) for k in range(16)]
         it[-1] = it[-1][:4] + (True,)
-        mms(it)
-        act(N("cand"), R(al, 0), AF.Sign, -24.5 * BIG, -1.0)
+        mms(it, closes=True)
+        act(N("cand"), R(be, 5), AF.Sign, -24.5 * BIG, -1.0)
         f3 = [V("f3", 3 * c0 + i * n, 3 * c0 + (i + 1) * n) for i in range(3)]
-        mms([(R(al, 1, 3), mat("I"), V("kq", 3 * c0, 3 * c0 + 3 * n), True, False), (R(al, 1), mat("TRI"), N("cand"), False, False),
-             (R(al, 2), mat("TRI"), N("cand"), False, False), (R(al, 3), mat("TRL"), N("cand"), False, True)])
-        act(V("f3", 3 * c0, 3 * c0 + 3 * n), R(al, 1, 3), AF.Sign)
-        group(R(al, 0), [(mat("I"), t("w16")), (mat("KW"), f3[0]), (mat("nO1k"), f3[0]), (mat("nKW"), f3[1]), (mat("O1k"), f3[1]),
-                         (mat("KW"), f3[2]), (mat("nO1k"), f3[2])])
-        scan(N("sv1"), t("d0"), R(al, 0))
+        mms([(R(w0, 0, 3), mat("I"), V("kq", 3 * C0[CH.index(n)], 3 * C0[CH.index(n)] + 3 * n), True, False)], opens=True)
+        mms([(R(w0, 0), mat("TRI"), N("cand"), False, False), (R(w0, 1), mat("TR0"), N("cand"), False, False),
+             (R(w0, 2), mat("TRL"), N("cand"), False, True)], closes=True)
+        act(V("f3", 3 * c0, 3 * c0 + 3 * n), R(w0, 0, 3), AF.Sign)
+        group(R(w1, 0), [(mat("I"), t("w16")), (mat("KW"), f3[0]), (mat("KW0"), f3[1]), (mat("KWL"), f3[2])], 1)
+        scan(N("sv1"), t("d0"), R(w1, 0))
         ko, co, lo = V("so", 32 * c, 32 * c + ns), V("so", 32 * c + 8, 32 * c + 8 + ns), V("so", 32 * c + 16, 32 * c + 16 + ns)
         ts(ko, S("sv1"), col(SCK), OP.add, float(16 * n), OP.min)
         tt(N("mx"), IND(V(e16), ko), x, OP.max)
         act(N("e"), IND(V(e16), ko), AF.Relu, -XO)
-        act(N("bz"), IND(V(e16), ko), AF.Relu, 32 * (XO + 16), -32.0)
-        pu, pp, px = R(be, 4), R(al, 1), R(w1, 0)
-        group(pu, [(mat("Hn"), x), (mat("Hp"), N("mx")), (mat("Hn"), N("e"))])
-        group(pp, [(mat("I240"), one), (mat("I17"), x), (mat("I"), xz), (mat("nI16"), N("mx")), (mat("I"), N("bz"))])
-        group(px, [(mat("nI"), x), (mat("I2"), N("mx")), (mat("nI"), N("e"))])
+        act(N("bz"), IND(V(e16), ko), AF.Relu, 512 * (XO + 16), -512.0)
+        pu, pp, px = R(be, 4), R(al, 0), R(w1, 1)
+        group(pu, [(mat("Hn"), x), (mat("Hp"), N("mx")), (mat("Hn"), N("e"))], 1)
+        group(pp, [(mat("I240"), one), (mat("I17"), x), (mat("I"), xz), (mat("nI16"), N("mx")), (mat("I"), N("bz"))], 3)
+        group(px, [(mat("nI"), x), (mat("I2"), N("mx")), (mat("nI"), N("e"))], 1)
         tt(N("tq"), pp, N("mx"), OP.max)
         act(N("xp"), px, AF.Identity, -XO / 16, 1 / 16)
         if s < ST - 1:
@@ -478,15 +528,15 @@ def plan():
         cp(co, c2)
         tt(N("my"), IND(V("ys", 0, P), co), N("xp"), OP.max)
         act(N("yg"), IND(V("ys", 0, P), co), AF.Copy)
-        act(N("kc"), IND(V("ks", 0, P), co), AF.Identity, -float(M))
+        act(N("kc"), IND(V("ks", 0, P), co), AF.Identity, -float(M), KS)
         act(N("c3"), IND(V("cio"), co), AF.Copy)
         act(N("r"), pu, AF.Identity, col(RB))
-        pv, ph, pd, pz = R(be, 2), R(be, 3), R(be, 4), R(be, 5)
-        group(pv, [(mat("Iv"), one), (mat("nI"), N("r")), (mat("H2"), N("xp"))])
+        pv, ph, pd = R(be, 2), R(be, 3), R(be, 4)
+        group(pv, [(mat("Iv"), one), (mat("nIr"), N("r")), (mat("H2"), N("xp"))])
         tt(N("prod"), pv, N("n"), OP.mult)
         tt(N("sm"), pk, N("prod"), OP.add)
         ts(N("new"), N("sm"), 5, OP.logical_shift_right, M - 1, OP.bitwise_and)
-        group(ph, [(mat("OB"), t("tht")), (mat("nOB"), N("xp")), (mat("nOB"), N("yg")), (mat("O2B"), N("my"))])
+        group(ph, [(mat("OB"), t("tht")), (mat("nOB"), N("xp")), (mat("nOB"), N("yg")), (mat("O2B"), N("my"))], 2)
         group(pd, [(mat("nI"), N("xp")), (mat("I"), N("yg"))])
         tt(N("kp"), ph, N("kc"), OP.max)
         ts(ho, ph, 0.0, OP.is_lt)
@@ -494,40 +544,47 @@ def plan():
             send(V("ox%d" % s, 3 * c0, 3 * c0 + 3 * n), V("lx%d" % (s + 1), 3 * c0, 3 * c0 + 3 * n), "ax%d_%d" % (s + 1, c))
         act(N("gs"), N("kp"), AF.Sign, 0.5)
         tt(N("he"), pn, N("kp"), OP.is_equal)
-        tt(N("tA"), N("kp"), N("new"), OP.min)
-        npc = -(-16 // (512 // n))
-        cuts = [-(-16 * i // npc) for i in range(npc + 1)]
-        pacc = R(al, 5)
+        tt(tA, N("kp"), N("new"), OP.min)
+        cuts, npc = CUTS, len(CUTS) - 1
+        pboth, pacc = V(w0, 512 - 2 * n, 512), V(w0, 513 - 2 * n, 512, 2)
         for i in range(npc):
             ka, kb = cuts[i], cuts[i + 1]
             zb = (wide + [al])[i]
-            it = []
-            for k in range(ka, kb):
-                it += terms(V(zb, (k - ka) * n, (k - ka + 1) * n), [(mat("I"), V(e16, k, 16 * n, 16)), (mat("nI"), N("tq"))])
-            mms(it)
-            act(V(wa, ka * n, kb * n), V(zb, 0, (kb - ka) * n), AF.Gelu, 0.0, FOLD)
+            zk = [V(zb, (k - ka) * n, (k - ka + 1) * n) for k in range(ka, kb)]
+            src = [[(mat("I"), V(e16, k, 16 * n, 16))] + ([(mat("I120"), V("qw", 16 * c0 + k, 16 * (c0 + n), 16))] if s == 0 else [])
+                   for k in range(ka, kb)]
+            if i < FRESH:
+                it = [(zk[k], l_, v, False, False) for k in range(kb - ka) for l_, v in src[k]]
+                mms([it[0][:3] + (True, False)] + it[1:], opens=True)
+                mms([(zk[k - ka], mat("nI"), N("tq"), False, k == kb - 1) for k in range(ka, kb)], closes=True)
+            else:
+                mms([m_ for k in range(kb - ka) for m_ in terms(zk[k], src[k] + [(mat("nI"), N("tq"))])])
+            act(V(wa, ka * n, kb * n), V(zb, 0, (kb - ka) * n), AF.Gelu, -FOLD * LOW / 2 if s == 0 and Q_ENG[c] == "act" else 0.0, FOLD)
             ts(V(wq, ka * n, kb * n), V(wa, ka * n, kb * n), MAGIC, OP.add, MAGIC, OP.not_equal)
         for i in range(npc):
             it = []
             if i == 0:
-                it = [(pacc, l_, r_, j == 0, False) for j, (l_, r_) in
-                      enumerate([(mat("IB"), t("dt%d" % s)), (mat("I16B"), sa), (mat("I16B"), f3[1]), (mat("nI16B"), f3[2])])]
+                it = [(pboth, mat("IB"), V("dt", 2 * NM * s, 2 * NM * s + 2 * n), True, False)]
+                it += [(pacc, l_, r_, False, False) for l_, r_ in [(mat("I16B"), sa), (mat("D15"), f3[1]), (mat("nD15"), f3[2])]]
             it += [(pacc, V("selh", 15 - k, 143 - k), V(wq, k * n, (k + 1) * n), False, False) for k in range(cuts[i], cuts[i + 1])]
             mms(it, opens=(i == 0))
         mms([(pacc, mat("I16B"), N("gs"), False, False), (pacc, mat("I32B"), N("he"), False, True)], closes=True)
-        tt(N("t1"), pacc, N("tA"), OP.max)
-        tt(to, N("nM"), N("t1"), OP.min)
+        scan(V("t2", 2 * c0, 2 * c0 + 2 * n), pboth, V("tn", 2 * c0, 2 * c0 + 2 * n), OP.max)
+        tf = V("t2", 2 * c0 + 1, 2 * c0 + 2 * n, 2)
         if s < ST - 1:
+            ts(to, tf, float(M), OP.add)
             send(to, V("lt%d" % (s + 1), c0, c0 + n), "at%d_%d" % (s + 1, c))
-        act(N("sw"), to, AF.Sign, 0.5 - M)
-        if s == ST - 1:
-            act(N("s2"), to, AF.Sign, 0.5)
-            group(pv, [(V("i32s"), to), (mat("nI2k"), N("s2"))])
+        else:
+            act(N("s2"), tf, AF.Sign, 0.5)
+            group(pv, [(V("i32s"), tf), (mat("nI2k"), N("s2"))])
             act(N("tout"), pv, AF.Identity, 2048.0)
             store("sp", "yt", c0, c0 + n, N("tout"), "oyt%d" % c)
         tt(N("hd"), pd, ho, OP.mult)
-        group(pz, [(mat("I2"), ho), (mat("I"), N("gs")), (mat("nI"), N("sw"))])
-        ts(N("zc"), pz, 1.0, OP.is_gt, float(M if s == ST - 1 else 3 * M), OP.mult)
+        group(R(be, 5), [(mat("I8k"), ho), (mat("I4k"), N("gs"))])
+        tt(N("zc"), R(be, 5), tf, OP.is_gt)
+        if s == ST - 1:
+            act(N("n"), pn, AF.Identity, float(M))
+            ts(N("zc"), N("zc"), float(M), OP.mult)
         cd, ct, eq = V("cd%d" % c, 0, ns), "ct%d" % c, "eq%d" % c
         ts(cd, c2, -256.0, OP.add)
         pt = V(w1, 0, 128, p1=ns)
@@ -555,11 +612,11 @@ def plan():
         left = [walk(s, c) for c in range(NC)]
         for c in range(NC):
             a, b = C0[c], C0[c] + CH[c]
-            cur[0] = LAG * c
+            cur[0] = float(c)
             tt(IND(V("ys"), left[c]), V("xp", a, b), V("hd", a, b), OP.add)
             tt(IND(V("kf" if s == ST - 1 else "ks"), left[c]), V("n", a, b), V("zc", a, b), OP.max)
         if s == ST - 2:
-            ts(V("kf", 0, P), V("ks", 0, P), float(M), OP.min)
+            ts(V("kf", 0, P), V("ks", 0, P), KS, OP.mult, float(M), OP.min)
     store("act", "yy", 0, P, V("ys", 0, P), "oyy")
     store("sp", "yk", 0, P, V("kf", 0, P), "oyk")
     return ops
@@ -631,22 +688,115 @@ def schedule(ops):
     pri = [0.0] * n
     for i in range(n - 1, -1, -1):
         pri[i] = cost[i] + max([ops[i]["lat"]] + [gp + pri[k] for k, gp in succ[i]])
-    seq = by_key([pri[i] - ops[i]["lag"] for i in range(n)])
     zero, tail = [0.0] * n, [o["lat"] for o in ops]
-    best = None
-    for r in range(ROUNDS):
-        for p in range(2):
-            end = place(seq, pred, zero)
-            span = max(end[i] + tail[i] for i in range(n))
-            if best is None or span <= best[0]:
-                best = (span, end)
-            back = place(sorted(range(n), key=lambda i: (-end[i], -i)), succ, tail)
-            seq = sorted(range(n), key=lambda i: (-back[i], i))
-        seq = by_key([cost[i] - best[1][i] + JIT * rnd() for i in range(n)])
-    span, end = best
+    found = []
+    for lag in LAGS:
+        seq = by_key([pri[i] - lag * ops[i]["lag"] for i in range(n)])
+        best = None
+        for r in range(ROUNDS):
+            for p in range(2):
+                end = place(seq, pred, zero)
+                span = max(end[i] + tail[i] for i in range(n))
+                if best is None or span <= best[0]:
+                    best = (span, end)
+                back = place(sorted(range(n), key=lambda i: (-end[i], -i)), succ, tail)
+                seq = sorted(range(n), key=lambda i: (-back[i], i))
+            seq = by_key([cost[i] - best[1][i] + JIT * rnd() for i in range(n)])
+        found.append(best)
+    span, end = min(found, key=lambda b: b[0])
     for i in range(n):
         ops[i]["at"] = end[i] - cost[i]
     return sorted(range(n), key=lambda i: (ops[i]["at"], i)), span
+
+
+def improve(ops, seq):
+    n = len(ops)
+    eng = [o["eng"] for o in ops]
+    banks = [o["banks"] for o in ops]
+    pred = [list(o["deps"]) for o in ops]
+    succ = [[] for _ in range(n)]
+    for i in range(n):
+        for j in pred[i]:
+            succ[j].append(i)
+    cases = []
+    for pace, wake in CASES:
+        cost = [o["cost"] * (pace if o["eng"] in ("pe", "dve", "act") and not o["sem"] else 1.0)
+                + (wake if o["eng"] == "pool" and not o.get("send") else 0.0) for o in ops]
+        gaps = [[(j, ops[j]["lat"] + wake if s else 0.0) for j, s in o["deps"].items()] for o in ops]
+        cases.append((cost, gaps, [o["lat"] + wake for o in ops]))
+    tail = [o["lat"] for o in ops]
+
+    def run(seq, case):
+        cost, gaps, hop = case
+        end, via, free, last = [0.0] * n, [-1] * n, {}, {}
+        for i in seq:
+            e = eng[i]
+            v = free.get(e, -1)
+            st = end[v] if v >= 0 and e != "net" else 0.0
+            for j, gp in gaps[i]:
+                if end[j] + gp > st:
+                    st, v = end[j] + gp, j
+            for bk in banks[i]:
+                j = last.get(bk, -1)
+                if j >= 0 and eng[j] != e and end[j] + hop[j] > st:
+                    st, v = end[j] + hop[j], j
+                last[bk] = i
+            end[i], via[i], free[e] = st + cost[i], v, i
+        k = max(range(n), key=lambda i: end[i] + tail[i])
+        return end[k] + tail[k], end, via, k
+
+    z = [SEED]
+
+    def rnd():
+        z[0] = (z[0] * 1103515245 + 12345) % 2147483648
+        return z[0] / 2147483648
+
+    def judge(seq):
+        r = [run(seq, c) for c in cases]
+        return sum(x[0] for x in r) / len(r), r
+
+    cur, runs = judge(seq)
+    best = (cur, seq, runs)
+    for it in range(MOVES):
+        span, end, via, k = runs[int(rnd() * len(runs))]
+        pairs = []
+        while via[k] >= 0:
+            if via[k] not in ops[k]["deps"]:
+                pairs.append((via[k], k))
+            k = via[k]
+        if not pairs:
+            break
+        a, b = pairs[int(rnd() * len(pairs))]
+        pa, pb = seq.index(a), seq.index(b)
+        if rnd() < 0.5:
+            if rnd() < 0.3:
+                pa = max(0, pa - int(12 * rnd()))
+            win, take = seq[pa:pb + 1], {b}
+            for x in reversed(win):
+                if x in take:
+                    take.update(pred[x])
+            if a in take:
+                continue
+            new = seq[:pa] + [x for x in win if x in take] + [x for x in win if x not in take] + seq[pb + 1:]
+        else:
+            if rnd() < 0.3:
+                pb = min(n - 1, pb + int(12 * rnd()))
+            win, take = seq[pa:pb + 1], {a}
+            for x in win:
+                if x in take:
+                    take.update(succ[x])
+            if b in take:
+                continue
+            new = seq[:pa] + [x for x in win if x not in take] + [x for x in win if x in take] + seq[pb + 1:]
+        val, r = judge(new)
+        if val <= cur + TEMP * rnd() * (1 - it / MOVES):
+            seq, cur, runs = new, val, r
+            if val < best[0]:
+                best = (val, new, r)
+    end = best[2][0][1]
+    for i in range(n):
+        ops[i]["at"] = end[i] - cases[0][0][i]
+    return best[1], best[0]
 
 
 def link(ops, seq):
@@ -658,7 +808,7 @@ def link(ops, seq):
         lst = order.setdefault(e, [])
         place[i] = len(lst)
         want = [j for j, sync in o["deps"].items() if sync]
-        if e == "pool" and lst and not o.get("send") and not ops[lst[-1]].get("send"):
+        if e == "pool" and lst and not o.get("send") and not ops[lst[-1]].get("send") and not o["sem"] and not ops[lst[-1]]["sem"]:
             want.append(lst[-1])
         for bk in o["banks"]:
             want += [j for e2, j in bank.setdefault(bk, {}).items() if e2 != e]
@@ -687,7 +837,7 @@ def rank_program(g, core, T, topo):
         return
     if not CACHE:
         CACHE["ops"] = plan()
-        CACHE["link"] = link(CACHE["ops"], schedule(CACHE["ops"])[0])
+        CACHE["link"] = link(CACHE["ops"], improve(CACHE["ops"], schedule(CACHE["ops"])[0])[0])
     ops = CACHE["ops"]
     order, waits, needed = CACHE["link"]
     nr = len(T.cores)

@@ -2,18 +2,28 @@ from concourse.mybir import AluOpType as OP, ActivationFunctionType as AF
 
 M, P, W, ST = 4096, 512, 160, 4
 CH = [80, 80]
-A_ENG = ["dve", "dve", "dve"]
-G_ENG = ["act", "act", "dve"]
+ROUND = False
+TWIN = 0.1
+ON_POOL = ["Iv", "nIr", "I32B", "I8k", "I4k"]
+KLATE = 10
+SOON = 0.0
+GCUT = [32, 32]
+LAYOUT = {
+    80: ([(32, "act", "dve", 0, 0, 1), (32, "act", "dve", 1, 0, 1), (16, "act", "dve", 2, 256, 1)], [(0, 6, 0), (6, 12, 2), (12, 16, 1)], 0, 2),
+    96: ([(32, "dve", "act", 0, 0, 1), (32, "act", "dve", 1, 0, 1), (32, "act", "dve", 2, 0, 1)], [(0, 5, 0), (5, 9, 1), (9, 13, 2), (13, 16, 0)], 1, 2),
+    64: ([(32, "dve", "act", 0, 0, 1), (32, "act", "dve", 1, 0, 1)], [(0, 6, 0), (6, 12, 1), (12, 16, 2)], 0, 1),
+}
 NLOAD, NFIX = 4, 8
-Q_ENG = ["act", "act"]
-G0_ENG = ["act", "act", "act"]
-FORCE = False
+Q_ENG = ["dve", "dve"]
+FIRST = ["hw", "th", "dw"]
+PAIRS = False
+APART = True
 NPOOL = 11
 LATE = ["mats3840", "mats4096", "dl0", "kf0", "ks0"]
-LAGS = [2000.0, 2500.0, 3000.0, 3500.0]
-ROUNDS = 10
-MOVES, TEMP = 15000, 60.0
-CASES = [(1.0, 190.0), (1.35, 190.0)]
+LAGS = [2000.0, 2500.0]
+ROUNDS = 4
+MOVES, TEMP = 33000, 70.0
+CASES = [(1.0, 1.0, 160.0), (1.25, 1.4, 200.0)]
 SEED = 2
 JIT = 150.0
 BIG = 16384.0
@@ -29,15 +39,15 @@ C0 = [sum(CH[:i]) for i in range(NC)]
 NM = max(CH)
 NS = NM // 16
 KX = 97
-DIAG = {"I": 1.0, "nI": -1.0, "I2": 2.0, "I17": 17.0, "nI16": -16.0, "IB": BIG, "I16B": 16 * BIG, "I32B": 32 * BIG,
-        "I8k": 2.0 * M, "I4k": 1.0 * M, "nI2k": -2048.0, "I240": LOW, "I120": LOW / 2, "Iv": VB * KS, "nIr": -KS, "Iw": VB - M}
-MATS = list(DIAG) + ["O1", "OH", "On2", "OB", "nOB", "O2B", "KW", "KW0", "KWL", "Hp", "Hn", "H2", "TRI", "TRS", "TRL", "TRV", "TR0", "D0", "D15", "nD15"]
+DIAG = {"I": 1.0, "nI": -1.0, "I17": 17.0, "nI16": -16.0, "IB": BIG, "I16B": 16 * BIG, "I32B": 32 * BIG,
+        "I8k": 2.0 * M, "I4k": 1.0 * M, "I240": LOW, "Iv": VB * KS, "nIr": -KS}
+MATS = list(DIAG) + ["O1", "OH", "On2", "OB", "nOB", "O2B", "KW", "KW0", "KWL", "Hp", "Hn", "H2", "TRI", "TRS", "TRV", "TR0", "TRL", "D0", "D15", "nD15"]
 NB16 = ["sa", "cand", "mx", "e", "bz", "tq", "xp", "r", "my", "yg", "gs", "he", "hd", "c3", "x0s", "rb", "s2"]
-NF32 = ["n", "sv1", "sv2", "sv3", "kc", "kp", "prod", "zc", "tin", "tout"]
+NF32 = ["n", "sv1", "sv2", "sv3", "kc", "kp", "prod", "zc", "tin", "tout", "pks"]
 NI32 = ["w1", "sm", "new", "t0s"]
 TILES = ["turn", "w16", "d0", "tht", "mk", "rr", "da", "db", "dc", "cm8"]
 CUTS = [0, 6, 12, 16]
-FRESH = 1
+FRESH = 2
 ON_DVE2 = 3
 ON_DVE = 3
 
@@ -46,16 +56,16 @@ SCRATCH = {
     "kf": ("sbuf", [128, P + NM], "float32"),
     "ys": ("sbuf", [128, P + NM], "bfloat16"), "ks": ("sbuf", [128, P + NM], "float32"), "k0s": ("sbuf", [128, P], "int32"),
     "mats": ("sbuf", [128, 128 * len(MATS)], "bfloat16"), "i32s": ("sbuf", [128, 128], "float32"),
-    "selh": ("sbuf", [128, 144], "bfloat16"), "selq": ("sbuf", [128, 144], "bfloat16"),
+    "selh": ("sbuf", [128, 144], "bfloat16"), "seln": ("sbuf", [128, 144], "bfloat16"), "selp": ("sbuf", [128, 144], "bfloat16"),
     "jrow": ("sbuf", [128, 144], "bfloat16"), "grow": ("sbuf", [128, 128], "bfloat16"),
     "jd": ("sbuf", [128, 128], "bfloat16"), "cio": ("sbuf", [128, P], "bfloat16"),
-    "rm": ("sbuf", [128, 16 * NM], "bfloat16"),
+    "rm": ("sbuf", [128, 16 * NM], "bfloat16"), "zp": ("sbuf", [128, 8 * NS * (NS + 1)], "bfloat16"),
     "ones": ("sbuf", [128, NM], "bfloat16"), "zr": ("sbuf", [128, NS * NM], "bfloat16"),
     "tiles": ("sbuf", [128, NM * len(TILES)], "bfloat16"), "dl": ("sbuf", [128, NM], "float32"),
     "cols": ("sbuf", [128, 32], "float32"), "icol": ("sbuf", [128, 8], "int32"), "hb": ("sbuf", [128, 8], "bfloat16"),
     "dws": ("sbuf", [128, 4], "int32"), "hws": ("sbuf", [128, 4], "int32"), "ths": ("sbuf", [128, 4], "int32"),
     "off": ("sbuf", [128, W], "uint16"), "so": ("sbuf", [128, 32 * NC], "uint16"), "ci": ("sbuf", [128, 16 * NC], "int32"),
-    "tn": ("sbuf", [128, 2 * W], "float32"), "t2": ("sbuf", [128, 2 * W], "float32"), "dt": ("sbuf", [128, 2 * NM * ST], "bfloat16"),
+    "tn": ("sbuf", [128, 2 * W], "float32"), "dt": ("sbuf", [128, 2 * NM * ST], "bfloat16"),
     "f3": ("sbuf", [128, 3 * W], "bfloat16"), "kq": ("sbuf", [128, 3 * W], "bfloat16"),
 }
 for _n in NB16:
@@ -76,6 +86,8 @@ for _c in range(NC):
 for _s in range(ST):
     SCRATCH["ox%d" % _s] = ("sbuf", [128, 3 * W], "bfloat16")
     SCRATCH["ot%d" % _s] = ("sbuf", [128, W], "uint16")
+    SCRATCH["op%d" % _s] = ("sbuf", [128, 2 * W], "float32")
+    SCRATCH["lp%d" % _s] = ("sbuf", [128, 2 * W], "float32")
     SCRATCH["lx%d" % _s] = ("sbuf", [128, 3 * W], "bfloat16")
     if _s:
         SCRATCH["lt%d" % _s] = ("sbuf", [128, W], "uint16")
@@ -87,10 +99,10 @@ SEMAPHORES = ["pe", "dve", "act", "pool", "sent"] + ["l" + s for s in LOADS] + [
 for _c in range(NC):
     SEMAPHORES += ["oyx%d" % _c, "oyt%d" % _c]
     for _s in range(1, ST):
-        SEMAPHORES += ["ax%d_%d" % (_s, _c), "at%d_%d" % (_s, _c)]
+        SEMAPHORES += ["ax%d_%d" % (_s, _c), "at%d_%d" % (_s, _c)] + (["ah%d_%d" % (_s, _c)] if APART else []) + (["ap%d_%d" % (_s, _c)] if PAIRS else [])
 
-PAR = {"CYC": 0.83, "PCYC": 0.42, "FIXV": 35.0, "FIXA": 45.0, "FIXP": 0.0, "GATH": 1.56, "SCAT": 3.8,
-       "LAT_X": 200.0, "LAT_S": 200.0, "LAT_B": 230.0, "LAT_NET": 3000.0, "SEND": 500.0}
+PAR = {"CYC": 0.83, "PCYC": 0.42, "FIXV": 35.0, "FIXA": 45.0, "FIXP": 0.0, "GATH": 1.6, "SCAT": 3.8,
+       "LAT_X": 200.0, "LAT_S": 200.0, "LAT_B": 230.0, "LAT_NET": 2500.0, "SEND": 500.0, "ROWS": 800.0, "BYTE": 0.8, "SAFE": 500.0, "FIRST": 2500.0, "MINC": 40}
 
 
 def V(name, c0=0, c1=None, step=1, p0=0, p1=128):
@@ -130,7 +142,7 @@ def ap(T, v):
 def plan():
     ops = []
     wr, rd, pe_in, shut = {}, {}, {}, {}
-    cur = [0.0]
+    cur = [0.0, -9]
     CYC, PCYC = PAR["CYC"], PAR["PCYC"]
 
     def add(eng, cost, fns, reads, writes, lat=0.0, sem=None):
@@ -166,7 +178,7 @@ def plan():
         for v in rs:
             rd.setdefault(v[0], []).append((i, v[3], v[4]))
         deps.pop(i, None)
-        ops.append({"eng": eng, "cost": cost, "fns": fns, "deps": deps, "lat": lat, "sem": sem, "lag": cur[0],
+        ops.append({"eng": eng, "cost": cost, "fns": fns, "deps": deps, "lat": lat, "sem": sem, "lag": cur[0], "step": cur[1],
                     "banks": sorted(set(v[0] for v in rs + ws if in_psum(v))), "tag": (ws[0][0] + str(ws[0][3]) if ws else "out")})
         return i
 
@@ -175,7 +187,7 @@ def plan():
             per = PAR["SCAT"]
         elif ins[0][0] == "#":
             per = max(per, PAR["GATH"])
-        return PAR["FIXV" if eng == "dve" else "FIXA"] + max(16, width(out) * per) * CYC
+        return PAR["FIXV" if eng == "dve" else "FIXA"] + max(PAR["MINC"], width(out) * per) * CYC
 
     def ts(out, in0, s1, op0, s2=None, op1=None):
         per = 0.5 if two_bytes(out) and two_bytes(in0) else 1.0
@@ -255,8 +267,11 @@ def plan():
 
     def send(src, dst, sem):
         i = add("pool", PAR["SEND"], [lambda g, T, x: g.remote_dma(ap(T, dst), ap(T, src), T.sem[sem], T.sem.sent, x["pid"], x["rid"], x["mask"])], [src], [])
+        if not any(o.get("send") for o in ops):
+            ops[i]["cost"] += PAR["FIRST"]
         ops[i]["send"] = True
-        j = add("net", 0.0, [], [], [dst], lat=PAR["LAT_NET"], sem=sem)
+        busy = PAR["ROWS"] + PAR["BYTE"] * (2 if two_bytes(dst) else 4) * width(dst)
+        j = add("net", busy, [], [], [dst], lat=PAR["LAT_NET"] - PAR["ROWS"], sem=sem)
         ops[j]["deps"][i] = False
 
     def mat(n):
@@ -278,26 +293,29 @@ def plan():
     load("act", V("t0s"), "t0", "lt0", 2500.0)
     load("act", V("x0s"), "x0", "lx0", 2500.0)
     cur[0] = 0.0
-    load("act", V("hws", 0, 1), "hw", "lhw", 2500.0)
-    load("act", V("dws"), "dw", "ldw", 2500.0)
-    load("act", V("ths", 0, 1), "th", "lth", 2500.0)
-    j = load("sp", V("k0s"), "k0", "lk0", 6800.0)
-    ops[j]["deps"][last] = None
-    j = load("sp", V("ys", 0, P), "y0", "ly0", 7200.0)
-    ops[j]["deps"][j - 1] = None
+    for out, src, lat in ((V("hws", 0, 1), "hw", 6200.0), (V("ths", 0, 1), "th", 6400.0), (V("dws"), "dw", 6600.0),
+                          (V("k0s"), "k0", 7400.0), (V("ys", 0, P), "y0", 7800.0)):
+        if src in FIRST:
+            load("act", out, src, "l" + src, 2500.0)
+            continue
+        j = load("sp", out, src, "l" + src, lat)
+        ops[j]["deps"][last] = None
+        last = j
 
     KC, G16, SC, SCK, CU, RB, PK, G15, KQ, HF, H1, H2C, H3, THC, TA_, TB_, KH, NKH, KL, K15, DF, KA, KB, KD, KE, KF, KG, KI = list(range(21)) + list(range(24, 31))
     iota(V("icol", 0, 1), [[0, 1]], 0, 1)
     iota(V("jd"), [[1, 128]], 0, -1)
     iota(V("grow"), [[16, 8], [0, 16]], 0, 0)
-    iota(V("jrow"), [[1, 144]], 0, 0)
+    iota(V("jrow"), [[1, 144]], -15, 0)
     iota(tile("turn"), [[0, NM // 4], [1, 4]], 0, 0)
     iota(tile("rr"), [[0, NS], [1, 16]], 0, 0)
-    ms(V("rm"), 1.0)
     ms(V("ones"), 1.0)
     ms(V("zr"), 1.0)
+    ms(V("rm"), 1.0)
     sel(V("rm", p1=KX - 1), V("rm", p1=KX - 1), [[1, NM], [0, 16]], OP.is_equal, 0.0, 0, -1)
     for i, (n, c) in enumerate(DIAG.items()):
+        if n in ON_POOL:
+            continue
         if i < ON_DVE:
             ts(mat(n), V("jd"), 0.0, OP.is_equal, c, OP.mult)
         else:
@@ -309,12 +327,8 @@ def plan():
     ts(col(SC), col(KC), -STEP, OP.mult, 15 * STEP, OP.add)
     ts(col(SCK), col(KC), -STEP, OP.mult, 15 * STEP + 60 + 1024, OP.add)
     ts(col(K15), col(KC), 15.0, OP.is_equal)
-    ts(col(KD), col(K15), -16 * BIG, OP.mult, 16 * BIG, OP.add)
-    ts(col(KE), col(K15), 16 * BIG, OP.mult, -16 * BIG, OP.add)
-    ts(col(KF), col(K15), -4.5, OP.mult)
     ts(col(KG), col(K15), -1.0, OP.mult, 1.0, OP.add)
     ts(col(PK), col(KC), 37.0 * 32, OP.mult, 33.0 * M - 2.0 ** 23, OP.add)
-    ts(col(G15), col(G16), 15.0, OP.add)
     ts(col(KQ), col(KC), -0.5, OP.mult, -3.5, OP.add)
     ts(col(KL), col(KC), 1.5, OP.mult, -34.5, OP.add)
     ts(col(KH), col(KC), 0.5, OP.mult)
@@ -322,27 +336,27 @@ def plan():
     ts(col(KA), col(K15), 1031.5, OP.mult, col(NKH), OP.add)
     ts(col(KB), col(K15), -7.5, OP.mult, col(KH), OP.add)
     ts(col(KI), col(K15), 3.5, OP.mult, col(KQ), OP.add)
-    ts(V("selh"), V("jrow"), col(G15), OP.is_equal, -BIG, OP.mult)
-    act_a = "act" in A_ENG
-    if act_a:
-        ts(V("selq"), V("jrow"), col(G15), OP.is_equal, -BIG / 2, OP.mult)
-    ts(col(H1), V("hws", 0, 1), 0.25, OP.mult)
-    ts(col(H2C), V("hws", 0, 1), -0.125, OP.mult)
-    ts(col(H3), V("hws", 0, 1), 2.0 * KS, OP.mult)
+    ts(V("selh"), V("jrow"), col(G16), OP.is_equal, -BIG, OP.mult)
+    cp(col(H1), V("hws", 0, 1))
     for i, (n, c) in enumerate((("O1", 1.0), ("OH", -0.5), ("On2", -2.0), ("OB", BIG), ("nOB", -BIG), ("O2B", 2 * BIG), ("KW", col(KH)),
-                                ("KW0", col(KA)), ("KWL", col(KB)), ("Hp", col(H1)), ("Hn", col(H2C)), ("H2", col(H3)))):
+                                ("KW0", col(KA)), ("KWL", col(KB)))):
         if i < ON_DVE2:
             ts(mat(n), V("grow"), col(G16), OP.is_equal, c, OP.mult)
         else:
             act(mat(n), mat("O1"), AF.Identity, 0.0, c)
-    for n, c in (("D0", KF), ("D15", KD), ("nD15", KE)):
-        ts(mat(n), V("jd"), 0.0, OP.is_equal, col(c), OP.mult)
+    for n, c in (("Hp", 0.25), ("Hn", -0.125), ("H2", 2.0 * KS)):
+        ts(mat(n), mat("O1"), col(H1), OP.mult, c, OP.mult)
+    ts(mat("D0"), mat("I"), col(K15), OP.mult, -4.5, OP.mult)
+    act(mat("D15"), mat("I16B"), AF.Identity, 0.0, col(KG))
+    act(mat("nD15"), mat("D15"), AF.Identity, 0.0, -1.0)
     sel(mat("TRS"), mat("OH"), [[1, 128]], OP.is_gt, 0.0, 0, -1)
     sel(mat("TRI"), mat("TRS"), [[1, 128]], OP.not_equal, 4.0, 0, -1)
     sel(mat("TRV"), mat("On2"), [[-1, 128]], OP.is_gt, 0.0, 0, 1)
-    tt(mat("TRL"), mat("TRI"), mat("TRV"), OP.add)
-    tt(mat("TR0"), mat("TRI"), mat("D0"), OP.add)
+    mms(terms(V("pb0", 0, 128), [(mat("I"), mat("TRI")), (mat("I"), mat("D0"))]) + terms(V("pb0", 128, 256), [(mat("I"), mat("TRI")), (mat("I"), mat("TRV"))]))
+    act(V("mats", mat("TR0")[3], mat("TR0")[3] + 256), V("pb0", 0, 256), AF.Copy)
     iota(tile("w16"), [[16, NM]], 0, 0)
+    for n in ON_POOL:
+        sel(mat(n), mat("I"), [[1, 128]], OP.not_equal, DIAG[n], 0, -1)
     iota(V("cio"), [[1, P]], -256, 0)
     for c in sorted(set(CH.index(n) for n in CH)):
         n, o = CH[c], 3 * C0[c]
@@ -351,41 +365,37 @@ def plan():
         ts(V("kq", o + n, o + 2 * n), V("kq", o + 2 * n, o + 3 * n), col(KI), OP.add)
         ts(V("kq", o + 2 * n, o + 3 * n), tile("turn", n), col(KL), OP.add)
     ts(tile("mk"), tile("rr"), col(KC), OP.not_equal)
-    ts(tile("da"), tile("rr"), col(KC), OP.is_equal, 64 * STEP, OP.mult)
-    ts(tile("db"), tile("rr"), col(KC), OP.is_gt, -STEP, OP.mult)
-    tt(tile("d0"), tile("da"), tile("db"), OP.add)
+    act(tile("d0"), tile("mk"), AF.Identity, 64 * STEP, -65 * STEP)
     ts(V("cols", DF, DF + 4), V("dws"), -32.5, OP.add)
-    ms(V("dt"), 1.0)
     for s in range(ST):
-        ts(V("dt", 2 * NM * s + 1, 2 * NM * (s + 1), 2), V("ones", 0, NM), col(DF + s), OP.mult)
+        act(V("dt", 2 * NM * s, 2 * NM * (s + 1), 2), V("ones", 0, NM), AF.Copy)
+        act(V("dt", 2 * NM * s + 1, 2 * NM * (s + 1), 2), V("ones", 0, NM), AF.Identity, 0.0, col(DF + s))
     ts(col(HF), V("ths", 0, 1), -1.0, OP.mult)
     ts(col(TA_), col(KC), 0.0, OP.is_equal, col(HF), OP.mult)
     ts(col(TB_), col(KC), 1.0, OP.is_equal, -0.5, OP.mult)
-    tt(col(THC), col(TA_), col(TB_), OP.add)
-    ts(tile("tht"), V("ones", 0, NM), col(THC), OP.mult)
+    act(tile("tht"), V("ones", 0, NM), AF.Identity, col(TB_), col(TA_))
     ms(V("hb"), XO)
+    if PAIRS:
+        ms(tile("da"), VB / BIG)
     group(V("pb1", 0, 2), [(mat("Hn"), V("hb", 0, 2))])
     ts(col(CU), V("pb1", 0, 1), col(SC), OP.add)
     ts(col(RB), V("pb1", 0, 1), VB - 2047.0, OP.add)
-    if act_a:
-        for i, e in enumerate(A_ENG):
-            if 32 * i < NM:
-                ms(V("tiles", tile("cm8")[3] + 32 * i, tile("cm8")[3] + min(NM, 32 * i + 32)), -8.0 if e == "act" else 0.0)
     iota(V("dl"), [[1, NM]], 256, 0)
-    ts(tile("dc"), tile("mk"), -4096.0, OP.mult)
+    act(tile("dc"), tile("mk"), AF.Identity, 0.0, -4096.0)
     tt(V("dl"), V("dl"), tile("dc"), OP.add)
     sel(V("zr", p0=0, p1=32), V("zr", p0=0, p1=32), [[1, NS], [0, NM]], OP.is_equal, 0.0, 0, -1)
     sel(V("zr", p0=32, p1=64), V("zr", p0=32, p1=64), [[-16, NS], [1, NM]], OP.is_ge, 0.0, 0, -1)
-    ms(V("ys", P, P + NM), 0.0)
-    ms(V("ks", P, P + NM), 0.0)
-    ms(V("kf", P, P + NM), 0.0)
-    ts(V("kf", 0, P), V("k0s"), 1 / KS, OP.mult)
-    act(V("pb5"), V("kf", 0, P), AF.Sign, (0.5 - M) / KS)
-    tt(V("ks", 0, P), V("pb5"), V("kf", 0, P), OP.max)
+    for j in range(NS):
+        act(V("zp", 8 * j * (j + 1), 8 * (j + 1) * (j + 2), p1=64), V("zr", j * NM, j * NM + 16 * (j + 1), p1=64), AF.Copy)
+    for n in ("ys", "ks", "kf"):
+        act(V(n, P, P + NM), V("ones"), AF.Copy)
     for c in range(NC):
-        ms(V("xt%d" % c), -XO)
-        ms(V("ct%d" % c, p0=0, p1=32), 0.0)
-        for h in range(0, 128, NM):
+        if not ROUND:
+            ms(V("xt%d" % c), XO)
+        act(V("ct%d" % c, p0=0, p1=32), V("jd", p0=0, p1=32), AF.Identity, 0.0, 0.0)
+        if c:
+            act(V("ct%d" % c, p0=32, p1=64), V("ct0", p0=32, p1=64), AF.Copy)
+        for h in range(0, 128 * (c == 0), NM):
             e = min(128, h + NM)
             ts(V("ct%d" % c, h, e, p0=32, p1=64), V("tiles", tile("rr")[3], tile("rr")[3] + e - h, p0=32, p1=64),
                V("cols", KC, KC + 1, p0=32, p1=64), OP.is_equal, 1024.0, OP.mult)
@@ -402,14 +412,14 @@ def plan():
         a, b = M * i // NFIX, M * (i + 1) // NFIX
         ts(V("ft", a, b), V("fr", a, b), 16.0, OP.is_lt, -LOW, OP.mult)
     add("pool", 1000.0, [lambda g, T, x: g.dma_start(T.ft[:, 0:M], T.fr[:, 0:M], accum_op=OP.add, max_dma_last_dim=4096)],
-        [V("fr"), V("ft", 0, M)], [V("ft", 0, M)], lat=6000.0, sem="lfa")
-    add("sp", 60.0, [lambda g, T, x: g.sync.dma_start(T.ft[:, M:2 * M], T.ft[:, 0:M])], [V("ft", 0, M)], [V("ft", M, 2 * M)], lat=4000.0, sem="lfb")
-    add("sp", 60.0, [lambda g, T, x: g.sync.dma_start(T.ft[:, 2 * M:3 * M], T.ft[:, 0:M])], [V("ft", 0, M)], [V("ft", 2 * M, 3 * M)], lat=6000.0, sem="lfc")
+        [V("fr"), V("ft", 0, M)], [V("ft", 0, M)], lat=7000.0, sem="lfa")
+    add("sp", 60.0, [lambda g, T, x: g.sync.dma_start(T.ft[:, M:2 * M], T.ft[:, 0:M])], [V("ft", 0, M)], [V("ft", M, 2 * M)], lat=4000.0 + PAR["SAFE"], sem="lfb")
+    add("sp", 60.0, [lambda g, T, x: g.sync.dma_start(T.ft[:, 2 * M:3 * M], T.ft[:, 0:M])], [V("ft", 0, M)], [V("ft", 2 * M, 3 * M)], lat=5000.0 + PAR["SAFE"], sem="lfc")
 
     def walk(s, c):
         n, c0 = CH[c], C0[c]
         ns = n // 16
-        cur[0] = float(c)
+        cur[0], cur[1] = float(c), s
         al, be, w0, w1 = ["pb%d" % (c * nbk + i) for i in range(4)]
         wide = [w0, w1]
 
@@ -430,74 +440,71 @@ def plan():
         x, xz, hit0 = [V("lx%d" % s, 3 * c0 + i * n, 3 * c0 + (i + 1) * n) for i in range(3)]
         to = V("ot%d" % s, c0, c0 + n)
         one = V("ones", 0, n)
-        sa, pn, pk = N("sa"), R(be, 0), R(be, 1)
+        sa, pn = N("sa"), R(be, 0)
+        pk, ps = (R(be, 1), R(be, 5)) if 6 * n <= 512 else (N("pks"), R(be, 1))
+        pieces, zcut, accb, dedb = LAYOUT[n]
+        accb, dedb = [w0, w1, al][accb], [w0, w1, al][dedb]
         tin = N("tin")
         tA, nM = V("tn", 2 * c0, 2 * c0 + 2 * n, 2), V("tn", 2 * c0 + 1, 2 * c0 + 2 * n, 2)
         if s == 0:
             off = "off"
             ts(N("w1"), N("t0s"), M - 1, OP.bitwise_and)
             cp(N("off"), N("w1"))
-            ts(tin, N("t0s"), float(M), OP.add)
+            ts(tin, N("t0s"), 0.0 if PAIRS else VB, OP.add)
             if c:
                 act(x, N("x0s"), AF.Identity, XO, 16.0)
             act(xz, N("x0s"), AF.Relu, 8192.0, -8192.0)
             win = V("fr")
         else:
             off = "lt%d" % s
-            cp(tin, N(off))
+            if PAIRS:
+                tin = V("lp%d" % s, 2 * c0 + 1, 2 * c0 + 2 * n, 2)
+            else:
+                ts(tin, N(off), VB - M, OP.add)
             win = V("ft")
-        act(sa, tin, AF.Sign, 0.5 - 2 * M)
-        act(N("rb"), tin, AF.Identity, VB - 2047.5)
+        act(sa, tin, AF.Sign, 0.5 - M - (0.0 if PAIRS else VB))
+        act(N("rb"), tin, AF.Identity, M - 2047.5 + (VB if PAIRS else 0.0))
         xq = V(be, 2 * n, 2 * n + 128, p1=n)
         group(xq, [(x, mat("I"))])
-        act(V("xt%d" % c, p1=n), xq, AF.Identity, -XO / 16, 1 / 16)
-        group(pn, [(V("i32s"), tin), (mat("nI"), N("rb")), (mat("Iw"), one)])
+        act(V("xt%d" % c, p1=n), xq, AF.Identity, XO / 16, -1 / 16)
+        group(pn, [(V("i32s"), tin), (mat("nI"), N("rb"))] + ([(mat("IB"), t("da"))] if PAIRS else []))
         act(N("n"), pn, AF.Identity, M / KS, 1 / KS)
         act(nM, pn, AF.Identity, 2.0 * M)
         act(pk, pn, AF.Identity, col(PK), 33.0)
-        sums = []
-        for i, a in enumerate(range(0, n, 32)):
-            b = min(n, a + 32)
-            src = IND(win, V(off, c0 + a, c0 + b))
+        b = 0
+        for size, eng, eng2, bk, at, early in pieces:
+            a, b = b, b + size
             fp, ep, wp = V(fw, 16 * a, 16 * b), V(e16, 16 * a, 16 * b), V(wa, 16 * a, 16 * b)
-            if (G_ENG if s else G0_ENG)[i] == "act":
-                act(fp, src, AF.Copy)
-            else:
-                cp(fp, src)
-            ts(ep, fp, XO - 7.5, OP.add)
-            if s == 0 and c == 0 and i == 0 and FORCE:
-                for j in consts:
-                    ops[-1]["deps"].setdefault(j, None)
-            if s == 0:
-                if Q_ENG[c] == "dve":
-                    ts(V("qw", 16 * (c0 + a), 16 * (c0 + b)), fp, 16.0, OP.is_lt, -2.0, OP.mult)
+            for h in range(a, b, GCUT[c]):
+                h1 = min(b, h + GCUT[c])
+                if eng == "act":
+                    act(V(fw, 16 * h, 16 * h1), IND(win, V(off, c0 + h, c0 + h1)), AF.Copy)
                 else:
-                    act(V("qw", 16 * (c0 + a), 16 * (c0 + b)), fp, AF.Sign, -15.5)
-            z = V(wide[i], 0, 16 * (b - a)) if i < 2 else V(al, 256, 256 + 16 * (b - a))
-            tm = [(V("xt%d" % c, p1=KX), V("rm", 16 * a, 16 * b, p1=KX)), (mat("I"), ep)]
-            if A_ENG[i] == "act":
-                group(z, tm + [(mat("nI"), fp)])
-                act(wp, z, AF.Sign, 0.5)
+                    cp(V(fw, 16 * h, 16 * h1), IND(win, V(off, c0 + h, c0 + h1)))
+            if eng2 == "act" and not ROUND:
+                act(ep, fp, AF.Identity, XO - 7.5)
             else:
-                group(z, tm)
-                tt(wp, z, fp, OP.is_ge)
-        tm = [(mat("I16B"), sa)]
-        if s:
-            tm.append((mat("IB"), hit0))
-        if act_a:
-            tm.append((mat("IB"), t("cm8")))
-        mms([(R(be, 5), l_, r_, i == 0, False) for i, (l_, r_) in enumerate(tm)], opens=True)
-        it, runs = [], []
-        for i, a in enumerate(range(0, n, 32)):
-            if runs and runs[-1][2] == A_ENG[i]:
-                runs[-1][1] = min(n, a + 32)
+                ts(ep, fp, XO - 7.5, OP.add)
+            if s == 0:
+                ts(V("qw", 16 * (c0 + a), 16 * (c0 + b)), fp, 16.0, OP.is_lt, -LOW, OP.mult)
+            z = V([w0, w1, al][bk], at, at + 16 * size)
+            if not ROUND:
+                group(z, [(V("xt%d" % c, p1=KX), V("rm", 16 * a, 16 * b, p1=KX)), (mat("I"), fp)], early)
+                tt(wp, z, ep, OP.is_le)
+                continue
+            group(z, [(V("xt%d" % c, p1=n), V("rm", 16 * a, 16 * b, p1=n)), (mat("I"), fp)], early)
+            if eng2 == "act":
+                act(wp, z, AF.Identity, XO - 8.5)
             else:
-                runs.append([a, min(n, a + 32), A_ENG[i]])
-        for a, b, e in runs:
-            it += [(V(be, 5 * n + a, 5 * n + b), V("selq" if e == "act" else "selh", 15 - k, 143 - k), V(wa, 16 * a + k, 16 * b, 16), False, False) for k in range(16)]
-        it[-1] = it[-1][:4] + (True,)
-        mms(it, closes=True)
-        act(N("cand"), R(be, 5), AF.Sign, -24.5 * BIG, -1.0)
+                ts(wp, z, XO - 8.5, OP.add)
+        tm = [(mat("I16B"), sa)] + ([(mat("IB"), hit0)] if s else [])
+        it = terms(ps, tm + [(V(sl, 15 - k, 143 - k), V(src, k, 16 * n, 16))
+                                   for sl, src in ((("seln", e16), ("selp", wa)) if ROUND else (("selh", wa),)) for k in range(16)])
+        mms(it[:len(tm)], opens=True)
+        if ROUND:
+            mms(it[len(tm):-16])
+        mms(it[-16:], closes=True)
+        act(N("cand"), ps, AF.Sign, -24.5 * BIG, -1.0)
         f3 = [V("f3", 3 * c0 + i * n, 3 * c0 + (i + 1) * n) for i in range(3)]
         mms([(R(w0, 0, 3), mat("I"), V("kq", 3 * C0[CH.index(n)], 3 * C0[CH.index(n)] + 3 * n), True, False)], opens=True)
         mms([(R(w0, 0), mat("TRI"), N("cand"), False, False), (R(w0, 1), mat("TR0"), N("cand"), False, False),
@@ -507,15 +514,23 @@ def plan():
         scan(N("sv1"), t("d0"), R(w1, 0))
         ko, co, lo = V("so", 32 * c, 32 * c + ns), V("so", 32 * c + 8, 32 * c + 8 + ns), V("so", 32 * c + 16, 32 * c + 16 + ns)
         ts(ko, S("sv1"), col(SCK), OP.add, float(16 * n), OP.min)
+        if s == 0 and c == 0:
+            j = len(ops) - 1 - KLATE
+            for h in range(0, P, 192):
+                e = min(P, h + 192)
+                ts(V("kf", h, e), V("k0s", h, e), 1 / KS, OP.mult)
+                ops[-1]["deps"].setdefault(j, None)
+                act(V(al, 320, 320 + e - h), V("kf", h, e), AF.Sign, (0.5 - M) / KS)
+                tt(V("ks", h, e), V(al, 320, 320 + e - h), V("kf", h, e), OP.max)
         tt(N("mx"), IND(V(e16), ko), x, OP.max)
         act(N("e"), IND(V(e16), ko), AF.Relu, -XO)
         act(N("bz"), IND(V(e16), ko), AF.Relu, 512 * (XO + 16), -512.0)
         pu, pp, px = R(be, 4), R(al, 0), R(w1, 1)
         group(pu, [(mat("Hn"), x), (mat("Hp"), N("mx")), (mat("Hn"), N("e"))], 1)
         group(pp, [(mat("I240"), one), (mat("I17"), x), (mat("I"), xz), (mat("nI16"), N("mx")), (mat("I"), N("bz"))], 3)
-        group(px, [(mat("nI"), x), (mat("I2"), N("mx")), (mat("nI"), N("e"))], 1)
+        group(px, [(mat("I"), x), (mat("nI"), N("e"))], 1)
         tt(N("tq"), pp, N("mx"), OP.max)
-        act(N("xp"), px, AF.Identity, -XO / 16, 1 / 16)
+        act(N("xp"), px, AF.Abs, -XO / 16, 1 / 16)
         if s < ST - 1:
             act(xo, N("xp"), AF.Identity, XO, 16.0)
             act(zo, N("xp"), AF.Relu, 8192.0, -8192.0)
@@ -541,17 +556,18 @@ def plan():
         tt(N("kp"), ph, N("kc"), OP.max)
         ts(ho, ph, 0.0, OP.is_lt)
         if s < ST - 1:
-            send(V("ox%d" % s, 3 * c0, 3 * c0 + 3 * n), V("lx%d" % (s + 1), 3 * c0, 3 * c0 + 3 * n), "ax%d_%d" % (s + 1, c))
+            k = 2 if APART else 3
+            send(V("ox%d" % s, 3 * c0, 3 * c0 + k * n), V("lx%d" % (s + 1), 3 * c0, 3 * c0 + k * n), "ax%d_%d" % (s + 1, c))
+            if APART:
+                send(ho, V("lx%d" % (s + 1), 3 * c0 + 2 * n, 3 * c0 + 3 * n), "ah%d_%d" % (s + 1, c))
         act(N("gs"), N("kp"), AF.Sign, 0.5)
         tt(N("he"), pn, N("kp"), OP.is_equal)
         tt(tA, N("kp"), N("new"), OP.min)
-        cuts, npc = CUTS, len(CUTS) - 1
-        pboth, pacc = V(w0, 512 - 2 * n, 512), V(w0, 513 - 2 * n, 512, 2)
-        for i in range(npc):
-            ka, kb = cuts[i], cuts[i + 1]
-            zb = (wide + [al])[i]
+        pboth, pacc = V(accb, 512 - 2 * n, 512), V(accb, 513 - 2 * n, 512, 2)
+        for i, (ka, kb, zb) in enumerate(zcut):
+            zb = [w0, w1, al][zb]
             zk = [V(zb, (k - ka) * n, (k - ka + 1) * n) for k in range(ka, kb)]
-            src = [[(mat("I"), V(e16, k, 16 * n, 16))] + ([(mat("I120"), V("qw", 16 * c0 + k, 16 * (c0 + n), 16))] if s == 0 else [])
+            src = [[(mat("I"), V(e16, k, 16 * n, 16))] + ([(mat("I"), V("qw", 16 * c0 + k, 16 * (c0 + n), 16))] if s == 0 else [])
                    for k in range(ka, kb)]
             if i < FRESH:
                 it = [(zk[k], l_, v, False, False) for k in range(kb - ka) for l_, v in src[k]]
@@ -559,41 +575,44 @@ def plan():
                 mms([(zk[k - ka], mat("nI"), N("tq"), False, k == kb - 1) for k in range(ka, kb)], closes=True)
             else:
                 mms([m_ for k in range(kb - ka) for m_ in terms(zk[k], src[k] + [(mat("nI"), N("tq"))])])
-            act(V(wa, ka * n, kb * n), V(zb, 0, (kb - ka) * n), AF.Gelu, -FOLD * LOW / 2 if s == 0 and Q_ENG[c] == "act" else 0.0, FOLD)
+            act(V(wa, ka * n, kb * n), V(zb, 0, (kb - ka) * n), AF.Gelu, 0.0, FOLD)
             ts(V(wq, ka * n, kb * n), V(wa, ka * n, kb * n), MAGIC, OP.add, MAGIC, OP.not_equal)
-        for i in range(npc):
+        for i, (ka, kb, zb) in enumerate(zcut):
             it = []
             if i == 0:
                 it = [(pboth, mat("IB"), V("dt", 2 * NM * s, 2 * NM * s + 2 * n), True, False)]
                 it += [(pacc, l_, r_, False, False) for l_, r_ in [(mat("I16B"), sa), (mat("D15"), f3[1]), (mat("nD15"), f3[2])]]
-            it += [(pacc, V("selh", 15 - k, 143 - k), V(wq, k * n, (k + 1) * n), False, False) for k in range(cuts[i], cuts[i + 1])]
+            it += [(pacc, V("selh", 15 - k, 143 - k), V(wq, k * n, (k + 1) * n), False, False) for k in range(ka, kb)]
             mms(it, opens=(i == 0))
         mms([(pacc, mat("I16B"), N("gs"), False, False), (pacc, mat("I32B"), N("he"), False, True)], closes=True)
-        scan(V("t2", 2 * c0, 2 * c0 + 2 * n), pboth, V("tn", 2 * c0, 2 * c0 + 2 * n), OP.max)
-        tf = V("t2", 2 * c0 + 1, 2 * c0 + 2 * n, 2)
+        scan(V("op%d" % s, 2 * c0, 2 * c0 + 2 * n), pboth, V("tn", 2 * c0, 2 * c0 + 2 * n), OP.max)
+        tf = V("op%d" % s, 2 * c0 + 1, 2 * c0 + 2 * n, 2)
         if s < ST - 1:
             ts(to, tf, float(M), OP.add)
             send(to, V("lt%d" % (s + 1), c0, c0 + n), "at%d_%d" % (s + 1, c))
+            if PAIRS:
+                send(V("op%d" % s, 2 * c0, 2 * c0 + 2 * n), V("lp%d" % (s + 1), 2 * c0, 2 * c0 + 2 * n), "ap%d_%d" % (s + 1, c))
         else:
-            act(N("s2"), tf, AF.Sign, 0.5)
-            group(pv, [(V("i32s"), tf), (mat("nI2k"), N("s2"))])
-            act(N("tout"), pv, AF.Identity, 2048.0)
+            ts(N("s2"), tf, 0.0, OP.is_lt, float(M), OP.mult)
+            tt(N("tout"), tf, N("s2"), OP.add)
             store("sp", "yt", c0, c0 + n, N("tout"), "oyt%d" % c)
         tt(N("hd"), pd, ho, OP.mult)
-        group(R(be, 5), [(mat("I8k"), ho), (mat("I4k"), N("gs"))])
-        tt(N("zc"), R(be, 5), tf, OP.is_gt)
+        group(ps, [(mat("I8k"), ho), (mat("I4k"), N("gs"))])
+        tt(N("zc"), ps, tf, OP.is_gt)
         if s == ST - 1:
             act(N("n"), pn, AF.Identity, float(M))
-            ts(N("zc"), N("zc"), float(M), OP.mult)
+            act(N("zc"), N("zc"), AF.Identity, 0.0, float(M))
         cd, ct, eq = V("cd%d" % c, 0, ns), "ct%d" % c, "eq%d" % c
         ts(cd, c2, -256.0, OP.add)
+        w1 = dedb
         pt = V(w1, 0, 128, p1=ns)
         group(pt, [(cd, mat("I"))])
         act(V(ct, p1=ns), pt, AF.Identity, 0.0, -1.0)
-        o, it = 0, []
+        o = 8 * ns * (ns + 1)
+        it, o = [(V(w1, 128, 128 + o), V(ct, p1=48), V("zp", 0, o, p1=48), True, False)], 0
         for j in range(ns):
             wd = 16 * (j + 1)
-            it += terms(V(w1, 128 + o, 128 + o + wd), [(V(ct, p1=48), V("zr", j * NM, j * NM + wd, p1=48)), (mat("I"), V("c3", c0, c0 + wd))])
+            it.append((V(w1, 128 + o, 128 + o + wd), mat("I"), V("c3", c0, c0 + wd), False, j == ns - 1))
             o += wd
         mms(it)
         ts(V(eq, 0, o), V(w1, 128, 128 + o), 0.0, OP.is_equal, 1 / 16, OP.mult)
@@ -704,9 +723,11 @@ def schedule(ops):
             seq = by_key([cost[i] - best[1][i] + JIT * rnd() for i in range(n)])
         found.append(best)
     span, end = min(found, key=lambda b: b[0])
+    soon = [0.0] * n
     for i in range(n):
+        soon[i] = max([0.0] + [soon[j] + cost[j] + gp for j, gp in pred[i]])
         ops[i]["at"] = end[i] - cost[i]
-    return sorted(range(n), key=lambda i: (ops[i]["at"], i)), span
+    return sorted(range(n), key=lambda i: (0, soon[i], i) if soon[i] < SOON else (1, ops[i]["at"], i)), span
 
 
 def improve(ops, seq):
@@ -719,20 +740,40 @@ def improve(ops, seq):
         for j in pred[i]:
             succ[j].append(i)
     cases = []
-    for pace, wake in CASES:
-        cost = [o["cost"] * (pace if o["eng"] in ("pe", "dve", "act") and not o["sem"] else 1.0)
+    for pace, pe, wake in CASES:
+        cost = [o["cost"] * (pe if o["eng"] == "pe" else pace if o["eng"] in ("dve", "act", "pool") and not o["sem"] and not o.get("send") else 1.0)
                 + (wake if o["eng"] == "pool" and not o.get("send") else 0.0) for o in ops]
         gaps = [[(j, ops[j]["lat"] + wake if s else 0.0) for j, s in o["deps"].items()] for o in ops]
         cases.append((cost, gaps, [o["lat"] + wake for o in ops]))
     tail = [o["lat"] for o in ops]
 
-    def run(seq, case):
+    ends = [i for i in range(n) if not succ[i]]
+    sent = set(i for i in range(n) if ops[i].get("send"))
+    role, who = [], {}
+    for i, o in enumerate(ops):
+        tag = o["tag"][:2] + o["tag"][3:] if o["tag"][:2] in ("ox", "ot", "lx", "lt", "op", "lp") else o["tag"]
+        k = 0
+        while (o["step"], o["lag"], o["eng"], tag, k) in who:
+            k += 1
+        role.append((o["step"], o["lag"], o["eng"], tag, k))
+        who[role[-1]] = i
+
+    def run(seq, case, old, p0):
         cost, gaps, hop = case
-        end, via, free, last = [0.0] * n, [-1] * n, {}, {}
-        for i in seq:
+        end, via, free, last = (list(old[1]), list(old[2]), {}, {}) if old else ([0.0] * n, [-1] * n, {}, {})
+        for i in seq[max(0, p0 - 400):p0]:
+            if eng[i] != "net":
+                free[eng[i]] = i
+            if i in sent:
+                free["net"] = i + 1
+            for bk in banks[i]:
+                last[bk] = i
+        for i in seq[p0:]:
             e = eng[i]
+            if e == "net":
+                continue
             v = free.get(e, -1)
-            st = end[v] if v >= 0 and e != "net" else 0.0
+            st = end[v] if v >= 0 else 0.0
             for j, gp in gaps[i]:
                 if end[j] + gp > st:
                     st, v = end[j] + gp, j
@@ -742,7 +783,11 @@ def improve(ops, seq):
                     st, v = end[j] + hop[j], j
                 last[bk] = i
             end[i], via[i], free[e] = st + cost[i], v, i
-        k = max(range(n), key=lambda i: end[i] + tail[i])
+            if i in sent:
+                j = free.get("net", -1)
+                late = j >= 0 and end[j] > end[i]
+                end[i + 1], via[i + 1], free["net"] = (end[j] if late else end[i]) + cost[i + 1], (j - 1 if late else i), i + 1
+        k = max(ends, key=lambda i: end[i] + tail[i])
         return end[k] + tail[k], end, via, k
 
     z = [SEED]
@@ -751,44 +796,56 @@ def improve(ops, seq):
         z[0] = (z[0] * 1103515245 + 12345) % 2147483648
         return z[0] / 2147483648
 
-    def judge(seq):
-        r = [run(seq, c) for c in cases]
+    def judge(seq, old, p0):
+        r = [run(seq, c, o, p0) for c, o in zip(cases, old)]
         return sum(x[0] for x in r) / len(r), r
 
-    cur, runs = judge(seq)
+    cur, runs = judge(seq, [None] * len(cases), 0)
     best = (cur, seq, runs)
     for it in range(MOVES):
         span, end, via, k = runs[int(rnd() * len(runs))]
         pairs = []
         while via[k] >= 0:
             if via[k] not in ops[k]["deps"]:
-                pairs.append((via[k], k))
+                pairs.append((via[k], k - 1 if eng[k] == "net" else k))
             k = via[k]
         if not pairs:
             break
         a, b = pairs[int(rnd() * len(pairs))]
-        pa, pb = seq.index(a), seq.index(b)
-        if rnd() < 0.5:
-            if rnd() < 0.3:
-                pa = max(0, pa - int(12 * rnd()))
-            win, take = seq[pa:pb + 1], {b}
-            for x in reversed(win):
-                if x in take:
-                    take.update(pred[x])
-            if a in take:
+        ahead, more = rnd() < 0.5, int(12 * rnd()) if rnd() < 0.3 else 0
+        todo = [(a, b)]
+        if rnd() < TWIN:
+            for d in range(1 - ST, ST):
+                a2, b2 = who.get((role[a][0] + d,) + role[a][1:]), who.get((role[b][0] + d,) + role[b][1:])
+                if d and a2 is not None and b2 is not None:
+                    todo.append((a2, b2))
+        new, p0 = seq, n
+        for a, b in todo:
+            pa, pb = new.index(a), new.index(b)
+            if pa > pb:
                 continue
-            new = seq[:pa] + [x for x in win if x in take] + [x for x in win if x not in take] + seq[pb + 1:]
-        else:
-            if rnd() < 0.3:
-                pb = min(n - 1, pb + int(12 * rnd()))
-            win, take = seq[pa:pb + 1], {a}
-            for x in win:
-                if x in take:
-                    take.update(succ[x])
-            if b in take:
-                continue
-            new = seq[:pa] + [x for x in win if x not in take] + [x for x in win if x in take] + seq[pb + 1:]
-        val, r = judge(new)
+            if ahead:
+                pa = max(0, pa - more)
+                win, take = new[pa:pb + 1], {b}
+                for x in reversed(win):
+                    if x in take:
+                        take.update(pred[x])
+                if a in take:
+                    continue
+                new = new[:pa] + [x for x in win if x in take] + [x for x in win if x not in take] + new[pb + 1:]
+            else:
+                pb = min(n - 1, pb + more)
+                win, take = new[pa:pb + 1], {a}
+                for x in win:
+                    if x in take:
+                        take.update(succ[x])
+                if b in take:
+                    continue
+                new = new[:pa] + [x for x in win if x not in take] + [x for x in win if x in take] + new[pb + 1:]
+            p0 = min(p0, pa)
+        if p0 == n:
+            continue
+        val, r = judge(new, runs, p0)
         if val <= cur + TEMP * rnd() * (1 - it / MOVES):
             seq, cur, runs = new, val, r
             if val < best[0]:

from concourse.mybir import AluOpType as OP, ActivationFunctionType as AF

M, P, W, ST = 4096, 512, 160, 4
CH = [80, 80]
ROUND = False
TWIN = 0.1
ON_POOL = ["Iv", "nIr", "I32B", "I8k", "I4k"]
KLATE = 10
SOON = 0.0
GCUT = [32, 32]
LAYOUT = {
    80: ([(32, "act", "dve", 0, 0, 1), (32, "act", "dve", 1, 0, 1), (16, "act", "dve", 2, 256, 1)], [(0, 6, 0), (6, 12, 2), (12, 16, 1)], 0, 2),
    96: ([(32, "dve", "act", 0, 0, 1), (32, "act", "dve", 1, 0, 1), (32, "act", "dve", 2, 0, 1)], [(0, 5, 0), (5, 9, 1), (9, 13, 2), (13, 16, 0)], 1, 2),
    64: ([(32, "dve", "act", 0, 0, 1), (32, "act", "dve", 1, 0, 1)], [(0, 6, 0), (6, 12, 1), (12, 16, 2)], 0, 1),
}
NLOAD, NFIX = 4, 8
Q_ENG = ["dve", "dve"]
FIRST = ["hw", "th", "dw"]
PAIRS = False
APART = True
NPOOL = 11
LATE = ["mats3840", "mats4096", "dl0", "kf0", "ks0"]
LAGS = [2000.0, 2500.0]
ROUNDS = 4
MOVES, TEMP = 33000, 70.0
CASES = [(1.0, 1.0, 160.0), (1.25, 1.4, 200.0)]
SEED = 2
JIT = 150.0
BIG = 16384.0
STEP = 131072.0
XO = 2320.0
LOW = 240.0
FOLD = 0.192 / 16
MAGIC = 1.5 * 2 ** 17
VB = 786432.0
KS = 4.0 * M
NC = len(CH)
C0 = [sum(CH[:i]) for i in range(NC)]
NM = max(CH)
NS = NM // 16
KX = 97
DIAG = {"I": 1.0, "nI": -1.0, "I17": 17.0, "nI16": -16.0, "IB": BIG, "I16B": 16 * BIG, "I32B": 32 * BIG,
        "I8k": 2.0 * M, "I4k": 1.0 * M, "I240": LOW, "Iv": VB * KS, "nIr": -KS}
MATS = list(DIAG) + ["O1", "OH", "On2", "OB", "nOB", "O2B", "KW", "KW0", "KWL", "Hp", "Hn", "H2", "TRI", "TRS", "TRV", "TR0", "TRL", "D0", "D15", "nD15"]
NB16 = ["sa", "cand", "mx", "e", "bz", "tq", "xp", "r", "my", "yg", "gs", "he", "hd", "c3", "x0s", "rb", "s2"]
NF32 = ["n", "sv1", "sv2", "sv3", "kc", "kp", "prod", "zc", "tin", "tout", "pks"]
NI32 = ["w1", "sm", "new", "t0s"]
TILES = ["turn", "w16", "d0", "tht", "mk", "rr", "da", "db", "dc", "cm8"]
CUTS = [0, 6, 12, 16]
FRESH = 2
ON_DVE2 = 3
ON_DVE = 3

SCRATCH = {
    "fr": ("sbuf", [128, M], "bfloat16"), "qw": ("sbuf", [128, 16 * W], "bfloat16"), "ft": ("sbuf", [128, 3 * M], "bfloat16"),
    "kf": ("sbuf", [128, P + NM], "float32"),
    "ys": ("sbuf", [128, P + NM], "bfloat16"), "ks": ("sbuf", [128, P + NM], "float32"), "k0s": ("sbuf", [128, P], "int32"),
    "mats": ("sbuf", [128, 128 * len(MATS)], "bfloat16"), "i32s": ("sbuf", [128, 128], "float32"),
    "selh": ("sbuf", [128, 144], "bfloat16"), "seln": ("sbuf", [128, 144], "bfloat16"), "selp": ("sbuf", [128, 144], "bfloat16"),
    "jrow": ("sbuf", [128, 144], "bfloat16"), "grow": ("sbuf", [128, 128], "bfloat16"),
    "jd": ("sbuf", [128, 128], "bfloat16"), "cio": ("sbuf", [128, P], "bfloat16"),
    "rm": ("sbuf", [128, 16 * NM], "bfloat16"), "zp": ("sbuf", [128, 8 * NS * (NS + 1)], "bfloat16"),
    "ones": ("sbuf", [128, NM], "bfloat16"), "zr": ("sbuf", [128, NS * NM], "bfloat16"),
    "tiles": ("sbuf", [128, NM * len(TILES)], "bfloat16"), "dl": ("sbuf", [128, NM], "float32"),
    "cols": ("sbuf", [128, 32], "float32"), "icol": ("sbuf", [128, 8], "int32"), "hb": ("sbuf", [128, 8], "bfloat16"),
    "dws": ("sbuf", [128, 4], "int32"), "hws": ("sbuf", [128, 4], "int32"), "ths": ("sbuf", [128, 4], "int32"),
    "off": ("sbuf", [128, W], "uint16"), "so": ("sbuf", [128, 32 * NC], "uint16"), "ci": ("sbuf", [128, 16 * NC], "int32"),
    "tn": ("sbuf", [128, 2 * W], "float32"), "dt": ("sbuf", [128, 2 * NM * ST], "bfloat16"),
    "f3": ("sbuf", [128, 3 * W], "bfloat16"), "kq": ("sbuf", [128, 3 * W], "bfloat16"),
}
for _n in NB16:
    SCRATCH[_n] = ("sbuf", [128, W], "bfloat16")
for _n in NF32:
    SCRATCH[_n] = ("sbuf", [128, W], "float32")
for _n in NI32:
    SCRATCH[_n] = ("sbuf", [128, W], "int32")
for _c in range(NC):
    SCRATCH["fw%d" % _c] = ("sbuf", [128, 16 * CH[_c]], "bfloat16")
    SCRATCH["e16_%d" % _c] = ("sbuf", [128, 16 * CH[_c] + 16], "bfloat16")
    SCRATCH["wa%d" % _c] = ("sbuf", [128, 16 * CH[_c]], "bfloat16")
    SCRATCH["wq%d" % _c] = ("sbuf", [128, 16 * CH[_c]], "bfloat16")
    SCRATCH["xt%d" % _c] = ("sbuf", [128, 128], "bfloat16")
    SCRATCH["ct%d" % _c] = ("sbuf", [128, 128], "bfloat16")
    SCRATCH["cd%d" % _c] = ("sbuf", [128, 8], "bfloat16")
    SCRATCH["eq%d" % _c] = ("sbuf", [128, 8 * NS * (NS + 1)], "bfloat16")
for _s in range(ST):
    SCRATCH["ox%d" % _s] = ("sbuf", [128, 3 * W], "bfloat16")
    SCRATCH["ot%d" % _s] = ("sbuf", [128, W], "uint16")
    SCRATCH["op%d" % _s] = ("sbuf", [128, 2 * W], "float32")
    SCRATCH["lp%d" % _s] = ("sbuf", [128, 2 * W], "float32")
    SCRATCH["lx%d" % _s] = ("sbuf", [128, 3 * W], "bfloat16")
    if _s:
        SCRATCH["lt%d" % _s] = ("sbuf", [128, W], "uint16")
for _b in range(8):
    SCRATCH["pb%d" % _b] = ("psum", [128, 512], "float32")

LOADS = ["f%d" % _i for _i in range(NLOAD)] + ["fa", "fb", "fc", "t0", "x0", "y0", "k0", "dw", "hw", "th"]
SEMAPHORES = ["pe", "dve", "act", "pool", "sent"] + ["l" + s for s in LOADS] + ["oyy", "oyk"]
for _c in range(NC):
    SEMAPHORES += ["oyx%d" % _c, "oyt%d" % _c]
    for _s in range(1, ST):
        SEMAPHORES += ["ax%d_%d" % (_s, _c), "at%d_%d" % (_s, _c)] + (["ah%d_%d" % (_s, _c)] if APART else []) + (["ap%d_%d" % (_s, _c)] if PAIRS else [])

PAR = {"CYC": 0.83, "PCYC": 0.42, "FIXV": 35.0, "FIXA": 45.0, "FIXP": 0.0, "GATH": 1.6, "SCAT": 3.8,
       "LAT_X": 200.0, "LAT_S": 200.0, "LAT_B": 230.0, "LAT_NET": 2500.0, "SEND": 500.0, "ROWS": 800.0, "BYTE": 0.8, "SAFE": 500.0, "FIRST": 2500.0, "MINC": 40}


def V(name, c0=0, c1=None, step=1, p0=0, p1=128):
    if c1 is None:
        c1 = SCRATCH[name][1][1]
    return (name, p0, p1, c0, c1, step)


def IND(win, off):
    return ("#", win, off)


def width(v):
    if v[0] == "#":
        return 16 * width(v[2])
    return len(range(v[3], v[4], v[5]))


def two_bytes(v):
    return SCRATCH[v[1][0] if v[0] == "#" else v[0]][2] in ("bfloat16", "uint16")


def in_psum(v):
    return v[0] != "#" and SCRATCH[v[0]][0] == "psum"


def ap(T, v):
    if not isinstance(v, tuple):
        return v
    if v[0] == "#":
        return ap(T, v[1]).indirect(ap(T, v[2]))
    if v[5] == 1:
        return T[v[0]][v[1]:v[2], v[3]:v[4]]
    return T[v[0]][v[1]:v[2], v[3]:v[4]:v[5]]


def plan():
    ops = []
    wr, rd, pe_in, shut = {}, {}, {}, {}
    cur = [0.0, -9]
    CYC, PCYC = PAR["CYC"], PAR["PCYC"]

    def add(eng, cost, fns, reads, writes, lat=0.0, sem=None):
        i = len(ops)
        deps = {}

        def dep(j, sync):
            deps[j] = deps.get(j, False) or sync or ops[j]["sem"] is not None or ops[j]["eng"] != eng

        rs, ws = [], []
        for v in reads:
            if isinstance(v, tuple):
                rs += [v[1], v[2]] if v[0] == "#" else [v]
        for v in writes:
            if v[0] == "#":
                ws.append(v[1])
                rs.append(v[2])
            else:
                ws.append(v)
        for v in rs:
            for (j, a, b) in wr.get(v[0], []):
                if a < v[4] and v[3] < b:
                    dep(j, True)
        for v in ws:
            for (j, a, b) in wr.get(v[0], []) + rd.get(v[0], []):
                if a < v[4] and v[3] < b:
                    dep(j, not in_psum(v))
        for v in ws:
            full = v[1] == 0 and v[2] == 128 and v[5] == 1
            wr[v[0]] = [e for e in wr.get(v[0], []) if not (full and v[3] <= e[1] and e[2] <= v[4])] + [(i, v[3], v[4])]
            if full:
                rd[v[0]] = [e for e in rd.get(v[0], []) if not (v[3] <= e[1] and e[2] <= v[4])]
        for v in rs:
            rd.setdefault(v[0], []).append((i, v[3], v[4]))
        deps.pop(i, None)
        ops.append({"eng": eng, "cost": cost, "fns": fns, "deps": deps, "lat": lat, "sem": sem, "lag": cur[0], "step": cur[1],
                    "banks": sorted(set(v[0] for v in rs + ws if in_psum(v))), "tag": (ws[0][0] + str(ws[0][3]) if ws else "out")})
        return i

    def ecost(eng, out, ins, per):
        if out[0] == "#":
            per = PAR["SCAT"]
        elif ins[0][0] == "#":
            per = max(per, PAR["GATH"])
        return PAR["FIXV" if eng == "dve" else "FIXA"] + max(PAR["MINC"], width(out) * per) * CYC

    def ts(out, in0, s1, op0, s2=None, op1=None):
        per = 0.5 if two_bytes(out) and two_bytes(in0) else 1.0
        if op1 is None:
            fn = lambda g, T, x: g.vector.tensor_scalar(ap(T, out), ap(T, in0), ap(T, s1), None, op0)
        else:
            fn = lambda g, T, x: g.vector.tensor_scalar(ap(T, out), ap(T, in0), ap(T, s1), ap(T, s2), op0, op1)
        add("dve", ecost("dve", out, [in0], per), [fn], [in0, s1, s2], [out])

    def tt(out, in0, in1, op):
        per = 1.0 if in_psum(in0) or in_psum(in1) else 2.0
        add("dve", ecost("dve", out, [in0], per), [lambda g, T, x: g.vector.tensor_tensor(ap(T, out), ap(T, in0), ap(T, in1), op)], [in0, in1], [out])

    def cp(out, in0):
        per = 0.5 if two_bytes(out) and two_bytes(in0) else 1.0
        add("dve", ecost("dve", out, [in0], per), [lambda g, T, x: g.vector.tensor_copy(ap(T, out), ap(T, in0))], [in0], [out])

    def ms(out, val):
        add("dve", ecost("dve", out, [out], 0.5 if two_bytes(out) else 1.0), [lambda g, T, x: g.vector.memset(ap(T, out), val)], [], [out])

    def scan(out, d0, d1, op0=OP.add):
        add("dve", ecost("dve", out, [d1], 1.0),
            [lambda g, T, x: g.vector.tensor_tensor_scan(ap(T, out), ap(T, d0), ap(T, d1), 0.0, op0, OP.min)], [d0, d1], [out])

    def act(out, in0, func, bias=0.0, scale=1.0):
        if func == AF.Copy:
            fn = lambda g, T, x: g.scalar.activation(ap(T, out), ap(T, in0), func)
        else:
            fn = lambda g, T, x: g.scalar.activation(ap(T, out), ap(T, in0), func, bias=ap(T, bias), scale=ap(T, scale))
        return add("act", ecost("act", out, [in0], 1.0), [fn], [in0, bias, scale], [out])

    def mms(items, opens=False, closes=False):
        fns, c = [], 0.0
        for (out, lhs, rhs, a, b) in items:
            c += PAR["FIXP"] + max(min(64, width(lhs)), width(rhs)) * PCYC * (1 if two_bytes(rhs) else 4)
            fns.append(lambda g, T, x, out=out, lhs=lhs, rhs=rhs, a=a, b=b: g.tensor.matmul(ap(T, out), ap(T, lhs), ap(T, rhs), a, b))
        i = add("pe", c, fns, [v for it in items for v in it[1:3]], [it[0] for it in items], lat=60.0)
        bk = items[0][0][0]
        if opens:
            for j in pe_in.get(bk, []):
                ops[i]["deps"].setdefault(j, False)
        if bk in shut:
            ops[i]["deps"].setdefault(shut[bk], False)
        if closes:
            shut[bk] = i
            pe_in[bk] = []
        pe_in.setdefault(bk, []).append(i)
        return i

    def terms(out, ts_):
        return [(out, lhs, rhs, i == 0, i == len(ts_) - 1) for i, (lhs, rhs) in enumerate(ts_)]

    def group(out, ts_, early=0):
        it = terms(out, ts_)
        if early:
            mms(it[:early], opens=True)
        mms(it[early:], closes=early > 0)

    def iota(out, pattern, base, ch):
        if SCRATCH[out[0]][2] == "int32":
            fn = lambda g, T, x: g.iota(ap(T, out), pattern, base, ch)
        else:
            fn = lambda g, T, x: g.iota(ap(T, out), pattern, base, ch, allow_small_or_imprecise_dtypes=True)
        add("pool", 130 + 2 * width(out) * CYC, [fn], [], [out])

    def sel(out, in0, pattern, cmp, fill, base, ch):
        add("pool", 170 + 2 * width(out) * CYC, [lambda g, T, x: g.affine_select(ap(T, out), ap(T, in0), pattern, cmp, fill, base, ch)], [in0], [out])

    def queue(g, q):
        return g.sync if q == "sp" else g.scalar

    def load(q, out, src, sem, lat, c0=None, c1=None):
        return add(q, 60.0, [lambda g, T, x: queue(g, q).dma_start(ap(T, out), T[src][:] if c0 is None else T[src][:, c0:c1])], [], [out], lat=lat, sem=sem)

    def store(q, dst, c0, c1, src, sem):
        add(q, 60.0, [lambda g, T, x: queue(g, q).dma_start(T[dst][:, c0:c1], ap(T, src))], [src], [], lat=2000.0, sem=sem)

    def send(src, dst, sem):
        i = add("pool", PAR["SEND"], [lambda g, T, x: g.remote_dma(ap(T, dst), ap(T, src), T.sem[sem], T.sem.sent, x["pid"], x["rid"], x["mask"])], [src], [])
        if not any(o.get("send") for o in ops):
            ops[i]["cost"] += PAR["FIRST"]
        ops[i]["send"] = True
        busy = PAR["ROWS"] + PAR["BYTE"] * (2 if two_bytes(dst) else 4) * width(dst)
        j = add("net", busy, [], [], [dst], lat=PAR["LAT_NET"] - PAR["ROWS"], sem=sem)
        ops[j]["deps"][i] = False

    def mat(n):
        return V("mats", 128 * MATS.index(n), 128 * MATS.index(n) + 128)

    def tile(n, w=NM):
        return V("tiles", NM * TILES.index(n), NM * TILES.index(n) + w)

    def col(i):
        return V("cols", i, i + 1)

    cur[0] = -1e3
    for i in range(NLOAD):
        a, b = M * i // NLOAD, M * (i + 1) // NLOAD
        j = load("sp", V("fr", a, b), "fx", "lf%d" % i, 2500.0 + 3500.0 * (i + 1) / NLOAD, a, b)
        if i:
            ops[j]["deps"][j - 1] = None
    last = len(ops) - 1
    load("act", V("t0s"), "t0", "lt0", 2500.0)
    load("act", V("x0s"), "x0", "lx0", 2500.0)
    cur[0] = 0.0
    for out, src, lat in ((V("hws", 0, 1), "hw", 6200.0), (V("ths", 0, 1), "th", 6400.0), (V("dws"), "dw", 6600.0),
                          (V("k0s"), "k0", 7400.0), (V("ys", 0, P), "y0", 7800.0)):
        if src in FIRST:
            load("act", out, src, "l" + src, 2500.0)
            continue
        j = load("sp", out, src, "l" + src, lat)
        ops[j]["deps"][last] = None
        last = j

    KC, G16, SC, SCK, CU, RB, PK, G15, KQ, HF, H1, H2C, H3, THC, TA_, TB_, KH, NKH, KL, K15, DF, KA, KB, KD, KE, KF, KG, KI = list(range(21)) + list(range(24, 31))
    iota(V("icol", 0, 1), [[0, 1]], 0, 1)
    iota(V("jd"), [[1, 128]], 0, -1)
    iota(V("grow"), [[16, 8], [0, 16]], 0, 0)
    iota(V("jrow"), [[1, 144]], -15, 0)
    iota(tile("turn"), [[0, NM // 4], [1, 4]], 0, 0)
    iota(tile("rr"), [[0, NS], [1, 16]], 0, 0)
    ms(V("ones"), 1.0)
    ms(V("zr"), 1.0)
    ms(V("rm"), 1.0)
    sel(V("rm", p1=KX - 1), V("rm", p1=KX - 1), [[1, NM], [0, 16]], OP.is_equal, 0.0, 0, -1)
    for i, (n, c) in enumerate(DIAG.items()):
        if n in ON_POOL:
            continue
        if i < ON_DVE:
            ts(mat(n), V("jd"), 0.0, OP.is_equal, c, OP.mult)
        else:
            act(mat(n), mat("I"), AF.Identity, 0.0, c)
    act(V("i32s"), mat("I"), AF.Copy)
    ts(V("icol", 1, 2), V("icol", 0, 1), 15, OP.bitwise_and)
    ts(V("icol", 2, 3), V("icol", 0, 1), 112, OP.bitwise_and)
    cp(V("cols", KC, G16 + 1), V("icol", 1, 3))
    ts(col(SC), col(KC), -STEP, OP.mult, 15 * STEP, OP.add)
    ts(col(SCK), col(KC), -STEP, OP.mult, 15 * STEP + 60 + 1024, OP.add)
    ts(col(K15), col(KC), 15.0, OP.is_equal)
    ts(col(KG), col(K15), -1.0, OP.mult, 1.0, OP.add)
    ts(col(PK), col(KC), 37.0 * 32, OP.mult, 33.0 * M - 2.0 ** 23, OP.add)
    ts(col(KQ), col(KC), -0.5, OP.mult, -3.5, OP.add)
    ts(col(KL), col(KC), 1.5, OP.mult, -34.5, OP.add)
    ts(col(KH), col(KC), 0.5, OP.mult)
    ts(col(NKH), col(KC), -0.5, OP.mult)
    ts(col(KA), col(K15), 1031.5, OP.mult, col(NKH), OP.add)
    ts(col(KB), col(K15), -7.5, OP.mult, col(KH), OP.add)
    ts(col(KI), col(K15), 3.5, OP.mult, col(KQ), OP.add)
    ts(V("selh"), V("jrow"), col(G16), OP.is_equal, -BIG, OP.mult)
    cp(col(H1), V("hws", 0, 1))
    for i, (n, c) in enumerate((("O1", 1.0), ("OH", -0.5), ("On2", -2.0), ("OB", BIG), ("nOB", -BIG), ("O2B", 2 * BIG), ("KW", col(KH)),
                                ("KW0", col(KA)), ("KWL", col(KB)))):
        if i < ON_DVE2:
            ts(mat(n), V("grow"), col(G16), OP.is_equal, c, OP.mult)
        else:
            act(mat(n), mat("O1"), AF.Identity, 0.0, c)
    for n, c in (("Hp", 0.25), ("Hn", -0.125), ("H2", 2.0 * KS)):
        ts(mat(n), mat("O1"), col(H1), OP.mult, c, OP.mult)
    ts(mat("D0"), mat("I"), col(K15), OP.mult, -4.5, OP.mult)
    act(mat("D15"), mat("I16B"), AF.Identity, 0.0, col(KG))
    act(mat("nD15"), mat("D15"), AF.Identity, 0.0, -1.0)
    sel(mat("TRS"), mat("OH"), [[1, 128]], OP.is_gt, 0.0, 0, -1)
    sel(mat("TRI"), mat("TRS"), [[1, 128]], OP.not_equal, 4.0, 0, -1)
    sel(mat("TRV"), mat("On2"), [[-1, 128]], OP.is_gt, 0.0, 0, 1)
    mms(terms(V("pb0", 0, 128), [(mat("I"), mat("TRI")), (mat("I"), mat("D0"))]) + terms(V("pb0", 128, 256), [(mat("I"), mat("TRI")), (mat("I"), mat("TRV"))]))
    act(V("mats", mat("TR0")[3], mat("TR0")[3] + 256), V("pb0", 0, 256), AF.Copy)
    iota(tile("w16"), [[16, NM]], 0, 0)
    for n in ON_POOL:
        sel(mat(n), mat("I"), [[1, 128]], OP.not_equal, DIAG[n], 0, -1)
    iota(V("cio"), [[1, P]], -256, 0)
    for c in sorted(set(CH.index(n) for n in CH)):
        n, o = CH[c], 3 * C0[c]
        ts(V("kq", o, o + n), tile("turn", n), col(KQ), OP.add)
        ts(V("kq", o + 2 * n, o + 3 * n), tile("turn", n), -1.0, OP.add, col(KG), OP.mult)
        ts(V("kq", o + n, o + 2 * n), V("kq", o + 2 * n, o + 3 * n), col(KI), OP.add)
        ts(V("kq", o + 2 * n, o + 3 * n), tile("turn", n), col(KL), OP.add)
    ts(tile("mk"), tile("rr"), col(KC), OP.not_equal)
    act(tile("d0"), tile("mk"), AF.Identity, 64 * STEP, -65 * STEP)
    ts(V("cols", DF, DF + 4), V("dws"), -32.5, OP.add)
    for s in range(ST):
        act(V("dt", 2 * NM * s, 2 * NM * (s + 1), 2), V("ones", 0, NM), AF.Copy)
        act(V("dt", 2 * NM * s + 1, 2 * NM * (s + 1), 2), V("ones", 0, NM), AF.Identity, 0.0, col(DF + s))
    ts(col(HF), V("ths", 0, 1), -1.0, OP.mult)
    ts(col(TA_), col(KC), 0.0, OP.is_equal, col(HF), OP.mult)
    ts(col(TB_), col(KC), 1.0, OP.is_equal, -0.5, OP.mult)
    act(tile("tht"), V("ones", 0, NM), AF.Identity, col(TB_), col(TA_))
    ms(V("hb"), XO)
    if PAIRS:
        ms(tile("da"), VB / BIG)
    group(V("pb1", 0, 2), [(mat("Hn"), V("hb", 0, 2))])
    ts(col(CU), V("pb1", 0, 1), col(SC), OP.add)
    ts(col(RB), V("pb1", 0, 1), VB - 2047.0, OP.add)
    iota(V("dl"), [[1, NM]], 256, 0)
    act(tile("dc"), tile("mk"), AF.Identity, 0.0, -4096.0)
    tt(V("dl"), V("dl"), tile("dc"), OP.add)
    sel(V("zr", p0=0, p1=32), V("zr", p0=0, p1=32), [[1, NS], [0, NM]], OP.is_equal, 0.0, 0, -1)
    sel(V("zr", p0=32, p1=64), V("zr", p0=32, p1=64), [[-16, NS], [1, NM]], OP.is_ge, 0.0, 0, -1)
    for j in range(NS):
        act(V("zp", 8 * j * (j + 1), 8 * (j + 1) * (j + 2), p1=64), V("zr", j * NM, j * NM + 16 * (j + 1), p1=64), AF.Copy)
    for n in ("ys", "ks", "kf"):
        act(V(n, P, P + NM), V("ones"), AF.Copy)
    for c in range(NC):
        if not ROUND:
            ms(V("xt%d" % c), XO)
        act(V("ct%d" % c, p0=0, p1=32), V("jd", p0=0, p1=32), AF.Identity, 0.0, 0.0)
        if c:
            act(V("ct%d" % c, p0=32, p1=64), V("ct0", p0=32, p1=64), AF.Copy)
        for h in range(0, 128 * (c == 0), NM):
            e = min(128, h + NM)
            ts(V("ct%d" % c, h, e, p0=32, p1=64), V("tiles", tile("rr")[3], tile("rr")[3] + e - h, p0=32, p1=64),
               V("cols", KC, KC + 1, p0=32, p1=64), OP.is_equal, 1024.0, OP.mult)
        ms(V("e16_%d" % c, 16 * CH[c], 16 * CH[c] + 16), XO - LOW)
    consts = [i for i, o in enumerate(ops) if o["eng"] == "dve" and o["tag"] not in LATE]
    pool = [i for i, o in enumerate(ops) if o["eng"] == "pool"][:NPOOL]
    for a, b in zip(pool, pool[1:]):
        ops[b]["deps"].setdefault(a, None)
    j = act(V("lx0", 0, CH[0]), V("x0s", 0, CH[0]), AF.Gelu, XO, 16.0)
    ops[j]["cost"] += 1300.0

    nbk = 8 // NC
    for i in range(NFIX):
        a, b = M * i // NFIX, M * (i + 1) // NFIX
        ts(V("ft", a, b), V("fr", a, b), 16.0, OP.is_lt, -LOW, OP.mult)
    add("pool", 1000.0, [lambda g, T, x: g.dma_start(T.ft[:, 0:M], T.fr[:, 0:M], accum_op=OP.add, max_dma_last_dim=4096)],
        [V("fr"), V("ft", 0, M)], [V("ft", 0, M)], lat=7000.0, sem="lfa")
    add("sp", 60.0, [lambda g, T, x: g.sync.dma_start(T.ft[:, M:2 * M], T.ft[:, 0:M])], [V("ft", 0, M)], [V("ft", M, 2 * M)], lat=4000.0 + PAR["SAFE"], sem="lfb")
    add("sp", 60.0, [lambda g, T, x: g.sync.dma_start(T.ft[:, 2 * M:3 * M], T.ft[:, 0:M])], [V("ft", 0, M)], [V("ft", 2 * M, 3 * M)], lat=5000.0 + PAR["SAFE"], sem="lfc")

    def walk(s, c):
        n, c0 = CH[c], C0[c]
        ns = n // 16
        cur[0], cur[1] = float(c), s
        al, be, w0, w1 = ["pb%d" % (c * nbk + i) for i in range(4)]
        wide = [w0, w1]

        def N(name):
            return V(name, c0, c0 + n)

        def S(name):
            return V(name, c0 + 15, c0 + n, 16)

        def t(name):
            return tile(name, n)

        def R(bk, i, k=1):
            return V(bk, i * n, (i + k) * n)

        fw, e16, wa, wq = "fw%d" % c, "e16_%d" % c, "wa%d" % c, "wq%d" % c
        xo, zo, ho = [V("ox%d" % s, 3 * c0 + i * n, 3 * c0 + (i + 1) * n) for i in range(3)]
        x, xz, hit0 = [V("lx%d" % s, 3 * c0 + i * n, 3 * c0 + (i + 1) * n) for i in range(3)]
        to = V("ot%d" % s, c0, c0 + n)
        one = V("ones", 0, n)
        sa, pn = N("sa"), R(be, 0)
        pk, ps = (R(be, 1), R(be, 5)) if 6 * n <= 512 else (N("pks"), R(be, 1))
        pieces, zcut, accb, dedb = LAYOUT[n]
        accb, dedb = [w0, w1, al][accb], [w0, w1, al][dedb]
        tin = N("tin")
        tA, nM = V("tn", 2 * c0, 2 * c0 + 2 * n, 2), V("tn", 2 * c0 + 1, 2 * c0 + 2 * n, 2)
        if s == 0:
            off = "off"
            ts(N("w1"), N("t0s"), M - 1, OP.bitwise_and)
            cp(N("off"), N("w1"))
            ts(tin, N("t0s"), 0.0 if PAIRS else VB, OP.add)
            if c:
                act(x, N("x0s"), AF.Identity, XO, 16.0)
            act(xz, N("x0s"), AF.Relu, 8192.0, -8192.0)
            win = V("fr")
        else:
            off = "lt%d" % s
            if PAIRS:
                tin = V("lp%d" % s, 2 * c0 + 1, 2 * c0 + 2 * n, 2)
            else:
                ts(tin, N(off), VB - M, OP.add)
            win = V("ft")
        act(sa, tin, AF.Sign, 0.5 - M - (0.0 if PAIRS else VB))
        act(N("rb"), tin, AF.Identity, M - 2047.5 + (VB if PAIRS else 0.0))
        xq = V(be, 2 * n, 2 * n + 128, p1=n)
        group(xq, [(x, mat("I"))])
        act(V("xt%d" % c, p1=n), xq, AF.Identity, XO / 16, -1 / 16)
        group(pn, [(V("i32s"), tin), (mat("nI"), N("rb"))] + ([(mat("IB"), t("da"))] if PAIRS else []))
        act(N("n"), pn, AF.Identity, M / KS, 1 / KS)
        act(nM, pn, AF.Identity, 2.0 * M)
        act(pk, pn, AF.Identity, col(PK), 33.0)
        b = 0
        for size, eng, eng2, bk, at, early in pieces:
            a, b = b, b + size
            fp, ep, wp = V(fw, 16 * a, 16 * b), V(e16, 16 * a, 16 * b), V(wa, 16 * a, 16 * b)
            for h in range(a, b, GCUT[c]):
                h1 = min(b, h + GCUT[c])
                if eng == "act":
                    act(V(fw, 16 * h, 16 * h1), IND(win, V(off, c0 + h, c0 + h1)), AF.Copy)
                else:
                    cp(V(fw, 16 * h, 16 * h1), IND(win, V(off, c0 + h, c0 + h1)))
            if eng2 == "act" and not ROUND:
                act(ep, fp, AF.Identity, XO - 7.5)
            else:
                ts(ep, fp, XO - 7.5, OP.add)
            if s == 0:
                ts(V("qw", 16 * (c0 + a), 16 * (c0 + b)), fp, 16.0, OP.is_lt, -LOW, OP.mult)
            z = V([w0, w1, al][bk], at, at + 16 * size)
            if not ROUND:
                group(z, [(V("xt%d" % c, p1=KX), V("rm", 16 * a, 16 * b, p1=KX)), (mat("I"), fp)], early)
                tt(wp, z, ep, OP.is_le)
                continue
            group(z, [(V("xt%d" % c, p1=n), V("rm", 16 * a, 16 * b, p1=n)), (mat("I"), fp)], early)
            if eng2 == "act":
                act(wp, z, AF.Identity, XO - 8.5)
            else:
                ts(wp, z, XO - 8.5, OP.add)
        tm = [(mat("I16B"), sa)] + ([(mat("IB"), hit0)] if s else [])
        it = terms(ps, tm + [(V(sl, 15 - k, 143 - k), V(src, k, 16 * n, 16))
                                   for sl, src in ((("seln", e16), ("selp", wa)) if ROUND else (("selh", wa),)) for k in range(16)])
        mms(it[:len(tm)], opens=True)
        if ROUND:
            mms(it[len(tm):-16])
        mms(it[-16:], closes=True)
        act(N("cand"), ps, AF.Sign, -24.5 * BIG, -1.0)
        f3 = [V("f3", 3 * c0 + i * n, 3 * c0 + (i + 1) * n) for i in range(3)]
        mms([(R(w0, 0, 3), mat("I"), V("kq", 3 * C0[CH.index(n)], 3 * C0[CH.index(n)] + 3 * n), True, False)], opens=True)
        mms([(R(w0, 0), mat("TRI"), N("cand"), False, False), (R(w0, 1), mat("TR0"), N("cand"), False, False),
             (R(w0, 2), mat("TRL"), N("cand"), False, True)], closes=True)
        act(V("f3", 3 * c0, 3 * c0 + 3 * n), R(w0, 0, 3), AF.Sign)
        group(R(w1, 0), [(mat("I"), t("w16")), (mat("KW"), f3[0]), (mat("KW0"), f3[1]), (mat("KWL"), f3[2])], 1)
        scan(N("sv1"), t("d0"), R(w1, 0))
        ko, co, lo = V("so", 32 * c, 32 * c + ns), V("so", 32 * c + 8, 32 * c + 8 + ns), V("so", 32 * c + 16, 32 * c + 16 + ns)
        ts(ko, S("sv1"), col(SCK), OP.add, float(16 * n), OP.min)
        if s == 0 and c == 0:
            j = len(ops) - 1 - KLATE
            for h in range(0, P, 192):
                e = min(P, h + 192)
                ts(V("kf", h, e), V("k0s", h, e), 1 / KS, OP.mult)
                ops[-1]["deps"].setdefault(j, None)
                act(V(al, 320, 320 + e - h), V("kf", h, e), AF.Sign, (0.5 - M) / KS)
                tt(V("ks", h, e), V(al, 320, 320 + e - h), V("kf", h, e), OP.max)
        tt(N("mx"), IND(V(e16), ko), x, OP.max)
        act(N("e"), IND(V(e16), ko), AF.Relu, -XO)
        act(N("bz"), IND(V(e16), ko), AF.Relu, 512 * (XO + 16), -512.0)
        pu, pp, px = R(be, 4), R(al, 0), R(w1, 1)
        group(pu, [(mat("Hn"), x), (mat("Hp"), N("mx")), (mat("Hn"), N("e"))], 1)
        group(pp, [(mat("I240"), one), (mat("I17"), x), (mat("I"), xz), (mat("nI16"), N("mx")), (mat("I"), N("bz"))], 3)
        group(px, [(mat("I"), x), (mat("nI"), N("e"))], 1)
        tt(N("tq"), pp, N("mx"), OP.max)
        act(N("xp"), px, AF.Abs, -XO / 16, 1 / 16)
        if s < ST - 1:
            act(xo, N("xp"), AF.Identity, XO, 16.0)
            act(zo, N("xp"), AF.Relu, 8192.0, -8192.0)
        else:
            store("act", "yx", c0, c0 + n, N("xp"), "oyx%d" % c)
        scan(N("sv2"), t("d0"), pu)
        c1, c2 = V("ci", 16 * c, 16 * c + ns), V("ci", 16 * c + 8, 16 * c + 8 + ns)
        ts(c1, S("sv2"), col(CU), OP.add, 120.5, OP.mult)
        ts(c2, c1, 6, OP.logical_shift_right, P - 1, OP.bitwise_and)
        cp(co, c2)
        tt(N("my"), IND(V("ys", 0, P), co), N("xp"), OP.max)
        act(N("yg"), IND(V("ys", 0, P), co), AF.Copy)
        act(N("kc"), IND(V("ks", 0, P), co), AF.Identity, -float(M), KS)
        act(N("c3"), IND(V("cio"), co), AF.Copy)
        act(N("r"), pu, AF.Identity, col(RB))
        pv, ph, pd = R(be, 2), R(be, 3), R(be, 4)
        group(pv, [(mat("Iv"), one), (mat("nIr"), N("r")), (mat("H2"), N("xp"))])
        tt(N("prod"), pv, N("n"), OP.mult)
        tt(N("sm"), pk, N("prod"), OP.add)
        ts(N("new"), N("sm"), 5, OP.logical_shift_right, M - 1, OP.bitwise_and)
        group(ph, [(mat("OB"), t("tht")), (mat("nOB"), N("xp")), (mat("nOB"), N("yg")), (mat("O2B"), N("my"))], 2)
        group(pd, [(mat("nI"), N("xp")), (mat("I"), N("yg"))])
        tt(N("kp"), ph, N("kc"), OP.max)
        ts(ho, ph, 0.0, OP.is_lt)
        if s < ST - 1:
            k = 2 if APART else 3
            send(V("ox%d" % s, 3 * c0, 3 * c0 + k * n), V("lx%d" % (s + 1), 3 * c0, 3 * c0 + k * n), "ax%d_%d" % (s + 1, c))
            if APART:
                send(ho, V("lx%d" % (s + 1), 3 * c0 + 2 * n, 3 * c0 + 3 * n), "ah%d_%d" % (s + 1, c))
        act(N("gs"), N("kp"), AF.Sign, 0.5)
        tt(N("he"), pn, N("kp"), OP.is_equal)
        tt(tA, N("kp"), N("new"), OP.min)
        pboth, pacc = V(accb, 512 - 2 * n, 512), V(accb, 513 - 2 * n, 512, 2)
        for i, (ka, kb, zb) in enumerate(zcut):
            zb = [w0, w1, al][zb]
            zk = [V(zb, (k - ka) * n, (k - ka + 1) * n) for k in range(ka, kb)]
            src = [[(mat("I"), V(e16, k, 16 * n, 16))] + ([(mat("I"), V("qw", 16 * c0 + k, 16 * (c0 + n), 16))] if s == 0 else [])
                   for k in range(ka, kb)]
            if i < FRESH:
                it = [(zk[k], l_, v, False, False) for k in range(kb - ka) for l_, v in src[k]]
                mms([it[0][:3] + (True, False)] + it[1:], opens=True)
                mms([(zk[k - ka], mat("nI"), N("tq"), False, k == kb - 1) for k in range(ka, kb)], closes=True)
            else:
                mms([m_ for k in range(kb - ka) for m_ in terms(zk[k], src[k] + [(mat("nI"), N("tq"))])])
            act(V(wa, ka * n, kb * n), V(zb, 0, (kb - ka) * n), AF.Gelu, 0.0, FOLD)
            ts(V(wq, ka * n, kb * n), V(wa, ka * n, kb * n), MAGIC, OP.add, MAGIC, OP.not_equal)
        for i, (ka, kb, zb) in enumerate(zcut):
            it = []
            if i == 0:
                it = [(pboth, mat("IB"), V("dt", 2 * NM * s, 2 * NM * s + 2 * n), True, False)]
                it += [(pacc, l_, r_, False, False) for l_, r_ in [(mat("I16B"), sa), (mat("D15"), f3[1]), (mat("nD15"), f3[2])]]
            it += [(pacc, V("selh", 15 - k, 143 - k), V(wq, k * n, (k + 1) * n), False, False) for k in range(ka, kb)]
            mms(it, opens=(i == 0))
        mms([(pacc, mat("I16B"), N("gs"), False, False), (pacc, mat("I32B"), N("he"), False, True)], closes=True)
        scan(V("op%d" % s, 2 * c0, 2 * c0 + 2 * n), pboth, V("tn", 2 * c0, 2 * c0 + 2 * n), OP.max)
        tf = V("op%d" % s, 2 * c0 + 1, 2 * c0 + 2 * n, 2)
        if s < ST - 1:
            ts(to, tf, float(M), OP.add)
            send(to, V("lt%d" % (s + 1), c0, c0 + n), "at%d_%d" % (s + 1, c))
            if PAIRS:
                send(V("op%d" % s, 2 * c0, 2 * c0 + 2 * n), V("lp%d" % (s + 1), 2 * c0, 2 * c0 + 2 * n), "ap%d_%d" % (s + 1, c))
        else:
            ts(N("s2"), tf, 0.0, OP.is_lt, float(M), OP.mult)
            tt(N("tout"), tf, N("s2"), OP.add)
            store("sp", "yt", c0, c0 + n, N("tout"), "oyt%d" % c)
        tt(N("hd"), pd, ho, OP.mult)
        group(ps, [(mat("I8k"), ho), (mat("I4k"), N("gs"))])
        tt(N("zc"), ps, tf, OP.is_gt)
        if s == ST - 1:
            act(N("n"), pn, AF.Identity, float(M))
            act(N("zc"), N("zc"), AF.Identity, 0.0, float(M))
        cd, ct, eq = V("cd%d" % c, 0, ns), "ct%d" % c, "eq%d" % c
        ts(cd, c2, -256.0, OP.add)
        w1 = dedb
        pt = V(w1, 0, 128, p1=ns)
        group(pt, [(cd, mat("I"))])
        act(V(ct, p1=ns), pt, AF.Identity, 0.0, -1.0)
        o = 8 * ns * (ns + 1)
        it, o = [(V(w1, 128, 128 + o), V(ct, p1=48), V("zp", 0, o, p1=48), True, False)], 0
        for j in range(ns):
            wd = 16 * (j + 1)
            it.append((V(w1, 128 + o, 128 + o + wd), mat("I"), V("c3", c0, c0 + wd), False, j == ns - 1))
            o += wd
        mms(it)
        ts(V(eq, 0, o), V(w1, 128, 128 + o), 0.0, OP.is_equal, 1 / 16, OP.mult)
        it = [(V(w1, 0, n), mat("I"), N("c3"), True, False), (V(w1, 0, n), mat("IB"), t("mk"), False, False)]
        o = 0
        for j in range(ns):
            wd = 16 * (j + 1)
            it.append((V(w1, 0, wd), mat("OB"), V(eq, o, o + wd), False, j == ns - 1))
            o += wd
        mms(it)
        scan(N("sv3"), V("dl", 0, n), V(w1, 0, n), OP.max)
        ts(lo, S("sv3"), 256.0, OP.add)
        return lo

    for s in range(ST):
        left = [walk(s, c) for c in range(NC)]
        for c in range(NC):
            a, b = C0[c], C0[c] + CH[c]
            cur[0] = float(c)
            tt(IND(V("ys"), left[c]), V("xp", a, b), V("hd", a, b), OP.add)
            tt(IND(V("kf" if s == ST - 1 else "ks"), left[c]), V("n", a, b), V("zc", a, b), OP.max)
        if s == ST - 2:
            ts(V("kf", 0, P), V("ks", 0, P), KS, OP.mult, float(M), OP.min)
    store("act", "yy", 0, P, V("ys", 0, P), "oyy")
    store("sp", "yk", 0, P, V("kf", 0, P), "oyk")
    return ops


def schedule(ops):
    n = len(ops)
    pred = [[] for _ in range(n)]
    succ = [[] for _ in range(n)]
    for i, o in enumerate(ops):
        for j, sync in o["deps"].items():
            gp = (ops[j]["lat"] + PAR["LAT_S" if ops[j]["eng"] == o["eng"] else "LAT_X"]) if sync else 0.0
            pred[i].append((j, gp))
            succ[j].append((i, gp))
    cost = [max(o["cost"], 1.0) + (PAR["LAT_S"] if o["eng"] == "pool" and not o.get("send") else 0.0) for o in ops]
    lb = PAR["LAT_B"]

    def first(lst, t):
        lo, hi = 0, len(lst)
        while lo < hi:
            mid = (lo + hi) // 2
            if lst[mid][1] <= t:
                lo = mid + 1
            else:
                hi = mid
        return lo

    def place(seq, before, head):
        busy, end = {}, [0.0] * n
        for i in seq:
            st = max([head[i]] + [end[j] + gp for j, gp in before[i]])
            e, c = ops[i]["eng"], cost[i]
            lst = busy.setdefault(e, [])
            while True:
                s0 = st
                lo = first(lst, st)
                while lo < len(lst) and lst[lo][0] < st + c:
                    st = max(st, lst[lo][1])
                    lo += 1
                for bk in ops[i]["banks"]:
                    for e2 in ("pe", "dve", "act"):
                        if e2 != e:
                            bl = busy.get((bk, e2), [])
                            k = first(bl, st - lb)
                            while k < len(bl) and bl[k][0] < st + c + lb:
                                st = max(st, bl[k][1] + lb)
                                k += 1
                if st == s0:
                    break
            lst.insert(lo, (st, st + c))
            for bk in ops[i]["banks"]:
                bl = busy.setdefault((bk, e), [])
                bl.insert(first(bl, st), (st, st + c))
            end[i] = st + c
        return end

    z = [SEED]

    def rnd():
        z[0] = (z[0] * 1103515245 + 12345) % 2147483648
        return z[0] / 2147483648

    def by_key(key):
        for i in range(n - 1, -1, -1):
            for k, gp in succ[i]:
                key[i] = max(key[i], key[k] + 1e-3)
        return sorted(range(n), key=lambda i: (-key[i], i))

    pri = [0.0] * n
    for i in range(n - 1, -1, -1):
        pri[i] = cost[i] + max([ops[i]["lat"]] + [gp + pri[k] for k, gp in succ[i]])
    zero, tail = [0.0] * n, [o["lat"] for o in ops]
    found = []
    for lag in LAGS:
        seq = by_key([pri[i] - lag * ops[i]["lag"] for i in range(n)])
        best = None
        for r in range(ROUNDS):
            for p in range(2):
                end = place(seq, pred, zero)
                span = max(end[i] + tail[i] for i in range(n))
                if best is None or span <= best[0]:
                    best = (span, end)
                back = place(sorted(range(n), key=lambda i: (-end[i], -i)), succ, tail)
                seq = sorted(range(n), key=lambda i: (-back[i], i))
            seq = by_key([cost[i] - best[1][i] + JIT * rnd() for i in range(n)])
        found.append(best)
    span, end = min(found, key=lambda b: b[0])
    soon = [0.0] * n
    for i in range(n):
        soon[i] = max([0.0] + [soon[j] + cost[j] + gp for j, gp in pred[i]])
        ops[i]["at"] = end[i] - cost[i]
    return sorted(range(n), key=lambda i: (0, soon[i], i) if soon[i] < SOON else (1, ops[i]["at"], i)), span


def improve(ops, seq):
    n = len(ops)
    eng = [o["eng"] for o in ops]
    banks = [o["banks"] for o in ops]
    pred = [list(o["deps"]) for o in ops]
    succ = [[] for _ in range(n)]
    for i in range(n):
        for j in pred[i]:
            succ[j].append(i)
    cases = []
    for pace, pe, wake in CASES:
        cost = [o["cost"] * (pe if o["eng"] == "pe" else pace if o["eng"] in ("dve", "act", "pool") and not o["sem"] and not o.get("send") else 1.0)
                + (wake if o["eng"] == "pool" and not o.get("send") else 0.0) for o in ops]
        gaps = [[(j, ops[j]["lat"] + wake if s else 0.0) for j, s in o["deps"].items()] for o in ops]
        cases.append((cost, gaps, [o["lat"] + wake for o in ops]))
    tail = [o["lat"] for o in ops]

    ends = [i for i in range(n) if not succ[i]]
    sent = set(i for i in range(n) if ops[i].get("send"))
    role, who = [], {}
    for i, o in enumerate(ops):
        tag = o["tag"][:2] + o["tag"][3:] if o["tag"][:2] in ("ox", "ot", "lx", "lt", "op", "lp") else o["tag"]
        k = 0
        while (o["step"], o["lag"], o["eng"], tag, k) in who:
            k += 1
        role.append((o["step"], o["lag"], o["eng"], tag, k))
        who[role[-1]] = i

    def run(seq, case, old, p0):
        cost, gaps, hop = case
        end, via, free, last = (list(old[1]), list(old[2]), {}, {}) if old else ([0.0] * n, [-1] * n, {}, {})
        for i in seq[max(0, p0 - 400):p0]:
            if eng[i] != "net":
                free[eng[i]] = i
            if i in sent:
                free["net"] = i + 1
            for bk in banks[i]:
                last[bk] = i
        for i in seq[p0:]:
            e = eng[i]
            if e == "net":
                continue
            v = free.get(e, -1)
            st = end[v] if v >= 0 else 0.0
            for j, gp in gaps[i]:
                if end[j] + gp > st:
                    st, v = end[j] + gp, j
            for bk in banks[i]:
                j = last.get(bk, -1)
                if j >= 0 and eng[j] != e and end[j] + hop[j] > st:
                    st, v = end[j] + hop[j], j
                last[bk] = i
            end[i], via[i], free[e] = st + cost[i], v, i
            if i in sent:
                j = free.get("net", -1)
                late = j >= 0 and end[j] > end[i]
                end[i + 1], via[i + 1], free["net"] = (end[j] if late else end[i]) + cost[i + 1], (j - 1 if late else i), i + 1
        k = max(ends, key=lambda i: end[i] + tail[i])
        return end[k] + tail[k], end, via, k

    z = [SEED]

    def rnd():
        z[0] = (z[0] * 1103515245 + 12345) % 2147483648
        return z[0] / 2147483648

    def judge(seq, old, p0):
        r = [run(seq, c, o, p0) for c, o in zip(cases, old)]
        return sum(x[0] for x in r) / len(r), r

    cur, runs = judge(seq, [None] * len(cases), 0)
    best = (cur, seq, runs)
    for it in range(MOVES):
        span, end, via, k = runs[int(rnd() * len(runs))]
        pairs = []
        while via[k] >= 0:
            if via[k] not in ops[k]["deps"]:
                pairs.append((via[k], k - 1 if eng[k] == "net" else k))
            k = via[k]
        if not pairs:
            break
        a, b = pairs[int(rnd() * len(pairs))]
        ahead, more = rnd() < 0.5, int(12 * rnd()) if rnd() < 0.3 else 0
        todo = [(a, b)]
        if rnd() < TWIN:
            for d in range(1 - ST, ST):
                a2, b2 = who.get((role[a][0] + d,) + role[a][1:]), who.get((role[b][0] + d,) + role[b][1:])
                if d and a2 is not None and b2 is not None:
                    todo.append((a2, b2))
        new, p0 = seq, n
        for a, b in todo:
            pa, pb = new.index(a), new.index(b)
            if pa > pb:
                continue
            if ahead:
                pa = max(0, pa - more)
                win, take = new[pa:pb + 1], {b}
                for x in reversed(win):
                    if x in take:
                        take.update(pred[x])
                if a in take:
                    continue
                new = new[:pa] + [x for x in win if x in take] + [x for x in win if x not in take] + new[pb + 1:]
            else:
                pb = min(n - 1, pb + more)
                win, take = new[pa:pb + 1], {a}
                for x in win:
                    if x in take:
                        take.update(succ[x])
                if b in take:
                    continue
                new = new[:pa] + [x for x in win if x not in take] + [x for x in win if x in take] + new[pb + 1:]
            p0 = min(p0, pa)
        if p0 == n:
            continue
        val, r = judge(new, runs, p0)
        if val <= cur + TEMP * rnd() * (1 - it / MOVES):
            seq, cur, runs = new, val, r
            if val < best[0]:
                best = (val, new, r)
    end = best[2][0][1]
    for i in range(n):
        ops[i]["at"] = end[i] - cases[0][0][i]
    return best[1], best[0]


def link(ops, seq):
    order, place, known, waits, needed = {}, {}, {}, {}, set()
    after, bank = {}, {}
    for i in seq:
        o = ops[i]
        e = o["eng"]
        lst = order.setdefault(e, [])
        place[i] = len(lst)
        want = [j for j, sync in o["deps"].items() if sync]
        if e == "pool" and lst and not o.get("send") and not ops[lst[-1]].get("send") and not o["sem"] and not ops[lst[-1]]["sem"]:
            want.append(lst[-1])
        for bk in o["banks"]:
            want += [j for e2, j in bank.setdefault(bk, {}).items() if e2 != e]
            bank[bk][e] = i
        lst.append(i)
        kn = known.setdefault(e, {})
        waits[i] = []
        for j in sorted(set(want), key=lambda j: -(ops[j]["at"] + ops[j]["cost"] + ops[j]["lat"])):
            key = ops[j]["sem"] or ops[j]["eng"]
            if kn.get(key, -1) < place[j]:
                waits[i].append(j)
                needed.add(j)
                for k, v in after[j].items():
                    kn[k] = max(kn.get(k, -1), v)
        after[i] = dict(kn) if e != "net" else {}
        after[i][o["sem"] or e] = place[i]
    return order, waits, needed


CACHE = {}


def rank_program(g, core, T, topo):
    rank = T.rank_of(core)
    if rank is None:
        return
    if not CACHE:
        CACHE["ops"] = plan()
        CACHE["link"] = link(CACHE["ops"], improve(CACHE["ops"], schedule(CACHE["ops"])[0])[0])
    ops = CACHE["ops"]
    order, waits, needed = CACHE["link"]
    nr = len(T.cores)
    nxt, prv = T.cores[(rank + 1) % nr], T.cores[(rank - 1) % nr]
    rid, pid = topo.addr(nxt, core)
    ctx = {"rid": rid, "pid": pid, "mask": topo.mask(core, nxt)}
    n_out, n_in = len(topo.engines(core, nxt)), len(topo.engines(prv, core))
    mark, total = {}, {}
    for e, lst in order.items():
        for i in lst:
            if ops[i]["sem"]:
                mark[i] = (ops[i]["sem"], n_in if e == "net" else 16)
                total[ops[i]["sem"]] = mark[i][1]
            elif i in needed:
                total[e] = total.get(e, 0) + 1
                mark[i] = (e, total[e])
    queues = {"pe": g.tensor, "dve": g.vector, "act": g.scalar, "pool": g, "sp": g.sync}
    sends = 0
    for e, q in queues.items():
        for i in order.get(e, []):
            for j in waits[i]:
                q.wait_ge(T.sem[mark[j][0]], mark[j][1])
            for fn in ops[i]["fns"]:
                ins = fn(g, T, ctx)
            if ops[i].get("send"):
                sends += 1
            elif i in mark:
                ins.then_inc(T.sem[mark[i][0]], 16 if ops[i]["sem"] else 1)
    for sem, cnt in total.items():
        g.wait_ge(T.sem[sem], cnt)
    g.wait_ge(T.sem.sent, sends * n_out)
